import numpy as np
import ml_dtypes


def mxq(x, axis, fmt="e4m3"):
    dtype, down = {"e4m3": (ml_dtypes.float8_e4m3fn, 7), "e5m2": (ml_dtypes.float8_e5m2, 14)}[fmt]
    v = np.moveaxis(np.asarray(x, np.float32).astype(ml_dtypes.bfloat16).astype(np.float64), axis, -1)
    blocks = v.reshape(v.shape[:-1] + (-1, 32))
    amax = np.abs(blocks).max(-1, keepdims=True)
    byte = np.maximum(np.where(amax > 0, np.frexp(amax)[1] - 1 + 127, 0) - down, 1)
    scale = np.exp2(byte - 127.0)
    codes = (blocks / scale).astype(np.float32).astype(dtype).astype(np.float64)
    return np.moveaxis((codes * scale).reshape(v.shape), -1, axis)


WIDE = False


def mx_kscale(k):
    if not WIDE:
        return np.ones(k)
    levels = np.array([10, -10, 5, -5, 0])
    if k % 512:
        return np.exp2(np.random.permutation(np.resize(levels, k // 32))).repeat(32)
    a = np.empty((k // 512, 16))
    for p in range(k // 512):
        a[p, :8] = np.random.permutation(np.resize(levels, 8))
        for g in range(8):
            far = levels[np.abs(levels - a[p, g]) >= 10]
            a[p, g + 8] = far[np.random.randint(len(far))]
    return np.exp2(a.ravel()).repeat(32)


def f64(x):
    return np.asarray(x).astype(np.float64)


def striped(idx):
    return np.tile(idx.reshape(-1, 16).T, (8, 1)).astype(np.uint16)


def unstriped(offs):
    return offs[:16].T.reshape(-1).astype(np.int64)


E2M1 = np.array([0.0, 0.5, 1.0, 1.5, 2.0, 3.0, 4.0, 6.0, -0.0, -0.5, -1.0, -1.5, -2.0, -3.0, -4.0, -6.0])


def pack_weight(w, fmt):
    k, n = w.shape
    w = f64(np.asarray(w, np.float32).astype(ml_dtypes.bfloat16)).reshape(k // 32, 32, n)
    amax = np.abs(w).max(1)
    if fmt == "e4m3":
        byte = np.frexp(amax)[1] - 1 + 127 - 7
    else:
        mant, ex = np.frexp(amax / 6.0)
        byte = np.where(mant > 0.5, ex, ex - 1) + 127
    byte = np.clip(np.where(amax > 0, byte, 1), 1, 254)
    scaled = (w * np.exp2(127.0 - byte)[:, None, :]).reshape(k, n).astype(np.float32)
    by_word = np.ascontiguousarray(scaled.reshape(k // 512, 128, 4, n).transpose(0, 1, 3, 2))
    if fmt == "e4m3":
        words = by_word.astype(ml_dtypes.float8_e4m3fn).view(np.uint8)
    else:
        c = by_word.astype(ml_dtypes.float4_e2m1fn).view(np.uint8) & 0xF
        words = (c[..., 0::2] | (c[..., 1::2] << 4)).reshape(k // 512, 128, 2 * n)
    return np.ascontiguousarray(words), np.ascontiguousarray(byte.astype(np.uint8).reshape(k // 512, 16, n))


def unpack_weight(words, scales, fmt):
    g, _, n = scales.shape
    words = np.ascontiguousarray(words).reshape(g, 128, n, -1)
    if fmt == "e4m3":
        vals = words.view(ml_dtypes.float8_e4m3fn).astype(np.float64)
    else:
        nib = np.empty((g, 128, n, 4), np.uint8)
        nib[..., 0::2] = words & 0xF
        nib[..., 1::2] = words >> 4
        vals = E2M1[nib]
    vals = vals * np.repeat(np.exp2(scales.astype(np.float64) - 127.0), 8, axis=1)[..., None]
    return vals.transpose(0, 1, 3, 2).reshape(g * 512, n)


K, T, E, B, H, N = 1024, 1024, 4, 6, 512, 512


def setup_inputs():
    n = np.random.standard_normal
    s = mx_kscale(K)
    u = mx_kscale(H)
    slot_token = np.random.permutation(T)[:128 * B]
    block = np.sort(np.random.randint(E, size=B))
    x = pack_weight(n((K, T)) * s[:, None], "e4m3")
    w = pack_weight(n((K, N)) / np.sqrt(K) / s[:, None], "e2m1")
    wa = pack_weight(n((K, E * H)) / np.sqrt(K) / s[:, None] * np.tile(u, E), "e4m3")
    wb = pack_weight(n((H, E * N)) / np.sqrt(H) / u[:, None], "e4m3")
    return {
        "x_words": x[0],
        "x_scales": x[1],
        "w_words": w[0],
        "w_scales": w[1],
        "wa_words": wa[0],
        "wa_scales": wa[1],
        "wb_words": wb[0],
        "wb_scales": wb[1],
        "gate": (np.tile(np.random.uniform(0.2, 1.0, 128 * B), (128, 1))).astype(np.float32),
        "offs": striped(slot_token),
        "offs2": striped((block[:, None] * H + np.arange(H)).reshape(-1)),
        "offs3": striped((block[:, None] * N + np.arange(N)).reshape(-1)),
    }


def reference(x_words, x_scales, w_words, w_scales, wa_words, wa_scales, wb_words, wb_scales, gate, offs, offs2, offs3):
    w = unpack_weight(w_words, w_scales, "e2m1")
    idx, idx2, idx3 = unstriped(offs), unstriped(offs2), unstriped(offs3)
    x = unpack_weight(x_words, x_scales, "e4m3")
    out = w.T @ x
    wa = unpack_weight(wa_words, wa_scales, "e4m3")[:, idx2]
    wb = unpack_weight(wb_words, wb_scales, "e4m3")[:, idx3]
    xq = x[:, idx]
    h = np.concatenate([wa[:, m * H:(m + 1) * H].T @ xq[:, 128 * m:128 * m + 128] for m in range(B)], axis=1)
    hq = mxq(h, 0, "e4m3")
    y = np.concatenate([wb[:, m * N:(m + 1) * N].T @ hq[:, 128 * m:128 * m + 128] for m in range(B)], axis=1)
    out[:, idx] += f64(gate[:1]) * y
    return out

@@ -1,0 +1,224 @@
+from contextlib import ExitStack
+
+import concourse.mybir as mybir
+from concourse.masks import make_identity
+
+K, T, E, B, H, N = 1024, 1024, 4, 6, 512, 512
+FLOPS = 2 * K * N * T + 2 * 128 * B * (K * H + H * N)
+
+F32 = mybir.dt.float32
+BF16 = mybir.dt.bfloat16
+I32 = mybir.dt.int32
+U32 = mybir.dt.uint32
+U16 = mybir.dt.uint16
+U8 = mybir.dt.uint8
+FP8X4 = mybir.dt.float8_e4m3fn_x4
+FP4X4 = mybir.dt.float4_e2m1fn_x4
+MULT = mybir.AluOpType.mult
+ADD = mybir.AluOpType.add
+
+P = 128
+PASSES = K // 512
+SLOTS = P * B
+BANK = 512
+HALF = B // 2
+ROWBLOCKS = N // P
+
+
+def tile_moe_dyl_none_kernel(
+    tc, x_words, x_scales, w_words, w_scales, wa_words, wa_scales, wb_words, wb_scales, gate, offs, offs2, offs3, out
+):
+    nc = tc.nc
+    with ExitStack() as ctx:
+        keep = ctx.enter_context(tc.tile_pool(name="keep", bufs=1))
+        ring = ctx.enter_context(tc.tile_pool(name="ring", bufs=2))
+        psum = ctx.enter_context(tc.psum_pool(name="psum", bufs=2))
+
+        def held(shape, dtype, name):
+            return keep.tile(shape, dtype, name=name, align_bytes=64)
+
+        def load_words(tile, words):
+            nc.sync.dma_start(out=tile[:], in_=words.rearrange("p c d -> p (c d)").bitcast(I32))
+
+        def load_scale_rows(plane, scales):
+            rows = 4 * scales.shape[0]
+            for q in range(4):
+                nc.sync.dma_start(
+                    out=plane[32 * q : 32 * q + rows, :].bitcast(I32),
+                    in_=scales[:, 4 * q : 4 * q + 4, :].bitcast(I32),
+                )
+
+        tok_list = held([P, SLOTS // 16], U16, "tok_list")
+        wa_list = held([P, B * H // 16], U16, "wa_list")
+        wb_list = held([P, B * N // 16], U16, "wb_list")
+        xw = [held([P, T], I32, "xw%d" % a) for a in range(PASSES)]
+        waw = [held([P, E * H], I32, "waw%d" % a) for a in range(PASSES)]
+        wbw = held([P, E * N], I32, "wbw")
+        xs = held([P, T], U8, "xs")
+        xs1 = held([P, T], U8, "xs1")
+        was = held([P, E * H], U8, "was")
+        wbs = held([P, E * N], U8, "wbs")
+        ww = held([P, PASSES, 2 * N], U8, "ww")
+        ws = held([P, PASSES, N], U8, "ws")
+        gate_sb = held([P, SLOTS], F32, "gate_sb")
+        ident = held([P, P], F32, "ident")
+        win = [held([P, T], F32, "win%d" % r) for r in range(ROWBLOCKS)]
+
+        for plane in (xs, was, wbs):
+            nc.vector.memset(plane[:].bitcast(I32), 0)
+        make_identity(nc, ident[:])
+        nc.gpsimd.memset(xs1[:].bitcast(I32), 0)
+        nc.gpsimd.memset(ws[:].rearrange("p a n -> p (a n)").bitcast(I32), 0)
+        nc.gpsimd.memset(win[0][:], 0.0)
+
+        nc.sync.dma_start(tok_list[:], offs)
+        load_words(xw[0], x_words[0])
+        load_words(xw[1], x_words[1])
+        nc.sync.dma_start(wa_list[:], offs2)
+        load_words(waw[0], wa_words[0])
+        load_scale_rows(xs, x_scales)
+        load_scale_rows(was, wa_scales)
+        load_words(waw[1], wa_words[1])
+        nc.sync.dma_start(wb_list[:], offs3)
+        load_words(wbw, wb_words[0])
+        load_scale_rows(wbs, wb_scales)
+        load_scale_rows(xs1, x_scales[1:2])
+        for q in range(4):
+            nc.sync.dma_start(
+                out=ws[32 * q : 32 * q + 4, :, :].bitcast(I32),
+                in_=w_scales[:, 4 * q : 4 * q + 4, :].rearrange("a r n -> r a n").bitcast(I32),
+            )
+        nc.sync.dma_start(out=ww[:].bitcast(I32), in_=w_words.rearrange("a p c -> p a c").bitcast(I32))
+        nc.sync.dma_start(out=gate_sb[:], in_=gate)
+
+        for r in range(1, ROWBLOCKS):
+            nc.scalar.copy(out=win[r][:], in_=win[0][:])
+
+        xq = [held([P, SLOTS], U32, "xq%d" % a) for a in range(PASSES)]
+        xsq = held([P, SLOTS], U8, "xsq")
+        for a in range(PASSES):
+            nc.vector.tensor_copy(xq[a][:], xw[a][:].bitcast(U32).indirect(tok_list[:]))
+        nc.vector.tensor_copy(xsq[:], xs[:].indirect(tok_list[:]))
+
+        width = HALF * H
+        hq = held([P, SLOTS], U32, "hq")
+        hqs = held([P, SLOTS], U8, "hqs")
+        grouped = [held([P, 2 * P, 4], BF16, "grouped%d" % g) for g in range(B // 2)]
+        for half in range(2):
+            entries = wa_list[:, half * width // 16 : (half + 1) * width // 16]
+            waq = [held([P, width], U32, "waq%d_%d" % (half, a)) for a in range(PASSES)]
+            wasq = held([P, width], U8, "wasq%d" % half)
+            for a in range(PASSES):
+                nc.vector.tensor_copy(waq[a][:], waw[a][:].bitcast(U32).indirect(entries))
+            nc.vector.tensor_copy(wasq[:], was[:].indirect(entries))
+            for j in range(HALF):
+                m = half * HALF + j
+                slots = slice(P * m, P * (m + 1))
+                cols = slice(H * j, H * (j + 1))
+                ht = psum.tile([P, H], F32, tag="ht")
+                for a in range(PASSES):
+                    nc.tensor.matmul_mx(
+                        out=ht[:],
+                        lhsT=xq[a][:, slots].bitcast(FP8X4),
+                        lhsT_scale=xsq[4 * a :, slots],
+                        rhs=waq[a][:, cols].bitcast(FP8X4),
+                        rhs_scale=wasq[4 * a :, cols],
+                        start=(a == 0),
+                        stop=(a == PASSES - 1),
+                    )
+                hb = ring.tile([P, H], BF16, tag="hb", align_bytes=64)
+                nc.scalar.copy(
+                    out=hb[:].rearrange("s (u p e) -> s u p e", u=2, e=2),
+                    in_=ht[:].rearrange("s (p u e) -> s u p e", u=2, e=2),
+                )
+                turned = psum.tile([P, 2, P], F32, tag="turned")
+                for u in range(2):
+                    nc.tensor.transpose(turned[:, u, :], hb[:].bitcast(F32)[:, P * u : P * (u + 1)], ident[:])
+                nc.scalar.copy(
+                    out=grouped[m // 2][:, P * (m % 2) : P * (m % 2 + 1), :].bitcast(F32),
+                    in_=turned[:].rearrange("p u s -> p s u"),
+                )
+                if m % 2 == 1:
+                    pair = slice(P * (m - 1), P * (m + 1))
+                    nc.vector.quantize_mx(
+                        out=hq[:, pair].bitcast(FP8X4),
+                        scales=hqs[:, pair],
+                        in_=grouped[m // 2][:].rearrange("p s t -> p (s t)"),
+                    )
+
+        width = HALF * N
+        ysb = [held([P, SLOTS], F32, "ysb%d" % r) for r in range(ROWBLOCKS)]
+        for half in range(2):
+            entries = wb_list[:, half * width // 16 : (half + 1) * width // 16]
+            wbq = held([P, width], U32, "wbq%d" % half)
+            wbsq = held([P, width], U8, "wbsq%d" % half)
+            nc.vector.tensor_copy(wbq[:], wbw[:].bitcast(U32).indirect(entries))
+            nc.vector.tensor_copy(wbsq[:], wbs[:].indirect(entries))
+            for r in range(ROWBLOCKS):
+                y = psum.tile([P, HALF * P], F32, tag="y")
+                for j in range(HALF):
+                    m = half * HALF + j
+                    slots = slice(P * m, P * (m + 1))
+                    cols = slice(N * j + P * r, N * j + P * (r + 1))
+                    nc.tensor.matmul_mx(
+                        out=y[:, P * j : P * (j + 1)],
+                        lhsT=wbq[:, cols].bitcast(FP8X4),
+                        lhsT_scale=wbsq[:, cols],
+                        rhs=hq[:, slots].bitcast(FP8X4),
+                        rhs_scale=hqs[:, slots],
+                        start=True,
+                        stop=True,
+                    )
+                nc.scalar.copy(out=ysb[r][:, half * HALF * P : (half + 1) * HALF * P], in_=y[:])
+
+        base = [held([P, T], F32, "base%d" % r) for r in range(ROWBLOCKS)]
+        for r in range(ROWBLOCKS):
+            for c in range(T // BANK):
+                toks = slice(BANK * c, BANK * (c + 1))
+                acc = psum.tile([P, BANK], F32, tag="acc")
+                for a in range(PASSES):
+                    nc.tensor.matmul_mx(
+                        out=acc[:],
+                        lhsT=ww[:, a, 2 * P * r : 2 * P * (r + 1)].bitcast(FP4X4),
+                        lhsT_scale=ws[:, a, P * r : P * (r + 1)],
+                        rhs=xw[a][:, toks].bitcast(FP8X4),
+                        rhs_scale=(xs, xs1)[a][:, toks],
+                        start=(a == 0),
+                        stop=(a == PASSES - 1),
+                    )
+                nc.scalar.copy(out=base[r][:, toks], in_=acc[:])
+
+        for r in range(ROWBLOCKS):
+            rows = slice(P * r, P * (r + 1))
+            if r == 0:
+                for half in range(2):
+                    part = slice(half * HALF * P, (half + 1) * HALF * P)
+                    entries = tok_list[:, part.start // 16 : part.stop // 16]
+                    nc.vector.tensor_tensor(win[r][:].indirect(entries), ysb[r][:, part], gate_sb[:, part], MULT)
+            else:
+                nc.vector.tensor_tensor(win[r][:].indirect(tok_list[:]), ysb[r][:], gate_sb[:], MULT)
+            for c in range(T // BANK):
+                toks = slice(BANK * c, BANK * (c + 1))
+                result = ring.tile([P, BANK], F32, tag="result", bufs=4, align_bytes=64)
+                if r == ROWBLOCKS - 1:
+                    nc.vector.tensor_tensor(result[:], base[r][:, toks], win[r][:, toks], ADD)
+                else:
+                    sum_t = psum.tile([P, BANK], F32, tag="acc")
+                    for j in range(BANK // P):
+                        tile_toks = slice(BANK * c + P * j, BANK * c + P * (j + 1))
+                        for step, term in enumerate((base[r], win[r])):
+                            nc.tensor.matmul(
+                                sum_t[:, P * j : P * (j + 1)],
+                                lhsT=term[:, tile_toks],
+                                rhs=ident[:],
+                                is_transpose=True,
+                                start=(step == 0),
+                                stop=(step == 1),
+                            )
+                    sum_sb = ring.tile([P, BANK], F32, tag="sum_sb", align_bytes=64)
+                    nc.scalar.copy(out=sum_sb[:], in_=sum_t[:])
+                    back = psum.tile([P, BANK], F32, tag="turned")
+                    for j in range(BANK // P):
+                        nc.tensor.transpose(back[:, P * j : P * (j + 1)], sum_sb[:, P * j : P * (j + 1)], ident[:])
+                    nc.scalar.copy(out=result[:], in_=back[:])
+                nc.sync.dma_start(out=out[rows, toks], in_=result[:])

@@ -32,10 +32,14 @@ def tile_moe_dyl_none_kernel(
     with ExitStack() as ctx:
         keep = ctx.enter_context(tc.tile_pool(name="keep", bufs=1))
         ring = ctx.enter_context(tc.tile_pool(name="ring", bufs=2))
-        psum = ctx.enter_context(tc.psum_pool(name="psum", bufs=2))
+        shared = ctx.enter_context(tc.tile_pool(name="shared", bufs=1))
+        psum = ctx.enter_context(tc.psum_pool(name="psum", bufs=1))
 
         def held(shape, dtype, name):
             return keep.tile(shape, dtype, name=name, align_bytes=64)
+
+        def bank(number, shape):
+            return psum.tile(shape, F32, name="bank%d" % number)
 
         def load_words(tile, words):
             nc.sync.dma_start(out=tile[:], in_=words.rearrange("p c d -> p (c d)").bitcast(I32))
@@ -53,7 +57,7 @@ def tile_moe_dyl_none_kernel(
         wb_list = held([P, B * N // 16], U16, "wb_list")
         xw = [held([P, T], I32, "xw%d" % a) for a in range(PASSES)]
         waw = [held([P, E * H], I32, "waw%d" % a) for a in range(PASSES)]
-        wbw = held([P, E * N], I32, "wbw")
+        wbw = keep.tile([P, E * N], I32, tag="wbw_then_hq", align_bytes=64)
         xs = held([P, T], U8, "xs")
         xs1 = held([P, T], U8, "xs1")
         was = held([P, E * H], U8, "was")
@@ -64,11 +68,11 @@ def tile_moe_dyl_none_kernel(
         ident = held([P, P], F32, "ident")
         win = [held([P, T], F32, "win%d" % r) for r in range(ROWBLOCKS)]
 
-        for plane in (xs, was, wbs):
+        for plane in (xs, was, xs1):
             nc.vector.memset(plane[:].bitcast(I32), 0)
-        make_identity(nc, ident[:])
-        nc.gpsimd.memset(xs1[:].bitcast(I32), 0)
         nc.gpsimd.memset(ws[:].rearrange("p a n -> p (a n)").bitcast(I32), 0)
+        nc.gpsimd.memset(wbs[:].bitcast(I32), 0)
+        make_identity(nc, ident[:])
         nc.gpsimd.memset(win[0][:], 0.0)
 
         nc.sync.dma_start(tok_list[:], offs)
@@ -79,20 +83,38 @@ def tile_moe_dyl_none_kernel(
         load_scale_rows(xs, x_scales)
         load_scale_rows(was, wa_scales)
         load_words(waw[1], wa_words[1])
-        nc.sync.dma_start(wb_list[:], offs3)
-        load_words(wbw, wb_words[0])
-        load_scale_rows(wbs, wb_scales)
+        nc.sync.dma_start(out=ww[:].bitcast(I32), in_=w_words.rearrange("a p c -> p a c").bitcast(I32))
         load_scale_rows(xs1, x_scales[1:2])
         for q in range(4):
             nc.sync.dma_start(
                 out=ws[32 * q : 32 * q + 4, :, :].bitcast(I32),
                 in_=w_scales[:, 4 * q : 4 * q + 4, :].rearrange("a r n -> r a n").bitcast(I32),
             )
-        nc.sync.dma_start(out=ww[:].bitcast(I32), in_=w_words.rearrange("a p c -> p a c").bitcast(I32))
+        nc.sync.dma_start(wb_list[:], offs3)
+        load_scale_rows(wbs, wb_scales)
+        load_words(wbw, wb_words[0])
         nc.sync.dma_start(out=gate_sb[:], in_=gate)
 
         for r in range(1, ROWBLOCKS):
             nc.scalar.copy(out=win[r][:], in_=win[0][:])
+
+        base = [held([P, T], F32, "base%d" % r) for r in range(ROWBLOCKS)]
+
+        def frozen(r, banks):
+            for c in range(T // BANK):
+                toks = slice(BANK * c, BANK * (c + 1))
+                acc = bank(banks[c], [P, BANK])
+                for a in range(PASSES):
+                    nc.tensor.matmul_mx(
+                        out=acc[:],
+                        lhsT=ww[:, a, 2 * P * r : 2 * P * (r + 1)].bitcast(FP4X4),
+                        lhsT_scale=ws[:, a, P * r : P * (r + 1)],
+                        rhs=xw[a][:, toks].bitcast(FP8X4),
+                        rhs_scale=(xs, xs1)[a][:, toks],
+                        start=(a == 0),
+                        stop=(a == PASSES - 1),
+                    )
+                nc.scalar.copy(out=base[r][:, toks], in_=acc[:])
 
         xq = [held([P, SLOTS], U32, "xq%d" % a) for a in range(PASSES)]
         xsq = held([P, SLOTS], U8, "xsq")
@@ -101,9 +123,8 @@ def tile_moe_dyl_none_kernel(
         nc.vector.tensor_copy(xsq[:], xs[:].indirect(tok_list[:]))
 
         width = HALF * H
-        hq = held([P, SLOTS], U32, "hq")
-        hqs = held([P, SLOTS], U8, "hqs")
-        grouped = [held([P, 2 * P, 4], BF16, "grouped%d" % g) for g in range(B // 2)]
+        grouped_a = held([P, 4 * P, 4], BF16, "grouped_a")
+        grouped_b = shared.tile([P, 2 * P, 4], BF16, offset=512, align_bytes=64)
         for half in range(2):
             entries = wa_list[:, half * width // 16 : (half + 1) * width // 16]
             waq = [held([P, width], U32, "waq%d_%d" % (half, a)) for a in range(PASSES)]
@@ -115,7 +136,7 @@ def tile_moe_dyl_none_kernel(
                 m = half * HALF + j
                 slots = slice(P * m, P * (m + 1))
                 cols = slice(H * j, H * (j + 1))
-                ht = psum.tile([P, H], F32, tag="ht")
+                ht = bank(j, [P, H])
                 for a in range(PASSES):
                     nc.tensor.matmul_mx(
                         out=ht[:],
@@ -131,94 +152,95 @@ def tile_moe_dyl_none_kernel(
                     out=hb[:].rearrange("s (u p e) -> s u p e", u=2, e=2),
                     in_=ht[:].rearrange("s (p u e) -> s u p e", u=2, e=2),
                 )
-                turned = psum.tile([P, 2, P], F32, tag="turned")
+                turned = bank(4 + j, [P, 2, P])
                 for u in range(2):
                     nc.tensor.transpose(turned[:, u, :], hb[:].bitcast(F32)[:, P * u : P * (u + 1)], ident[:])
                 nc.scalar.copy(
-                    out=grouped[m // 2][:, P * (m % 2) : P * (m % 2 + 1), :].bitcast(F32),
+                    out=(grouped_a, grouped_b)[m // 4][:, P * (m % 4) : P * (m % 4 + 1), :].bitcast(F32),
                     in_=turned[:].rearrange("p u s -> p s u"),
                 )
-                if m % 2 == 1:
-                    pair = slice(P * (m - 1), P * (m + 1))
-                    nc.vector.quantize_mx(
-                        out=hq[:, pair].bitcast(FP8X4),
-                        scales=hqs[:, pair],
-                        in_=grouped[m // 2][:].rearrange("p s t -> p (s t)"),
-                    )
+            if half == 0:
+                frozen(0, (0, 1))
+                frozen(1, (2, 6))
 
         width = HALF * N
+        wbq = [held([P, width], U32, "wbq%d" % half) for half in range(2)]
+        wbsq_a = held([P, width], U8, "wbsq_a")
+        wb_entries = [wb_list[:, half * width // 16 : (half + 1) * width // 16] for half in range(2)]
+        nc.vector.tensor_copy(wbsq_a[:], wbs[:].indirect(wb_entries[0]))
+        for half in range(2):
+            nc.vector.tensor_copy(wbq[half][:], wbw[:].bitcast(U32).indirect(wb_entries[half]))
+        hq = keep.tile([P, SLOTS], U32, tag="wbw_then_hq", align_bytes=64)
+        hqs = held([P, SLOTS], U8, "hqs")
+        for grouped, slots in ((grouped_b, slice(4 * P, SLOTS)), (grouped_a, slice(0, 4 * P))):
+            nc.vector.quantize_mx(
+                out=hq[:, slots].bitcast(FP8X4),
+                scales=hqs[:, slots],
+                in_=grouped[:].rearrange("p s t -> p (s t)"),
+            )
+        wbsq_b = shared.tile([P, width], U8, offset=0, align_bytes=64)
+        nc.vector.tensor_copy(wbsq_b[:], wbs[:].indirect(wb_entries[1]))
+        y_first = shared.tile([P, HALF * P], F32, offset=1536, align_bytes=64)
         ysb = [held([P, SLOTS], F32, "ysb%d" % r) for r in range(ROWBLOCKS)]
         for half in range(2):
-            entries = wb_list[:, half * width // 16 : (half + 1) * width // 16]
-            wbq = held([P, width], U32, "wbq%d" % half)
-            wbsq = held([P, width], U8, "wbsq%d" % half)
-            nc.vector.tensor_copy(wbq[:], wbw[:].bitcast(U32).indirect(entries))
-            nc.vector.tensor_copy(wbsq[:], wbs[:].indirect(entries))
+            wbsq = (wbsq_a, wbsq_b)[half]
             for r in range(ROWBLOCKS):
-                y = psum.tile([P, HALF * P], F32, tag="y")
+                y = bank(ROWBLOCKS * half + r, [P, HALF * P])
                 for j in range(HALF):
                     m = half * HALF + j
                     slots = slice(P * m, P * (m + 1))
                     cols = slice(N * j + P * r, N * j + P * (r + 1))
                     nc.tensor.matmul_mx(
                         out=y[:, P * j : P * (j + 1)],
-                        lhsT=wbq[:, cols].bitcast(FP8X4),
+                        lhsT=wbq[half][:, cols].bitcast(FP8X4),
                         lhsT_scale=wbsq[:, cols],
                         rhs=hq[:, slots].bitcast(FP8X4),
                         rhs_scale=hqs[:, slots],
                         start=True,
                         stop=True,
                     )
-                nc.scalar.copy(out=ysb[r][:, half * HALF * P : (half + 1) * HALF * P], in_=y[:])
+                if half == 0 and r == 0:
+                    nc.scalar.copy(out=y_first[:], in_=y[:])
+                else:
+                    nc.scalar.copy(out=ysb[r][:, half * HALF * P : (half + 1) * HALF * P], in_=y[:])
+        frozen(2, (4, 5))
+        frozen(3, (6, 7))
 
-        base = [held([P, T], F32, "base%d" % r) for r in range(ROWBLOCKS)]
-        for r in range(ROWBLOCKS):
-            for c in range(T // BANK):
-                toks = slice(BANK * c, BANK * (c + 1))
-                acc = psum.tile([P, BANK], F32, tag="acc")
-                for a in range(PASSES):
-                    nc.tensor.matmul_mx(
-                        out=acc[:],
-                        lhsT=ww[:, a, 2 * P * r : 2 * P * (r + 1)].bitcast(FP4X4),
-                        lhsT_scale=ws[:, a, P * r : P * (r + 1)],
-                        rhs=xw[a][:, toks].bitcast(FP8X4),
-                        rhs_scale=(xs, xs1)[a][:, toks],
-                        start=(a == 0),
-                        stop=(a == PASSES - 1),
-                    )
-                nc.scalar.copy(out=base[r][:, toks], in_=acc[:])
-
+        sum_banks, back_banks = (4, 5), (0, 1)
         for r in range(ROWBLOCKS):
             rows = slice(P * r, P * (r + 1))
             if r == 0:
                 for half in range(2):
                     part = slice(half * HALF * P, (half + 1) * HALF * P)
                     entries = tok_list[:, part.start // 16 : part.stop // 16]
-                    nc.vector.tensor_tensor(win[r][:].indirect(entries), ysb[r][:, part], gate_sb[:, part], MULT)
+                    values = y_first[:] if half == 0 else ysb[r][:, part]
+                    nc.vector.tensor_tensor(win[r][:].indirect(entries), values, gate_sb[:, part], MULT)
             else:
                 nc.vector.tensor_tensor(win[r][:].indirect(tok_list[:]), ysb[r][:], gate_sb[:], MULT)
             for c in range(T // BANK):
                 toks = slice(BANK * c, BANK * (c + 1))
-                result = ring.tile([P, BANK], F32, tag="result", bufs=4, align_bytes=64)
+                result = held([P, BANK], F32, "result%d_%d" % (r, c))
                 if r == ROWBLOCKS - 1:
                     nc.vector.tensor_tensor(result[:], base[r][:, toks], win[r][:, toks], ADD)
-                else:
-                    sum_t = psum.tile([P, BANK], F32, tag="acc")
-                    for j in range(BANK // P):
-                        tile_toks = slice(BANK * c + P * j, BANK * c + P * (j + 1))
-                        for step, term in enumerate((base[r], win[r])):
-                            nc.tensor.matmul(
-                                sum_t[:, P * j : P * (j + 1)],
-                                lhsT=term[:, tile_toks],
-                                rhs=ident[:],
-                                is_transpose=True,
-                                start=(step == 0),
-                                stop=(step == 1),
-                            )
-                    sum_sb = ring.tile([P, BANK], F32, tag="sum_sb", align_bytes=64)
-                    nc.scalar.copy(out=sum_sb[:], in_=sum_t[:])
-                    back = psum.tile([P, BANK], F32, tag="turned")
-                    for j in range(BANK // P):
-                        nc.tensor.transpose(back[:, P * j : P * (j + 1)], sum_sb[:, P * j : P * (j + 1)], ident[:])
-                    nc.scalar.copy(out=result[:], in_=back[:])
-                nc.sync.dma_start(out=out[rows, toks], in_=result[:])
+                    nc.sync.dma_start(out=out[rows, toks], in_=result[:])
+                    continue
+                sum_t = bank(sum_banks[c], [P, BANK])
+                for j in range(BANK // P):
+                    tile_toks = slice(BANK * c + P * j, BANK * c + P * (j + 1))
+                    for step, term in enumerate((base[r], win[r])):
+                        nc.tensor.matmul(
+                            sum_t[:, P * j : P * (j + 1)],
+                            lhsT=term[:, tile_toks],
+                            rhs=ident[:],
+                            is_transpose=True,
+                            start=(step == 0),
+                            stop=(step == 1),
+                        )
+                sum_sb = ring.tile([P, BANK], F32, tag="sum_sb", align_bytes=64)
+                nc.scalar.copy(out=sum_sb[:], in_=sum_t[:])
+                back = bank(back_banks[c], [P, BANK])
+                for j in range(BANK // P):
+                    nc.tensor.transpose(back[:, P * j : P * (j + 1)], sum_sb[:, P * j : P * (j + 1)], ident[:])
+                nc.scalar.copy(out=result[:], in_=back[:])
+                nc.scalar.dma_start(out=out[rows, toks], in_=result[:])
+            sum_banks, back_banks = back_banks[::-1], sum_banks

@@ -68,28 +68,29 @@ def tile_moe_dyl_none_kernel(
         ident = held([P, P], F32, "ident")
         win = [held([P, T], F32, "win%d" % r) for r in range(ROWBLOCKS)]
 
-        for plane in (xs, was, xs1):
-            nc.vector.memset(plane[:].bitcast(I32), 0)
-        nc.gpsimd.memset(ws[:].rearrange("p a n -> p (a n)").bitcast(I32), 0)
-        nc.gpsimd.memset(wbs[:].bitcast(I32), 0)
+        for plane in (xs, was):
+            nc.gpsimd.memset(plane[:].bitcast(I32), 0)
         make_identity(nc, ident[:])
         nc.gpsimd.memset(win[0][:], 0.0)
+        nc.vector.memset(xs1[:].bitcast(I32), 0)
+        nc.vector.memset(ws[:].rearrange("p a n -> p (a n)").bitcast(I32), 0)
+        nc.vector.memset(wbs[:].bitcast(I32), 0)
 
         nc.sync.dma_start(tok_list[:], offs)
+        nc.sync.dma_start(wa_list[:], offs2)
+        load_scale_rows(xs, x_scales)
         load_words(xw[0], x_words[0])
         load_words(xw[1], x_words[1])
-        nc.sync.dma_start(wa_list[:], offs2)
-        load_words(waw[0], wa_words[0])
-        load_scale_rows(xs, x_scales)
         load_scale_rows(was, wa_scales)
-        load_words(waw[1], wa_words[1])
-        nc.sync.dma_start(out=ww[:].bitcast(I32), in_=w_words.rearrange("a p c -> p a c").bitcast(I32))
+        load_words(waw[0], wa_words[0])
         load_scale_rows(xs1, x_scales[1:2])
+        load_words(waw[1], wa_words[1])
         for q in range(4):
             nc.sync.dma_start(
                 out=ws[32 * q : 32 * q + 4, :, :].bitcast(I32),
                 in_=w_scales[:, 4 * q : 4 * q + 4, :].rearrange("a r n -> r a n").bitcast(I32),
             )
+        nc.sync.dma_start(out=ww[:].bitcast(I32), in_=w_words.rearrange("a p c -> p a c").bitcast(I32))
         nc.sync.dma_start(wb_list[:], offs3)
         load_scale_rows(wbs, wb_scales)
         load_words(wbw, wb_words[0])
@@ -118,20 +119,24 @@ def tile_moe_dyl_none_kernel(
 
         xq = [held([P, SLOTS], U32, "xq%d" % a) for a in range(PASSES)]
         xsq = held([P, SLOTS], U8, "xsq")
+        nc.vector.tensor_copy(xsq[:], xs[:].indirect(tok_list[:]))
         for a in range(PASSES):
             nc.vector.tensor_copy(xq[a][:], xw[a][:].bitcast(U32).indirect(tok_list[:]))
-        nc.vector.tensor_copy(xsq[:], xs[:].indirect(tok_list[:]))
-
         width = HALF * H
+        wa_entries = [wa_list[:, half * width // 16 : (half + 1) * width // 16] for half in range(2)]
+        wasq = [held([P, width], U8, "wasq%d" % half) for half in range(2)]
+        for half in range(2):
+            nc.vector.tensor_copy(wasq[half][:], was[:].indirect(wa_entries[half]))
+
+        for r in range(ROWBLOCKS):
+            frozen(r, (2 * (r % 2), 2 * (r % 2) + 1))
+
         grouped_a = held([P, 4 * P, 4], BF16, "grouped_a")
         grouped_b = shared.tile([P, 2 * P, 4], BF16, offset=512, align_bytes=64)
         for half in range(2):
-            entries = wa_list[:, half * width // 16 : (half + 1) * width // 16]
             waq = [held([P, width], U32, "waq%d_%d" % (half, a)) for a in range(PASSES)]
-            wasq = held([P, width], U8, "wasq%d" % half)
             for a in range(PASSES):
-                nc.vector.tensor_copy(waq[a][:], waw[a][:].bitcast(U32).indirect(entries))
-            nc.vector.tensor_copy(wasq[:], was[:].indirect(entries))
+                nc.vector.tensor_copy(waq[a][:], waw[a][:].bitcast(U32).indirect(wa_entries[half]))
             for j in range(HALF):
                 m = half * HALF + j
                 slots = slice(P * m, P * (m + 1))
@@ -143,7 +148,7 @@ def tile_moe_dyl_none_kernel(
                         lhsT=xq[a][:, slots].bitcast(FP8X4),
                         lhsT_scale=xsq[4 * a :, slots],
                         rhs=waq[a][:, cols].bitcast(FP8X4),
-                        rhs_scale=wasq[4 * a :, cols],
+                        rhs_scale=wasq[half][4 * a :, cols],
                         start=(a == 0),
                         stop=(a == PASSES - 1),
                     )
@@ -159,9 +164,6 @@ def tile_moe_dyl_none_kernel(
                     out=(grouped_a, grouped_b)[m // 4][:, P * (m % 4) : P * (m % 4 + 1), :].bitcast(F32),
                     in_=turned[:].rearrange("p u s -> p s u"),
                 )
-            if half == 0:
-                frozen(0, (0, 1))
-                frozen(1, (2, 6))
 
         width = HALF * N
         wbq = [held([P, width], U32, "wbq%d" % half) for half in range(2)]
@@ -185,7 +187,7 @@ def tile_moe_dyl_none_kernel(
         for half in range(2):
             wbsq = (wbsq_a, wbsq_b)[half]
             for r in range(ROWBLOCKS):
-                y = bank(ROWBLOCKS * half + r, [P, HALF * P])
+                y = bank(r, [P, HALF * P])
                 for j in range(HALF):
                     m = half * HALF + j
                     slots = slice(P * m, P * (m + 1))
@@ -203,10 +205,10 @@ def tile_moe_dyl_none_kernel(
                     nc.scalar.copy(out=y_first[:], in_=y[:])
                 else:
                     nc.scalar.copy(out=ysb[r][:, half * HALF * P : (half + 1) * HALF * P], in_=y[:])
-        frozen(2, (4, 5))
-        frozen(3, (6, 7))
 
-        sum_banks, back_banks = (4, 5), (0, 1)
+
+        sum_banks, back_banks = (2, 3), (0, 1)
+        last = None
         for r in range(ROWBLOCKS):
             rows = slice(P * r, P * (r + 1))
             if r == 0:
@@ -219,11 +221,13 @@ def tile_moe_dyl_none_kernel(
                 nc.vector.tensor_tensor(win[r][:].indirect(tok_list[:]), ysb[r][:], gate_sb[:], MULT)
             for c in range(T // BANK):
                 toks = slice(BANK * c, BANK * (c + 1))
-                result = held([P, BANK], F32, "result%d_%d" % (r, c))
                 if r == ROWBLOCKS - 1:
-                    nc.vector.tensor_tensor(result[:], base[r][:, toks], win[r][:, toks], ADD)
-                    nc.sync.dma_start(out=out[rows, toks], in_=result[:])
+                    if c == 0:
+                        last = held([P, T], F32, "result1_1")
+                    nc.vector.tensor_tensor(last[:, toks], base[r][:, toks], win[r][:, toks], ADD)
+                    nc.sync.dma_start(out=out[rows, toks], in_=last[:, toks])
                     continue
+                result = held([P, BANK], F32, "result%d_%d" % (r, c))
                 sum_t = bank(sum_banks[c], [P, BANK])
                 for j in range(BANK // P):
                     tile_toks = slice(BANK * c + P * j, BANK * c + P * (j + 1))
@@ -236,11 +240,11 @@ def tile_moe_dyl_none_kernel(
                             start=(step == 0),
                             stop=(step == 1),
                         )
-                sum_sb = ring.tile([P, BANK], F32, tag="sum_sb", align_bytes=64)
+                sum_sb = keep.tile([P, BANK], F32, tag="sum_sb%d" % c, align_bytes=64)
                 nc.scalar.copy(out=sum_sb[:], in_=sum_t[:])
                 back = bank(back_banks[c], [P, BANK])
                 for j in range(BANK // P):
                     nc.tensor.transpose(back[:, P * j : P * (j + 1)], sum_sb[:, P * j : P * (j + 1)], ident[:])
                 nc.scalar.copy(out=result[:], in_=back[:])
-                nc.scalar.dma_start(out=out[rows, toks], in_=result[:])
-            sum_banks, back_banks = back_banks[::-1], sum_banks
+                (nc.scalar if r == ROWBLOCKS - 2 else nc.sync).dma_start(out=out[rows, toks], in_=result[:])
+            sum_banks = sum_banks[::-1]

@@ -39,7 +39,7 @@ def tile_moe_dyl_none_kernel(
             return keep.tile(shape, dtype, name=name, align_bytes=64)
 
         def bank(number, shape):
-            return psum.tile(shape, F32, name="bank%d" % number)
+            return psum.tile(shape, F32, name="bank%d" % number, offset=4 * BANK * number)
 
         def load_words(tile, words):
             nc.sync.dma_start(out=tile[:], in_=words.rearrange("p c d -> p (c d)").bitcast(I32))
@@ -169,9 +169,9 @@ def tile_moe_dyl_none_kernel(
         wbq = [held([P, width], U32, "wbq%d" % half) for half in range(2)]
         wbsq_a = held([P, width], U8, "wbsq_a")
         wb_entries = [wb_list[:, half * width // 16 : (half + 1) * width // 16] for half in range(2)]
-        nc.vector.tensor_copy(wbsq_a[:], wbs[:].indirect(wb_entries[0]))
         for half in range(2):
             nc.vector.tensor_copy(wbq[half][:], wbw[:].bitcast(U32).indirect(wb_entries[half]))
+        nc.vector.tensor_copy(wbsq_a[:], wbs[:].indirect(wb_entries[0]))
         hq = keep.tile([P, SLOTS], U32, tag="wbw_then_hq", align_bytes=64)
         hqs = held([P, SLOTS], U8, "hqs")
         for grouped, slots in ((grouped_b, slice(4 * P, SLOTS)), (grouped_a, slice(0, 4 * P))):
@@ -207,7 +207,6 @@ def tile_moe_dyl_none_kernel(
                     nc.scalar.copy(out=ysb[r][:, half * HALF * P : (half + 1) * HALF * P], in_=y[:])
 
 
-        sum_banks, back_banks = (2, 3), (0, 1)
         last = None
         for r in range(ROWBLOCKS):
             rows = slice(P * r, P * (r + 1))
@@ -219,6 +218,18 @@ def tile_moe_dyl_none_kernel(
                     nc.vector.tensor_tensor(win[r][:].indirect(entries), values, gate_sb[:, part], MULT)
             else:
                 nc.vector.tensor_tensor(win[r][:].indirect(tok_list[:]), ysb[r][:], gate_sb[:], MULT)
+            if r < ROWBLOCKS - 1:
+                sum_t = psum.tile([P, T], F32, name="sum_t", offset=4 * BANK * 2)
+                for step, term in enumerate((base[r], win[r])):
+                    for j in range(T // P):
+                        nc.tensor.matmul(
+                            sum_t[:, P * j : P * (j + 1)],
+                            lhsT=term[:, P * j : P * (j + 1)],
+                            rhs=ident[:],
+                            is_transpose=True,
+                            start=(step == 0 and j % 4 == 0),
+                            stop=(step == 1 and j % 4 == 3),
+                        )
             for c in range(T // BANK):
                 toks = slice(BANK * c, BANK * (c + 1))
                 if r == ROWBLOCKS - 1:
@@ -228,23 +239,10 @@ def tile_moe_dyl_none_kernel(
                     nc.sync.dma_start(out=out[rows, toks], in_=last[:, toks])
                     continue
                 result = held([P, BANK], F32, "result%d_%d" % (r, c))
-                sum_t = bank(sum_banks[c], [P, BANK])
-                for j in range(BANK // P):
-                    tile_toks = slice(BANK * c + P * j, BANK * c + P * (j + 1))
-                    for step, term in enumerate((base[r], win[r])):
-                        nc.tensor.matmul(
-                            sum_t[:, P * j : P * (j + 1)],
-                            lhsT=term[:, tile_toks],
-                            rhs=ident[:],
-                            is_transpose=True,
-                            start=(step == 0),
-                            stop=(step == 1),
-                        )
                 sum_sb = keep.tile([P, BANK], F32, tag="sum_sb%d" % c, align_bytes=64)
-                nc.scalar.copy(out=sum_sb[:], in_=sum_t[:])
-                back = bank(back_banks[c], [P, BANK])
+                nc.scalar.copy(out=sum_sb[:], in_=sum_t[:, toks])
+                back = bank(c, [P, BANK])
                 for j in range(BANK // P):
                     nc.tensor.transpose(back[:, P * j : P * (j + 1)], sum_sb[:, P * j : P * (j + 1)], ident[:])
                 nc.scalar.copy(out=result[:], in_=back[:])
                 (nc.scalar if r == ROWBLOCKS - 2 else nc.sync).dma_start(out=out[rows, toks], in_=result[:])
-            sum_banks = sum_banks[::-1]

@@ -15,7 +15,6 @@ U8 = mybir.dt.uint8
 FP8X4 = mybir.dt.float8_e4m3fn_x4
 FP4X4 = mybir.dt.float4_e2m1fn_x4
 MULT = mybir.AluOpType.mult
-ADD = mybir.AluOpType.add
 
 P = 128
 PASSES = K // 512
@@ -23,6 +22,9 @@ SLOTS = P * B
 BANK = 512
 HALF = B // 2
 ROWBLOCKS = N // P
+SUMMED = 2
+DIRECT = ROWBLOCKS - SUMMED
+COPY = mybir.ActivationFunctionType.Copy
 
 
 def tile_moe_dyl_none_kernel(
@@ -68,13 +70,16 @@ def tile_moe_dyl_none_kernel(
         ident = held([P, P], F32, "ident")
         win = [held([P, T], F32, "win%d" % r) for r in range(ROWBLOCKS)]
 
-        for plane in (xs, was):
-            nc.gpsimd.memset(plane[:].bitcast(I32), 0)
+        xsq1 = held([P, SLOTS], U8, "xsq1")
+
+        nc.gpsimd.memset(xs[:].bitcast(I32), 0)
         make_identity(nc, ident[:])
-        nc.gpsimd.memset(win[0][:], 0.0)
+        nc.vector.memset(was[:].bitcast(I32), 0)
         nc.vector.memset(xs1[:].bitcast(I32), 0)
         nc.vector.memset(ws[:].rearrange("p a n -> p (a n)").bitcast(I32), 0)
         nc.vector.memset(wbs[:].bitcast(I32), 0)
+        nc.vector.memset(xsq1[:].bitcast(I32), 0)
+        nc.vector.memset(win[0][:], 0.0)
 
         nc.sync.dma_start(tok_list[:], offs)
         nc.sync.dma_start(wa_list[:], offs2)
@@ -96,10 +101,10 @@ def tile_moe_dyl_none_kernel(
         load_words(wbw, wb_words[0])
         nc.sync.dma_start(out=gate_sb[:], in_=gate)
 
-        for r in range(1, ROWBLOCKS):
+        for r in range(1, SUMMED):
             nc.scalar.copy(out=win[r][:], in_=win[0][:])
 
-        base = [held([P, T], F32, "base%d" % r) for r in range(ROWBLOCKS)]
+        base = [held([P, T], F32, "base%d" % r) for r in range(SUMMED)] + win[SUMMED:]
 
         def frozen(r, banks):
             for c in range(T // BANK):
@@ -128,8 +133,40 @@ def tile_moe_dyl_none_kernel(
         for half in range(2):
             nc.vector.tensor_copy(wasq[half][:], was[:].indirect(wa_entries[half]))
 
+        for q in range(4):
+            nc.sync.dma_start(
+                out=xsq1[32 * q : 32 * q + 4, :].bitcast(I32), in_=xsq[32 * q + 4 : 32 * q + 8, :].bitcast(I32)
+            )
+
         for r in range(ROWBLOCKS):
             frozen(r, (2 * (r % 2), 2 * (r % 2) + 1))
+
+        slot_base = [held([P, 2, DIRECT * P], F32, "slot_base%d" % pair) for pair in range(HALF)]
+        for pair in range(HALF):
+            acc = bank(4 + pair, [P, 2, DIRECT * P])
+            for j in range(2):
+                slots = slice(P * (2 * pair + j), P * (2 * pair + j + 1))
+                for d in range(DIRECT):
+                    r = SUMMED + d
+                    for a in range(PASSES):
+                        nc.tensor.matmul_mx(
+                            out=acc[:, j, P * d : P * (d + 1)],
+                            lhsT=xq[a][:, slots].bitcast(FP8X4),
+                            lhsT_scale=(xsq, xsq1)[a][:, slots],
+                            rhs=ww[:, a, 2 * P * r : 2 * P * (r + 1)].bitcast(FP4X4),
+                            rhs_scale=ws[:, a, P * r : P * (r + 1)],
+                            start=(a == 0),
+                            stop=(a == PASSES - 1),
+                        )
+            nc.scalar.activation(slot_base[pair][:], acc[:], COPY)
+
+        gate_col = held([P, B], F32, "gate_col")
+        for half in range(2):
+            turned_gate = bank(7, [P, HALF, P])
+            for j in range(HALF):
+                m = half * HALF + j
+                nc.tensor.transpose(turned_gate[:, j, :], gate_sb[:, P * m : P * (m + 1)], ident[:])
+            nc.scalar.copy(out=gate_col[:, half * HALF : (half + 1) * HALF], in_=turned_gate[:, :, 0])
 
         grouped_a = held([P, 4 * P, 4], BF16, "grouped_a")
         grouped_b = shared.tile([P, 2 * P, 4], BF16, offset=512, align_bytes=64)
@@ -137,14 +174,14 @@ def tile_moe_dyl_none_kernel(
             waq = [held([P, width], U32, "waq%d_%d" % (half, a)) for a in range(PASSES)]
             for a in range(PASSES):
                 nc.vector.tensor_copy(waq[a][:], waw[a][:].bitcast(U32).indirect(wa_entries[half]))
-            for j in range(HALF):
-                m = half * HALF + j
-                slots = slice(P * m, P * (m + 1))
-                cols = slice(H * j, H * (j + 1))
-                ht = bank(j, [P, H])
-                for a in range(PASSES):
+            hts = [bank(j, [P, H]) for j in range(HALF)]
+            for a in range(PASSES):
+                for j in range(HALF):
+                    m = half * HALF + j
+                    slots = slice(P * m, P * (m + 1))
+                    cols = slice(H * j, H * (j + 1))
                     nc.tensor.matmul_mx(
-                        out=ht[:],
+                        out=hts[j][:],
                         lhsT=xq[a][:, slots].bitcast(FP8X4),
                         lhsT_scale=xsq[4 * a :, slots],
                         rhs=waq[a][:, cols].bitcast(FP8X4),
@@ -152,6 +189,9 @@ def tile_moe_dyl_none_kernel(
                         start=(a == 0),
                         stop=(a == PASSES - 1),
                     )
+            for j in range(HALF):
+                m = half * HALF + j
+                ht = hts[j]
                 hb = ring.tile([P, H], BF16, tag="hb", align_bytes=64)
                 nc.scalar.copy(
                     out=hb[:].rearrange("s (u p e) -> s u p e", u=2, e=2),
@@ -186,8 +226,8 @@ def tile_moe_dyl_none_kernel(
         ysb = [held([P, SLOTS], F32, "ysb%d" % r) for r in range(ROWBLOCKS)]
         for half in range(2):
             wbsq = (wbsq_a, wbsq_b)[half]
-            for r in range(ROWBLOCKS):
-                y = bank(r, [P, HALF * P])
+            for r in range(SUMMED):
+                y = bank(2 * half + r, [P, HALF * P])
                 for j in range(HALF):
                     m = half * HALF + j
                     slots = slice(P * m, P * (m + 1))
@@ -206,8 +246,42 @@ def tile_moe_dyl_none_kernel(
                 else:
                     nc.scalar.copy(out=ysb[r][:, half * HALF * P : (half + 1) * HALF * P], in_=y[:])
 
+        gated = [held([P, DIRECT * P], F32, "gated%d" % m) for m in range(B)]
+        for pair in range(HALF):
+            yt = bank(4 + pair, [P, 2, DIRECT * P])
+            for j in range(2):
+                m = 2 * pair + j
+                slots = slice(P * m, P * (m + 1))
+                cols = slice(N * (m % HALF) + P * SUMMED, N * (m % HALF + 1))
+                nc.tensor.matmul_mx(
+                    out=yt[:, j, :],
+                    lhsT=hq[:, slots].bitcast(FP8X4),
+                    lhsT_scale=hqs[:, slots],
+                    rhs=wbq[m // HALF][:, cols].bitcast(FP8X4),
+                    rhs_scale=(wbsq_a, wbsq_b)[m // HALF][:, cols],
+                    start=True,
+                    stop=True,
+                )
+            for j in range(2):
+                m = 2 * pair + j
+                nc.scalar.activation(gated[m][:], yt[:, j, :], COPY, scale=gate_col[:, m : m + 1])
+        for d in range(DIRECT):
+            cols = slice(P * d, P * (d + 1))
+            for half in range(2):
+                total = bank(2 * d + half, [P, HALF * P])
+                for step in range(2):
+                    for j in range(HALF):
+                        m = half * HALF + j
+                        nc.tensor.matmul(
+                            total[:, P * j : P * (j + 1)],
+                            lhsT=(slot_base[m // 2][:, m % 2, cols], gated[m][:, cols])[step],
+                            rhs=ident[:],
+                            is_transpose=True,
+                            start=(step == 0 and j == 0),
+                            stop=(step == 1 and j == HALF - 1),
+                        )
+                nc.scalar.copy(out=ysb[SUMMED + d][:, half * HALF * P : (half + 1) * HALF * P], in_=total[:])
 
-        last = None
         for r in range(ROWBLOCKS):
             rows = slice(P * r, P * (r + 1))
             if r == 0:
@@ -216,33 +290,32 @@ def tile_moe_dyl_none_kernel(
                     entries = tok_list[:, part.start // 16 : part.stop // 16]
                     values = y_first[:] if half == 0 else ysb[r][:, part]
                     nc.vector.tensor_tensor(win[r][:].indirect(entries), values, gate_sb[:, part], MULT)
-            else:
+            elif r < SUMMED:
                 nc.vector.tensor_tensor(win[r][:].indirect(tok_list[:]), ysb[r][:], gate_sb[:], MULT)
-            if r < ROWBLOCKS - 1:
-                sum_t = psum.tile([P, T], F32, name="sum_t", offset=4 * BANK * 2)
-                for step, term in enumerate((base[r], win[r])):
-                    for j in range(T // P):
-                        nc.tensor.matmul(
-                            sum_t[:, P * j : P * (j + 1)],
-                            lhsT=term[:, P * j : P * (j + 1)],
-                            rhs=ident[:],
-                            is_transpose=True,
-                            start=(step == 0 and j % 4 == 0),
-                            stop=(step == 1 and j % 4 == 3),
-                        )
+            else:
+                nc.vector.tensor_copy(win[r][:].indirect(tok_list[:]), ysb[r][:])
+                for c in range(T // BANK):
+                    toks = slice(BANK * c, BANK * (c + 1))
+                    nc.sync.dma_start(out=out[rows, toks], in_=win[r][:, toks])
+                continue
+            sum_t = psum.tile([P, T], F32, name="sum_t", offset=4 * BANK * 2)
+            for step, term in enumerate((base[r], win[r])):
+                for j in range(T // P):
+                    nc.tensor.matmul(
+                        sum_t[:, P * j : P * (j + 1)],
+                        lhsT=term[:, P * j : P * (j + 1)],
+                        rhs=ident[:],
+                        is_transpose=True,
+                        start=(step == 0 and j % 4 == 0),
+                        stop=(step == 1 and j % 4 == 3),
+                    )
             for c in range(T // BANK):
                 toks = slice(BANK * c, BANK * (c + 1))
-                if r == ROWBLOCKS - 1:
-                    if c == 0:
-                        last = held([P, T], F32, "result1_1")
-                    nc.vector.tensor_tensor(last[:, toks], base[r][:, toks], win[r][:, toks], ADD)
-                    nc.sync.dma_start(out=out[rows, toks], in_=last[:, toks])
-                    continue
                 result = held([P, BANK], F32, "result%d_%d" % (r, c))
                 sum_sb = keep.tile([P, BANK], F32, tag="sum_sb%d" % c, align_bytes=64)
                 nc.scalar.copy(out=sum_sb[:], in_=sum_t[:, toks])
-                back = bank(c, [P, BANK])
+                back = bank(4 + c, [P, BANK])
                 for j in range(BANK // P):
                     nc.tensor.transpose(back[:, P * j : P * (j + 1)], sum_sb[:, P * j : P * (j + 1)], ident[:])
                 nc.scalar.copy(out=result[:], in_=back[:])
-                (nc.scalar if r == ROWBLOCKS - 2 else nc.sync).dma_start(out=out[rows, toks], in_=result[:])
+                nc.scalar.dma_start(out=out[rows, toks], in_=result[:])

@@ -33,7 +33,7 @@ def tile_moe_dyl_none_kernel(
     nc = tc.nc
     with ExitStack() as ctx:
         keep = ctx.enter_context(tc.tile_pool(name="keep", bufs=1))
-        ring = ctx.enter_context(tc.tile_pool(name="ring", bufs=2))
+        ring = ctx.enter_context(tc.tile_pool(name="ring", bufs=HALF))
         shared = ctx.enter_context(tc.tile_pool(name="shared", bufs=1))
         psum = ctx.enter_context(tc.psum_pool(name="psum", bufs=1))
 
@@ -54,11 +54,14 @@ def tile_moe_dyl_none_kernel(
                     in_=scales[:, 4 * q : 4 * q + 4, :].bitcast(I32),
                 )
 
+        def lower_second_plane(lowered, planes):
+            nc.sync.dma_start(out=lowered[0:100, :].bitcast(I32), in_=planes[4:104, :].bitcast(I32))
+
         tok_list = held([P, SLOTS // 16], U16, "tok_list")
         wa_list = held([P, B * H // 16], U16, "wa_list")
         wb_list = held([P, B * N // 16], U16, "wb_list")
         xw = [held([P, T], I32, "xw%d" % a) for a in range(PASSES)]
-        waw = [held([P, E * H], I32, "waw%d" % a) for a in range(PASSES)]
+        waw = held([P, PASSES, E * H], I32, "waw")
         wbw = keep.tile([P, E * N], I32, tag="wbw_then_hq", align_bytes=64)
         xs = held([P, T], U8, "xs")
         xs1 = held([P, T], U8, "xs1")
@@ -74,35 +77,40 @@ def tile_moe_dyl_none_kernel(
 
         nc.gpsimd.memset(xs[:].bitcast(I32), 0)
         make_identity(nc, ident[:])
-        nc.vector.memset(was[:].bitcast(I32), 0)
-        nc.vector.memset(xs1[:].bitcast(I32), 0)
         nc.vector.memset(ws[:].rearrange("p a n -> p (a n)").bitcast(I32), 0)
+        nc.vector.memset(xs1[:].bitcast(I32), 0)
+        nc.vector.memset(was[:].bitcast(I32), 0)
         nc.vector.memset(wbs[:].bitcast(I32), 0)
         nc.vector.memset(xsq1[:].bitcast(I32), 0)
-        nc.vector.memset(win[0][:], 0.0)
+        zeros = held([P, 64], F32, "zeros")
+        nc.vector.memset(zeros[:], 0.0)
 
         nc.sync.dma_start(tok_list[:], offs)
-        nc.sync.dma_start(wa_list[:], offs2)
         load_scale_rows(xs, x_scales)
         load_words(xw[0], x_words[0])
         load_words(xw[1], x_words[1])
-        load_scale_rows(was, wa_scales)
-        load_words(waw[0], wa_words[0])
-        load_scale_rows(xs1, x_scales[1:2])
-        load_words(waw[1], wa_words[1])
+        nc.sync.dma_start(out=ww[:].bitcast(I32), in_=w_words.rearrange("a p c -> p a c").bitcast(I32))
+        nc.sync.dma_start(wa_list[:], offs2)
         for q in range(4):
             nc.sync.dma_start(
                 out=ws[32 * q : 32 * q + 4, :, :].bitcast(I32),
                 in_=w_scales[:, 4 * q : 4 * q + 4, :].rearrange("a r n -> r a n").bitcast(I32),
             )
-        nc.sync.dma_start(out=ww[:].bitcast(I32), in_=w_words.rearrange("a p c -> p a c").bitcast(I32))
+        lower_second_plane(xs1, xs)
+        load_scale_rows(was, wa_scales)
+        nc.sync.dma_start(out=waw[:], in_=wa_words.rearrange("a p c d -> p a (c d)").bitcast(I32))
+        xsq = held([P, SLOTS], U8, "xsq")
+        nc.vector.tensor_copy(xsq[:], xs[:].indirect(tok_list[:]))
+        lower_second_plane(xsq1, xsq)
         nc.sync.dma_start(wb_list[:], offs3)
-        load_scale_rows(wbs, wb_scales)
         load_words(wbw, wb_words[0])
+        load_scale_rows(wbs, wb_scales)
         nc.sync.dma_start(out=gate_sb[:], in_=gate)
 
-        for r in range(1, SUMMED):
-            nc.scalar.copy(out=win[r][:], in_=win[0][:])
+        for r in range(SUMMED):
+            nc.scalar.copy(
+                out=win[r][:].rearrange("p (a b) -> p a b", b=64), in_=zeros[:].unsqueeze(1).to_broadcast([P, T // 64, 64])
+            )
 
         base = [held([P, T], F32, "base%d" % r) for r in range(SUMMED)] + win[SUMMED:]
 
@@ -123,8 +131,6 @@ def tile_moe_dyl_none_kernel(
                 nc.scalar.copy(out=base[r][:, toks], in_=acc[:])
 
         xq = [held([P, SLOTS], U32, "xq%d" % a) for a in range(PASSES)]
-        xsq = held([P, SLOTS], U8, "xsq")
-        nc.vector.tensor_copy(xsq[:], xs[:].indirect(tok_list[:]))
         for a in range(PASSES):
             nc.vector.tensor_copy(xq[a][:], xw[a][:].bitcast(U32).indirect(tok_list[:]))
         width = HALF * H
@@ -133,17 +139,12 @@ def tile_moe_dyl_none_kernel(
         for half in range(2):
             nc.vector.tensor_copy(wasq[half][:], was[:].indirect(wa_entries[half]))
 
-        for q in range(4):
-            nc.sync.dma_start(
-                out=xsq1[32 * q : 32 * q + 4, :].bitcast(I32), in_=xsq[32 * q + 4 : 32 * q + 8, :].bitcast(I32)
-            )
-
         for r in range(ROWBLOCKS):
             frozen(r, (2 * (r % 2), 2 * (r % 2) + 1))
 
         slot_base = [held([P, 2, DIRECT * P], F32, "slot_base%d" % pair) for pair in range(HALF)]
         for pair in range(HALF):
-            acc = bank(4 + pair, [P, 2, DIRECT * P])
+            acc = bank((7, 3, 7)[pair], [P, 2, DIRECT * P])
             for j in range(2):
                 slots = slice(P * (2 * pair + j), P * (2 * pair + j + 1))
                 for d in range(DIRECT):
@@ -160,20 +161,12 @@ def tile_moe_dyl_none_kernel(
                         )
             nc.scalar.activation(slot_base[pair][:], acc[:], COPY)
 
-        gate_col = held([P, B], F32, "gate_col")
-        for half in range(2):
-            turned_gate = bank(7, [P, HALF, P])
-            for j in range(HALF):
-                m = half * HALF + j
-                nc.tensor.transpose(turned_gate[:, j, :], gate_sb[:, P * m : P * (m + 1)], ident[:])
-            nc.scalar.copy(out=gate_col[:, half * HALF : (half + 1) * HALF], in_=turned_gate[:, :, 0])
-
         grouped_a = held([P, 4 * P, 4], BF16, "grouped_a")
         grouped_b = shared.tile([P, 2 * P, 4], BF16, offset=512, align_bytes=64)
         for half in range(2):
             waq = [held([P, width], U32, "waq%d_%d" % (half, a)) for a in range(PASSES)]
             for a in range(PASSES):
-                nc.vector.tensor_copy(waq[a][:], waw[a][:].bitcast(U32).indirect(wa_entries[half]))
+                nc.vector.tensor_copy(waq[a][:], waw[:, a, :].bitcast(U32).indirect(wa_entries[half]))
             hts = [bank(j, [P, H]) for j in range(HALF)]
             for a in range(PASSES):
                 for j in range(HALF):
@@ -204,6 +197,14 @@ def tile_moe_dyl_none_kernel(
                     out=(grouped_a, grouped_b)[m // 4][:, P * (m % 4) : P * (m % 4 + 1), :].bitcast(F32),
                     in_=turned[:].rearrange("p u s -> p s u"),
                 )
+
+        gate_col = held([P, B], F32, "gate_col")
+        for half in range(2):
+            turned_gate = bank(5 + half, [P, HALF, P])
+            for j in range(HALF):
+                m = half * HALF + j
+                nc.tensor.transpose(turned_gate[:, j, :], gate_sb[:, P * m : P * (m + 1)], ident[:])
+            nc.scalar.copy(out=gate_col[:, half * HALF : (half + 1) * HALF], in_=turned_gate[:, :, 0])
 
         width = HALF * N
         wbq = [held([P, width], U32, "wbq%d" % half) for half in range(2)]

@@ -34,7 +34,6 @@ def tile_moe_dyl_none_kernel(
     with ExitStack() as ctx:
         keep = ctx.enter_context(tc.tile_pool(name="keep", bufs=1))
         ring = ctx.enter_context(tc.tile_pool(name="ring", bufs=HALF))
-        shared = ctx.enter_context(tc.tile_pool(name="shared", bufs=1))
         psum = ctx.enter_context(tc.psum_pool(name="psum", bufs=1))
 
         def held(shape, dtype, name):
@@ -44,7 +43,7 @@ def tile_moe_dyl_none_kernel(
             return psum.tile(shape, F32, name="bank%d" % number, offset=4 * BANK * number)
 
         def load_words(tile, words):
-            nc.sync.dma_start(out=tile[:], in_=words.rearrange("p c d -> p (c d)").bitcast(I32))
+            nc.sync.dma_start(out=tile, in_=words.rearrange("p c d -> p (c d)").bitcast(I32))
 
         def load_scale_rows(plane, scales):
             rows = 4 * scales.shape[0]
@@ -61,7 +60,7 @@ def tile_moe_dyl_none_kernel(
         wa_list = held([P, B * H // 16], U16, "wa_list")
         wb_list = held([P, B * N // 16], U16, "wb_list")
         xw = [held([P, T], I32, "xw%d" % a) for a in range(PASSES)]
-        waw = held([P, PASSES, E * H], I32, "waw")
+        waw = held([P, PASSES * E * H], I32, "waw")
         wbw = keep.tile([P, E * N], I32, tag="wbw_then_hq", align_bytes=64)
         xs = held([P, T], U8, "xs")
         xs1 = held([P, T], U8, "xs1")
@@ -87,8 +86,8 @@ def tile_moe_dyl_none_kernel(
 
         nc.sync.dma_start(tok_list[:], offs)
         load_scale_rows(xs, x_scales)
-        load_words(xw[0], x_words[0])
-        load_words(xw[1], x_words[1])
+        load_words(xw[0][:], x_words[0])
+        load_words(xw[1][:], x_words[1])
         nc.sync.dma_start(out=ww[:].bitcast(I32), in_=w_words.rearrange("a p c -> p a c").bitcast(I32))
         nc.sync.dma_start(wa_list[:], offs2)
         for q in range(4):
@@ -98,12 +97,13 @@ def tile_moe_dyl_none_kernel(
             )
         lower_second_plane(xs1, xs)
         load_scale_rows(was, wa_scales)
-        nc.sync.dma_start(out=waw[:], in_=wa_words.rearrange("a p c d -> p a (c d)").bitcast(I32))
+        load_words(waw[:, : E * H], wa_words[0])
         xsq = held([P, SLOTS], U8, "xsq")
         nc.vector.tensor_copy(xsq[:], xs[:].indirect(tok_list[:]))
         lower_second_plane(xsq1, xsq)
+        load_words(waw[:, E * H :], wa_words[1])
         nc.sync.dma_start(wb_list[:], offs3)
-        load_words(wbw, wb_words[0])
+        load_words(wbw[:], wb_words[0])
         load_scale_rows(wbs, wb_scales)
         nc.sync.dma_start(out=gate_sb[:], in_=gate)
 
@@ -161,12 +161,13 @@ def tile_moe_dyl_none_kernel(
                         )
             nc.scalar.activation(slot_base[pair][:], acc[:], COPY)
 
-        grouped_a = held([P, 4 * P, 4], BF16, "grouped_a")
-        grouped_b = shared.tile([P, 2 * P, 4], BF16, offset=512, align_bytes=64)
+        grouped_a = keep.tile([P, 4 * P, 4], BF16, tag="grouped_then_wbsq", align_bytes=64)
+        grouped_b = held([P, 2 * P, 4], BF16, "grouped_b")
         for half in range(2):
             waq = [held([P, width], U32, "waq%d_%d" % (half, a)) for a in range(PASSES)]
             for a in range(PASSES):
-                nc.vector.tensor_copy(waq[a][:], waw[:, a, :].bitcast(U32).indirect(wa_entries[half]))
+                window = waw[:, E * H * a : E * H * (PASSES if half else a + 1)]
+                nc.vector.tensor_copy(waq[a][:], window.bitcast(U32).indirect(wa_entries[half]))
             hts = [bank(j, [P, H]) for j in range(HALF)]
             for a in range(PASSES):
                 for j in range(HALF):
@@ -215,15 +216,19 @@ def tile_moe_dyl_none_kernel(
         nc.vector.tensor_copy(wbsq_a[:], wbs[:].indirect(wb_entries[0]))
         hq = keep.tile([P, SLOTS], U32, tag="wbw_then_hq", align_bytes=64)
         hqs = held([P, SLOTS], U8, "hqs")
-        for grouped, slots in ((grouped_b, slice(4 * P, SLOTS)), (grouped_a, slice(0, 4 * P))):
+
+        def quantise(grouped, slots):
             nc.vector.quantize_mx(
                 out=hq[:, slots].bitcast(FP8X4),
                 scales=hqs[:, slots],
                 in_=grouped[:].rearrange("p s t -> p (s t)"),
             )
-        wbsq_b = shared.tile([P, width], U8, offset=0, align_bytes=64)
+
+        quantise(grouped_a, slice(0, 4 * P))
+        wbsq_b = keep.tile([P, width], U8, tag="grouped_then_wbsq", align_bytes=64)
         nc.vector.tensor_copy(wbsq_b[:], wbs[:].indirect(wb_entries[1]))
-        y_first = shared.tile([P, HALF * P], F32, offset=1536, align_bytes=64)
+        quantise(grouped_b, slice(4 * P, SLOTS))
+        y_first = held([P, HALF * P], F32, "y_first")
         ysb = [held([P, SLOTS], F32, "ysb%d" % r) for r in range(ROWBLOCKS)]
         for half in range(2):
             wbsq = (wbsq_a, wbsq_b)[half]

@@ -45,10 +45,10 @@ def tile_moe_dyl_none_kernel(
         def load_words(tile, words):
             nc.sync.dma_start(out=tile, in_=words.rearrange("p c d -> p (c d)").bitcast(I32))
 
-        def load_scale_rows(plane, scales):
+        def load_scale_rows(plane, scales, quadrants, queue=nc.sync):
             rows = 4 * scales.shape[0]
-            for q in range(4):
-                nc.sync.dma_start(
+            for q in quadrants:
+                queue.dma_start(
                     out=plane[32 * q : 32 * q + rows, :].bitcast(I32),
                     in_=scales[:, 4 * q : 4 * q + 4, :].bitcast(I32),
                 )
@@ -77,26 +77,28 @@ def tile_moe_dyl_none_kernel(
         nc.gpsimd.memset(xs[:].bitcast(I32), 0)
         make_identity(nc, ident[:])
         nc.vector.memset(ws[:].rearrange("p a n -> p (a n)").bitcast(I32), 0)
-        nc.vector.memset(xs1[:].bitcast(I32), 0)
         nc.vector.memset(was[:].bitcast(I32), 0)
+        nc.vector.memset(xs1[:].bitcast(I32), 0)
         nc.vector.memset(wbs[:].bitcast(I32), 0)
         nc.vector.memset(xsq1[:].bitcast(I32), 0)
         zeros = held([P, 64], F32, "zeros")
         nc.vector.memset(zeros[:], 0.0)
 
         nc.sync.dma_start(tok_list[:], offs)
-        load_scale_rows(xs, x_scales)
+        load_scale_rows(xs, x_scales, range(2))
+        load_scale_rows(xs, x_scales, range(2, 4), nc.scalar)
         load_words(xw[0][:], x_words[0])
-        load_words(xw[1][:], x_words[1])
-        nc.sync.dma_start(out=ww[:].bitcast(I32), in_=w_words.rearrange("a p c -> p a c").bitcast(I32))
-        nc.sync.dma_start(wa_list[:], offs2)
         for q in range(4):
             nc.sync.dma_start(
                 out=ws[32 * q : 32 * q + 4, :, :].bitcast(I32),
                 in_=w_scales[:, 4 * q : 4 * q + 4, :].rearrange("a r n -> r a n").bitcast(I32),
             )
+        load_words(xw[1][:], x_words[1])
+        load_scale_rows(was, wa_scales, range(2))
+        nc.sync.dma_start(out=ww[:].bitcast(I32), in_=w_words.rearrange("a p c -> p a c").bitcast(I32))
         lower_second_plane(xs1, xs)
-        load_scale_rows(was, wa_scales)
+        load_scale_rows(was, wa_scales, range(2, 4))
+        nc.sync.dma_start(wa_list[:], offs2)
         load_words(waw[:, : E * H], wa_words[0])
         xsq = held([P, SLOTS], U8, "xsq")
         nc.vector.tensor_copy(xsq[:], xs[:].indirect(tok_list[:]))
@@ -104,12 +106,12 @@ def tile_moe_dyl_none_kernel(
         load_words(waw[:, E * H :], wa_words[1])
         nc.sync.dma_start(wb_list[:], offs3)
         load_words(wbw[:], wb_words[0])
-        load_scale_rows(wbs, wb_scales)
+        load_scale_rows(wbs, wb_scales, range(4))
         nc.sync.dma_start(out=gate_sb[:], in_=gate)
 
         for r in range(SUMMED):
-            nc.scalar.copy(
-                out=win[r][:].rearrange("p (a b) -> p a b", b=64), in_=zeros[:].unsqueeze(1).to_broadcast([P, T // 64, 64])
+            nc.scalar.activation(
+                win[r][:].rearrange("p (a b) -> p a b", b=64), zeros[:].unsqueeze(1).to_broadcast([P, T // 64, 64]), COPY
             )
 
         base = [held([P, T], F32, "base%d" % r) for r in range(SUMMED)] + win[SUMMED:]
@@ -228,7 +230,6 @@ def tile_moe_dyl_none_kernel(
         wbsq_b = keep.tile([P, width], U8, tag="grouped_then_wbsq", align_bytes=64)
         nc.vector.tensor_copy(wbsq_b[:], wbs[:].indirect(wb_entries[1]))
         quantise(grouped_b, slice(4 * P, SLOTS))
-        y_first = held([P, HALF * P], F32, "y_first")
         ysb = [held([P, SLOTS], F32, "ysb%d" % r) for r in range(ROWBLOCKS)]
         for half in range(2):
             wbsq = (wbsq_a, wbsq_b)[half]
@@ -247,10 +248,10 @@ def tile_moe_dyl_none_kernel(
                         start=True,
                         stop=True,
                     )
-                if half == 0 and r == 0:
-                    nc.scalar.copy(out=y_first[:], in_=y[:])
-                else:
-                    nc.scalar.copy(out=ysb[r][:, half * HALF * P : (half + 1) * HALF * P], in_=y[:])
+                part = slice(half * HALF * P, (half + 1) * HALF * P)
+                nc.scalar.copy(out=ysb[r][:, part], in_=y[:])
+                entries = tok_list[:, part.start // 16 : part.stop // 16]
+                nc.vector.tensor_tensor(win[r][:].indirect(entries), ysb[r][:, part], gate_sb[:, part], MULT)
 
         gated = [held([P, DIRECT * P], F32, "gated%d" % m) for m in range(B)]
         for pair in range(HALF):
@@ -290,19 +291,9 @@ def tile_moe_dyl_none_kernel(
 
         for r in range(ROWBLOCKS):
             rows = slice(P * r, P * (r + 1))
-            if r == 0:
-                for half in range(2):
-                    part = slice(half * HALF * P, (half + 1) * HALF * P)
-                    entries = tok_list[:, part.start // 16 : part.stop // 16]
-                    values = y_first[:] if half == 0 else ysb[r][:, part]
-                    nc.vector.tensor_tensor(win[r][:].indirect(entries), values, gate_sb[:, part], MULT)
-            elif r < SUMMED:
-                nc.vector.tensor_tensor(win[r][:].indirect(tok_list[:]), ysb[r][:], gate_sb[:], MULT)
-            else:
+            if r >= SUMMED:
                 nc.vector.tensor_copy(win[r][:].indirect(tok_list[:]), ysb[r][:])
-                for c in range(T // BANK):
-                    toks = slice(BANK * c, BANK * (c + 1))
-                    nc.sync.dma_start(out=out[rows, toks], in_=win[r][:, toks])
+                nc.sync.dma_start(out=out[rows, :], in_=win[r][:])
                 continue
             sum_t = psum.tile([P, T], F32, name="sum_t", offset=4 * BANK * 2)
             for step, term in enumerate((base[r], win[r])):

@@ -33,7 +33,7 @@ def tile_moe_dyl_none_kernel(
     nc = tc.nc
     with ExitStack() as ctx:
         keep = ctx.enter_context(tc.tile_pool(name="keep", bufs=1))
-        ring = ctx.enter_context(tc.tile_pool(name="ring", bufs=HALF))
+        ring = ctx.enter_context(tc.tile_pool(name="ring", bufs=2))
         psum = ctx.enter_context(tc.psum_pool(name="psum", bufs=1))
 
         def held(shape, dtype, name):
@@ -74,15 +74,11 @@ def tile_moe_dyl_none_kernel(
 
         xsq1 = held([P, SLOTS], U8, "xsq1")
 
-        nc.gpsimd.memset(xs[:].bitcast(I32), 0)
+        for plane in (xs, xs1, xsq1, wbs):
+            nc.gpsimd.memset(plane[:].bitcast(I32), 0)
         make_identity(nc, ident[:])
         nc.vector.memset(ws[:].rearrange("p a n -> p (a n)").bitcast(I32), 0)
         nc.vector.memset(was[:].bitcast(I32), 0)
-        nc.vector.memset(xs1[:].bitcast(I32), 0)
-        nc.vector.memset(wbs[:].bitcast(I32), 0)
-        nc.vector.memset(xsq1[:].bitcast(I32), 0)
-        zeros = held([P, 64], F32, "zeros")
-        nc.vector.memset(zeros[:], 0.0)
 
         nc.sync.dma_start(tok_list[:], offs)
         load_scale_rows(xs, x_scales, range(2))
@@ -111,7 +107,10 @@ def tile_moe_dyl_none_kernel(
 
         for r in range(SUMMED):
             nc.scalar.activation(
-                win[r][:].rearrange("p (a b) -> p a b", b=64), zeros[:].unsqueeze(1).to_broadcast([P, T // 64, 64]), COPY
+                win[r][:].rearrange("p (a b) -> p a b", b=P),
+                ident[:].unsqueeze(1).to_broadcast([P, T // P, P]),
+                COPY,
+                scale=0.0,
             )
 
         base = [held([P, T], F32, "base%d" % r) for r in range(SUMMED)] + win[SUMMED:]
@@ -163,7 +162,7 @@ def tile_moe_dyl_none_kernel(
                         )
             nc.scalar.activation(slot_base[pair][:], acc[:], COPY)
 
-        grouped_a = keep.tile([P, 4 * P, 4], BF16, tag="grouped_then_wbsq", align_bytes=64)
+        grouped_a = held([P, 4 * P, 4], BF16, "grouped_a")
         grouped_b = held([P, 2 * P, 4], BF16, "grouped_b")
         for half in range(2):
             waq = [held([P, width], U32, "waq%d_%d" % (half, a)) for a in range(PASSES)]
@@ -188,7 +187,10 @@ def tile_moe_dyl_none_kernel(
             for j in range(HALF):
                 m = half * HALF + j
                 ht = hts[j]
-                hb = ring.tile([P, H], BF16, tag="hb", align_bytes=64)
+                if m < B - 1:
+                    hb = ring.tile([P, H], BF16, tag="hb", align_bytes=64)
+                else:
+                    hb = keep.tile([P, H], BF16, tag="hb_then_wbsq", align_bytes=64)
                 nc.scalar.copy(
                     out=hb[:].rearrange("s (u p e) -> s u p e", u=2, e=2),
                     in_=ht[:].rearrange("s (p u e) -> s u p e", u=2, e=2),
@@ -227,31 +229,33 @@ def tile_moe_dyl_none_kernel(
             )
 
         quantise(grouped_a, slice(0, 4 * P))
-        wbsq_b = keep.tile([P, width], U8, tag="grouped_then_wbsq", align_bytes=64)
+        wbsq_b = keep.tile([P, width], U8, tag="hb_then_wbsq", align_bytes=64)
         nc.vector.tensor_copy(wbsq_b[:], wbs[:].indirect(wb_entries[1]))
         quantise(grouped_b, slice(4 * P, SLOTS))
         ysb = [held([P, SLOTS], F32, "ysb%d" % r) for r in range(ROWBLOCKS)]
-        for half in range(2):
+        for number, (r, half) in enumerate(((0, 0), (1, 0), (1, 1), (0, 1))):
             wbsq = (wbsq_a, wbsq_b)[half]
-            for r in range(SUMMED):
-                y = bank(2 * half + r, [P, HALF * P])
-                for j in range(HALF):
-                    m = half * HALF + j
-                    slots = slice(P * m, P * (m + 1))
-                    cols = slice(N * j + P * r, N * j + P * (r + 1))
-                    nc.tensor.matmul_mx(
-                        out=y[:, P * j : P * (j + 1)],
-                        lhsT=wbq[half][:, cols].bitcast(FP8X4),
-                        lhsT_scale=wbsq[:, cols],
-                        rhs=hq[:, slots].bitcast(FP8X4),
-                        rhs_scale=hqs[:, slots],
-                        start=True,
-                        stop=True,
-                    )
-                part = slice(half * HALF * P, (half + 1) * HALF * P)
-                nc.scalar.copy(out=ysb[r][:, part], in_=y[:])
+            y = bank(number, [P, HALF * P])
+            for j in range(HALF):
+                m = half * HALF + j
+                slots = slice(P * m, P * (m + 1))
+                cols = slice(N * j + P * r, N * j + P * (r + 1))
+                nc.tensor.matmul_mx(
+                    out=y[:, P * j : P * (j + 1)],
+                    lhsT=wbq[half][:, cols].bitcast(FP8X4),
+                    lhsT_scale=wbsq[:, cols],
+                    rhs=hq[:, slots].bitcast(FP8X4),
+                    rhs_scale=hqs[:, slots],
+                    start=True,
+                    stop=True,
+                )
+            part = slice(half * HALF * P, (half + 1) * HALF * P)
+            nc.scalar.copy(out=ysb[r][:, part], in_=y[:])
+            if r == 0:
                 entries = tok_list[:, part.start // 16 : part.stop // 16]
                 nc.vector.tensor_tensor(win[r][:].indirect(entries), ysb[r][:, part], gate_sb[:, part], MULT)
+            elif half == 1:
+                nc.vector.tensor_tensor(win[r][:].indirect(tok_list[:]), ysb[r][:], gate_sb[:], MULT)
 
         gated = [held([P, DIRECT * P], F32, "gated%d" % m) for m in range(B)]
         for pair in range(HALF):
@@ -289,7 +293,7 @@ def tile_moe_dyl_none_kernel(
                         )
                 nc.scalar.copy(out=ysb[SUMMED + d][:, half * HALF * P : (half + 1) * HALF * P], in_=total[:])
 
-        for r in range(ROWBLOCKS):
+        for r in (2, 3, 1, 0):
             rows = slice(P * r, P * (r + 1))
             if r >= SUMMED:
                 nc.vector.tensor_copy(win[r][:].indirect(tok_list[:]), ysb[r][:])

@@ -45,65 +45,67 @@ def tile_moe_dyl_none_kernel(
         def load_words(tile, words):
             nc.sync.dma_start(out=tile, in_=words.rearrange("p c d -> p (c d)").bitcast(I32))
 
-        def load_scale_rows(plane, scales, quadrants, queue=nc.sync):
+        def load_scale_rows(plane, scales):
             rows = 4 * scales.shape[0]
-            for q in quadrants:
-                queue.dma_start(
-                    out=plane[32 * q : 32 * q + rows, :].bitcast(I32),
+            for q in range(4):
+                nc.sync.dma_start(
+                    out=plane[32 * q : 32 * q + rows, : scales.shape[2]].bitcast(I32),
                     in_=scales[:, 4 * q : 4 * q + 4, :].bitcast(I32),
                 )
 
-        def lower_second_plane(lowered, planes):
-            nc.sync.dma_start(out=lowered[0:100, :].bitcast(I32), in_=planes[4:104, :].bitcast(I32))
+        def load_planes(planes, scales):
+            for q in range(4):
+                nc.sync.dma_start(
+                    out=planes[32 * q : 32 * q + 4, :, :].bitcast(I32),
+                    in_=scales[:, 4 * q : 4 * q + 4, :].rearrange("a r n -> r a n").bitcast(I32),
+                )
 
         tok_list = held([P, SLOTS // 16], U16, "tok_list")
         wa_list = held([P, B * H // 16], U16, "wa_list")
         wb_list = held([P, B * N // 16], U16, "wb_list")
         xw = [held([P, T], I32, "xw%d" % a) for a in range(PASSES)]
-        waw = held([P, PASSES * E * H], I32, "waw")
-        wbw = keep.tile([P, E * N], I32, tag="wbw_then_hq", align_bytes=64)
-        xs = held([P, T], U8, "xs")
-        xs1 = held([P, T], U8, "xs1")
-        was = held([P, E * H], U8, "was")
+        xs = keep.tile([P, T + 4], U8, tag="xs_then_waw", align_bytes=64)
+        xs_planes = keep.tile([P, PASSES, T], U8, tag="planes_then_gate", align_bytes=64)
+        was = held([P, E * H + 4], U8, "was")
         wbs = held([P, E * N], U8, "wbs")
         ww = held([P, PASSES, 2 * N], U8, "ww")
         ws = held([P, PASSES, N], U8, "ws")
-        gate_sb = held([P, SLOTS], F32, "gate_sb")
         ident = held([P, P], F32, "ident")
         win = [held([P, T], F32, "win%d" % r) for r in range(ROWBLOCKS)]
 
-        xsq1 = held([P, SLOTS], U8, "xsq1")
-
-        for plane in (xs, xs1, xsq1, wbs):
-            nc.gpsimd.memset(plane[:].bitcast(I32), 0)
-        make_identity(nc, ident[:])
-        nc.vector.memset(ws[:].rearrange("p a n -> p (a n)").bitcast(I32), 0)
+        nc.vector.memset(xs[32:64, :].bitcast(I32), 0)
+        nc.vector.memset(xs[64:, :].bitcast(I32), 0)
         nc.vector.memset(was[:].bitcast(I32), 0)
+        nc.gpsimd.memset(ws[:].rearrange("p a n -> p (a n)").bitcast(I32), 0)
+        nc.gpsimd.memset(xs_planes[:].rearrange("p a n -> p (a n)").bitcast(I32), 0)
+        make_identity(nc, ident[:])
+        nc.gpsimd.memset(wbs[:].bitcast(I32), 0)
 
         nc.sync.dma_start(tok_list[:], offs)
-        load_scale_rows(xs, x_scales, range(2))
-        load_scale_rows(xs, x_scales, range(2, 4), nc.scalar)
+        nc.scalar.dma_start(out=xs[:32, :T].bitcast(I32), in_=x_scales.rearrange("a b t -> (a b) t").bitcast(I32))
         load_words(xw[0][:], x_words[0])
-        for q in range(4):
-            nc.sync.dma_start(
-                out=ws[32 * q : 32 * q + 4, :, :].bitcast(I32),
-                in_=w_scales[:, 4 * q : 4 * q + 4, :].rearrange("a r n -> r a n").bitcast(I32),
-            )
         load_words(xw[1][:], x_words[1])
-        load_scale_rows(was, wa_scales, range(2))
-        nc.sync.dma_start(out=ww[:].bitcast(I32), in_=w_words.rearrange("a p c -> p a c").bitcast(I32))
-        lower_second_plane(xs1, xs)
-        load_scale_rows(was, wa_scales, range(2, 4))
+        load_scale_rows(was, wa_scales)
         nc.sync.dma_start(wa_list[:], offs2)
+        load_planes(ws, w_scales)
+        load_planes(xs_planes, x_scales)
+        nc.sync.dma_start(out=ww[:].bitcast(I32), in_=w_words.rearrange("a p c -> p a c").bitcast(I32))
+        xs_rows = keep.tile([P, SLOTS], U8, tag="wbw_then_hq", align_bytes=64)
+        nc.vector.tensor_copy(xs_rows[:], xs[:, :T].indirect(tok_list[:]))
+        waw = keep.tile([P, PASSES * E * H], I32, tag="xs_then_waw", align_bytes=64)
         load_words(waw[:, : E * H], wa_words[0])
-        xsq = held([P, SLOTS], U8, "xsq")
-        nc.vector.tensor_copy(xsq[:], xs[:].indirect(tok_list[:]))
-        lower_second_plane(xsq1, xsq)
         load_words(waw[:, E * H :], wa_words[1])
+        xsq = [held([P, SLOTS], U8, "xsq%d" % a) for a in range(PASSES)]
+        for a in range(PASSES):
+            for q in range(4):
+                first = 16 * a + 4 * q
+                nc.sync.dma_start(
+                    out=xsq[a][32 * q : 32 * (q + 1), :].bitcast(I32), in_=xs_rows[first : first + 32, :].bitcast(I32)
+                )
         nc.sync.dma_start(wb_list[:], offs3)
+        wbw = keep.tile([P, E * N], I32, tag="wbw_then_hq", align_bytes=64)
         load_words(wbw[:], wb_words[0])
-        load_scale_rows(wbs, wb_scales, range(4))
-        nc.sync.dma_start(out=gate_sb[:], in_=gate)
+        load_scale_rows(wbs, wb_scales)
 
         for r in range(SUMMED):
             nc.scalar.activation(
@@ -125,7 +127,7 @@ def tile_moe_dyl_none_kernel(
                         lhsT=ww[:, a, 2 * P * r : 2 * P * (r + 1)].bitcast(FP4X4),
                         lhsT_scale=ws[:, a, P * r : P * (r + 1)],
                         rhs=xw[a][:, toks].bitcast(FP8X4),
-                        rhs_scale=(xs, xs1)[a][:, toks],
+                        rhs_scale=xs_planes[:, a, toks],
                         start=(a == 0),
                         stop=(a == PASSES - 1),
                     )
@@ -142,25 +144,8 @@ def tile_moe_dyl_none_kernel(
 
         for r in range(ROWBLOCKS):
             frozen(r, (2 * (r % 2), 2 * (r % 2) + 1))
-
-        slot_base = [held([P, 2, DIRECT * P], F32, "slot_base%d" % pair) for pair in range(HALF)]
-        for pair in range(HALF):
-            acc = bank((7, 3, 7)[pair], [P, 2, DIRECT * P])
-            for j in range(2):
-                slots = slice(P * (2 * pair + j), P * (2 * pair + j + 1))
-                for d in range(DIRECT):
-                    r = SUMMED + d
-                    for a in range(PASSES):
-                        nc.tensor.matmul_mx(
-                            out=acc[:, j, P * d : P * (d + 1)],
-                            lhsT=xq[a][:, slots].bitcast(FP8X4),
-                            lhsT_scale=(xsq, xsq1)[a][:, slots],
-                            rhs=ww[:, a, 2 * P * r : 2 * P * (r + 1)].bitcast(FP4X4),
-                            rhs_scale=ws[:, a, P * r : P * (r + 1)],
-                            start=(a == 0),
-                            stop=(a == PASSES - 1),
-                        )
-            nc.scalar.activation(slot_base[pair][:], acc[:], COPY)
+        gate_sb = keep.tile([P, SLOTS], F32, tag="planes_then_gate", align_bytes=64)
+        nc.sync.dma_start(out=gate_sb[:], in_=gate)
 
         grouped_a = held([P, 4 * P, 4], BF16, "grouped_a")
         grouped_b = held([P, 2 * P, 4], BF16, "grouped_b")
@@ -178,7 +163,7 @@ def tile_moe_dyl_none_kernel(
                     nc.tensor.matmul_mx(
                         out=hts[j][:],
                         lhsT=xq[a][:, slots].bitcast(FP8X4),
-                        lhsT_scale=xsq[4 * a :, slots],
+                        lhsT_scale=xsq[a][:, slots],
                         rhs=waq[a][:, cols].bitcast(FP8X4),
                         rhs_scale=wasq[half][4 * a :, cols],
                         start=(a == 0),
@@ -203,9 +188,28 @@ def tile_moe_dyl_none_kernel(
                     in_=turned[:].rearrange("p u s -> p s u"),
                 )
 
+        slot_base = [held([P, 2, DIRECT * P], F32, "slot_base%d" % pair) for pair in range(HALF)]
+        for pair in range(HALF):
+            acc = bank(4 + pair, [P, 2, DIRECT * P])
+            for j in range(2):
+                slots = slice(P * (2 * pair + j), P * (2 * pair + j + 1))
+                for d in range(DIRECT):
+                    r = SUMMED + d
+                    for a in range(PASSES):
+                        nc.tensor.matmul_mx(
+                            out=acc[:, j, P * d : P * (d + 1)],
+                            lhsT=xq[a][:, slots].bitcast(FP8X4),
+                            lhsT_scale=xsq[a][:, slots],
+                            rhs=ww[:, a, 2 * P * r : 2 * P * (r + 1)].bitcast(FP4X4),
+                            rhs_scale=ws[:, a, P * r : P * (r + 1)],
+                            start=(a == 0),
+                            stop=(a == PASSES - 1),
+                        )
+            nc.scalar.activation(slot_base[pair][:], acc[:], COPY)
+
         gate_col = held([P, B], F32, "gate_col")
         for half in range(2):
-            turned_gate = bank(5 + half, [P, HALF, P])
+            turned_gate = bank((7, 3)[half], [P, HALF, P])
             for j in range(HALF):
                 m = half * HALF + j
                 nc.tensor.transpose(turned_gate[:, j, :], gate_sb[:, P * m : P * (m + 1)], ident[:])

@@ -24,6 +24,7 @@ HALF = B // 2
 ROWBLOCKS = N // P
 SUMMED = 2
 DIRECT = ROWBLOCKS - SUMMED
+WA_BYTES = 4 * PASSES * E * H
 COPY = mybir.ActivationFunctionType.Copy
 
 
@@ -33,7 +34,7 @@ def tile_moe_dyl_none_kernel(
     nc = tc.nc
     with ExitStack() as ctx:
         keep = ctx.enter_context(tc.tile_pool(name="keep", bufs=1))
-        ring = ctx.enter_context(tc.tile_pool(name="ring", bufs=2))
+        placed = ctx.enter_context(tc.tile_pool(name="placed", bufs=1))
         psum = ctx.enter_context(tc.psum_pool(name="psum", bufs=1))
 
         def held(shape, dtype, name):
@@ -64,7 +65,7 @@ def tile_moe_dyl_none_kernel(
         wa_list = held([P, B * H // 16], U16, "wa_list")
         wb_list = held([P, B * N // 16], U16, "wb_list")
         xw = [held([P, T], I32, "xw%d" % a) for a in range(PASSES)]
-        xs = keep.tile([P, T + 4], U8, tag="xs_then_waw", align_bytes=64)
+        xs = placed.tile([P, T + 4], U8, name="xs", offset=WA_BYTES - T // 2, align_bytes=64)
         xs_planes = keep.tile([P, PASSES, T], U8, tag="planes_then_gate", align_bytes=64)
         was = held([P, E * H + 4], U8, "was")
         wbs = held([P, E * N], U8, "wbs")
@@ -87,13 +88,15 @@ def tile_moe_dyl_none_kernel(
         load_words(xw[1][:], x_words[1])
         load_scale_rows(was, wa_scales)
         nc.sync.dma_start(wa_list[:], offs2)
+        nc.sync.dma_start(wb_list[:], offs3)
         load_planes(ws, w_scales)
         load_planes(xs_planes, x_scales)
         nc.sync.dma_start(out=ww[:].bitcast(I32), in_=w_words.rearrange("a p c -> p a c").bitcast(I32))
-        xs_rows = keep.tile([P, SLOTS], U8, tag="wbw_then_hq", align_bytes=64)
+        xs_rows = held([P, SLOTS], U8, "xs_rows")
         nc.vector.tensor_copy(xs_rows[:], xs[:, :T].indirect(tok_list[:]))
-        waw = keep.tile([P, PASSES * E * H], I32, tag="xs_then_waw", align_bytes=64)
+        waw = placed.tile([P, PASSES * E * H], I32, name="waw", offset=0, align_bytes=64)
         load_words(waw[:, : E * H], wa_words[0])
+        load_scale_rows(wbs, wb_scales)
         load_words(waw[:, E * H :], wa_words[1])
         xsq = [held([P, SLOTS], U8, "xsq%d" % a) for a in range(PASSES)]
         for a in range(PASSES):
@@ -102,10 +105,8 @@ def tile_moe_dyl_none_kernel(
                 nc.sync.dma_start(
                     out=xsq[a][32 * q : 32 * (q + 1), :].bitcast(I32), in_=xs_rows[first : first + 32, :].bitcast(I32)
                 )
-        nc.sync.dma_start(wb_list[:], offs3)
-        wbw = keep.tile([P, E * N], I32, tag="wbw_then_hq", align_bytes=64)
+        wbw = placed.tile([P, E * N], I32, name="wbw", offset=WA_BYTES, align_bytes=64)
         load_words(wbw[:], wb_words[0])
-        load_scale_rows(wbs, wb_scales)
 
         for r in range(SUMMED):
             nc.scalar.activation(
@@ -142,6 +143,10 @@ def tile_moe_dyl_none_kernel(
         for half in range(2):
             nc.vector.tensor_copy(wasq[half][:], was[:].indirect(wa_entries[half]))
 
+        wbsq_a = held([P, width], U8, "wbsq_a")
+        wb_entries = [wb_list[:, half * width // 16 : (half + 1) * width // 16] for half in range(2)]
+        nc.vector.tensor_copy(wbsq_a[:], wbs[:].indirect(wb_entries[0]))
+
         for r in range(ROWBLOCKS):
             frozen(r, (2 * (r % 2), 2 * (r % 2) + 1))
         gate_sb = keep.tile([P, SLOTS], F32, tag="planes_then_gate", align_bytes=64)
@@ -172,10 +177,7 @@ def tile_moe_dyl_none_kernel(
             for j in range(HALF):
                 m = half * HALF + j
                 ht = hts[j]
-                if m < B - 1:
-                    hb = ring.tile([P, H], BF16, tag="hb", align_bytes=64)
-                else:
-                    hb = keep.tile([P, H], BF16, tag="hb_then_wbsq", align_bytes=64)
+                hb = keep.tile([P, H], BF16, tag="hb%d" % (m % 2), align_bytes=64)
                 nc.scalar.copy(
                     out=hb[:].rearrange("s (u p e) -> s u p e", u=2, e=2),
                     in_=ht[:].rearrange("s (p u e) -> s u p e", u=2, e=2),
@@ -188,25 +190,6 @@ def tile_moe_dyl_none_kernel(
                     in_=turned[:].rearrange("p u s -> p s u"),
                 )
 
-        slot_base = [held([P, 2, DIRECT * P], F32, "slot_base%d" % pair) for pair in range(HALF)]
-        for pair in range(HALF):
-            acc = bank(4 + pair, [P, 2, DIRECT * P])
-            for j in range(2):
-                slots = slice(P * (2 * pair + j), P * (2 * pair + j + 1))
-                for d in range(DIRECT):
-                    r = SUMMED + d
-                    for a in range(PASSES):
-                        nc.tensor.matmul_mx(
-                            out=acc[:, j, P * d : P * (d + 1)],
-                            lhsT=xq[a][:, slots].bitcast(FP8X4),
-                            lhsT_scale=xsq[a][:, slots],
-                            rhs=ww[:, a, 2 * P * r : 2 * P * (r + 1)].bitcast(FP4X4),
-                            rhs_scale=ws[:, a, P * r : P * (r + 1)],
-                            start=(a == 0),
-                            stop=(a == PASSES - 1),
-                        )
-            nc.scalar.activation(slot_base[pair][:], acc[:], COPY)
-
         gate_col = held([P, B], F32, "gate_col")
         for half in range(2):
             turned_gate = bank((7, 3)[half], [P, HALF, P])
@@ -217,12 +200,9 @@ def tile_moe_dyl_none_kernel(
 
         width = HALF * N
         wbq = [held([P, width], U32, "wbq%d" % half) for half in range(2)]
-        wbsq_a = held([P, width], U8, "wbsq_a")
-        wb_entries = [wb_list[:, half * width // 16 : (half + 1) * width // 16] for half in range(2)]
         for half in range(2):
             nc.vector.tensor_copy(wbq[half][:], wbw[:].bitcast(U32).indirect(wb_entries[half]))
-        nc.vector.tensor_copy(wbsq_a[:], wbs[:].indirect(wb_entries[0]))
-        hq = keep.tile([P, SLOTS], U32, tag="wbw_then_hq", align_bytes=64)
+        hq = held([P, SLOTS], U32, "hq")
         hqs = held([P, SLOTS], U8, "hqs")
 
         def quantise(grouped, slots):
@@ -233,7 +213,7 @@ def tile_moe_dyl_none_kernel(
             )
 
         quantise(grouped_a, slice(0, 4 * P))
-        wbsq_b = keep.tile([P, width], U8, tag="hb_then_wbsq", align_bytes=64)
+        wbsq_b = keep.tile([P, width], U8, tag="hb1", align_bytes=64)
         nc.vector.tensor_copy(wbsq_b[:], wbs[:].indirect(wb_entries[1]))
         quantise(grouped_b, slice(4 * P, SLOTS))
         ysb = [held([P, SLOTS], F32, "ysb%d" % r) for r in range(ROWBLOCKS)]
@@ -260,6 +240,25 @@ def tile_moe_dyl_none_kernel(
                 nc.vector.tensor_tensor(win[r][:].indirect(entries), ysb[r][:, part], gate_sb[:, part], MULT)
             elif half == 1:
                 nc.vector.tensor_tensor(win[r][:].indirect(tok_list[:]), ysb[r][:], gate_sb[:], MULT)
+
+        slot_base = [held([P, 2, DIRECT * P], F32, "slot_base%d" % pair) for pair in range(HALF)]
+        for pair in range(HALF):
+            acc = bank(2 + pair % 2, [P, 2, DIRECT * P])
+            for j in range(2):
+                slots = slice(P * (2 * pair + j), P * (2 * pair + j + 1))
+                for d in range(DIRECT):
+                    r = SUMMED + d
+                    for a in range(PASSES):
+                        nc.tensor.matmul_mx(
+                            out=acc[:, j, P * d : P * (d + 1)],
+                            lhsT=xq[a][:, slots].bitcast(FP8X4),
+                            lhsT_scale=xsq[a][:, slots],
+                            rhs=ww[:, a, 2 * P * r : 2 * P * (r + 1)].bitcast(FP4X4),
+                            rhs_scale=ws[:, a, P * r : P * (r + 1)],
+                            start=(a == 0),
+                            stop=(a == PASSES - 1),
+                        )
+            nc.scalar.activation(slot_base[pair][:], acc[:], COPY)
 
         gated = [held([P, DIRECT * P], F32, "gated%d" % m) for m in range(B)]
         for pair in range(HALF):

@@ -74,12 +74,13 @@ def tile_moe_dyl_none_kernel(
         ident = held([P, P], F32, "ident")
         win = [held([P, T], F32, "win%d" % r) for r in range(ROWBLOCKS)]
 
+        nc.vector.memset(ident[:], 0.0)
+        make_identity(nc, ident[:], nomemset=True)
         nc.vector.memset(xs[32:64, :].bitcast(I32), 0)
         nc.vector.memset(xs[64:, :].bitcast(I32), 0)
         nc.vector.memset(was[:].bitcast(I32), 0)
         nc.gpsimd.memset(ws[:].rearrange("p a n -> p (a n)").bitcast(I32), 0)
         nc.gpsimd.memset(xs_planes[:].rearrange("p a n -> p (a n)").bitcast(I32), 0)
-        make_identity(nc, ident[:])
         nc.gpsimd.memset(wbs[:].bitcast(I32), 0)
 
         nc.sync.dma_start(tok_list[:], offs)

@@ -61,6 +61,12 @@ def tile_moe_dyl_none_kernel(
                     in_=scales[:, 4 * q : 4 * q + 4, :].rearrange("a r n -> r a n").bitcast(I32),
                 )
 
+        def gather(dst, window, entries):
+            nc.vector.tensor_copy(dst[:], window.indirect(entries))
+
+        def block_cols(j, first, count):
+            return slice(H * j + first, H * j + first + count)
+
         tok_list = held([P, SLOTS // 16], U16, "tok_list")
         wa_list = held([P, B * H // 16], U16, "wa_list")
         wb_list = held([P, B * N // 16], U16, "wb_list")
@@ -89,16 +95,16 @@ def tile_moe_dyl_none_kernel(
         load_words(xw[1][:], x_words[1])
         load_scale_rows(was, wa_scales)
         nc.sync.dma_start(wa_list[:], offs2)
-        nc.sync.dma_start(wb_list[:], offs3)
+        nc.sync.dma_start(out=ww[:].bitcast(I32), in_=w_words.rearrange("a p c -> p a c").bitcast(I32))
         load_planes(ws, w_scales)
         load_planes(xs_planes, x_scales)
-        nc.sync.dma_start(out=ww[:].bitcast(I32), in_=w_words.rearrange("a p c -> p a c").bitcast(I32))
         xs_rows = held([P, SLOTS], U8, "xs_rows")
         nc.vector.tensor_copy(xs_rows[:], xs[:, :T].indirect(tok_list[:]))
         waw = placed.tile([P, PASSES * E * H], I32, name="waw", offset=0, align_bytes=64)
         load_words(waw[:, : E * H], wa_words[0])
-        load_scale_rows(wbs, wb_scales)
         load_words(waw[:, E * H :], wa_words[1])
+        nc.sync.dma_start(wb_list[:], offs3)
+        load_scale_rows(wbs, wb_scales)
         xsq = [held([P, SLOTS], U8, "xsq%d" % a) for a in range(PASSES)]
         for a in range(PASSES):
             for q in range(4):
@@ -142,11 +148,10 @@ def tile_moe_dyl_none_kernel(
         wa_entries = [wa_list[:, half * width // 16 : (half + 1) * width // 16] for half in range(2)]
         wasq = [held([P, width], U8, "wasq%d" % half) for half in range(2)]
         for half in range(2):
-            nc.vector.tensor_copy(wasq[half][:], was[:].indirect(wa_entries[half]))
+            gather(wasq[half], was[:], wa_entries[half])
 
         wbsq_a = held([P, width], U8, "wbsq_a")
         wb_entries = [wb_list[:, half * width // 16 : (half + 1) * width // 16] for half in range(2)]
-        nc.vector.tensor_copy(wbsq_a[:], wbs[:].indirect(wb_entries[0]))
 
         for r in range(ROWBLOCKS):
             frozen(r, (2 * (r % 2), 2 * (r % 2) + 1))
@@ -159,13 +164,13 @@ def tile_moe_dyl_none_kernel(
             waq = [held([P, width], U32, "waq%d_%d" % (half, a)) for a in range(PASSES)]
             for a in range(PASSES):
                 window = waw[:, E * H * a : E * H * (PASSES if half else a + 1)]
-                nc.vector.tensor_copy(waq[a][:], window.bitcast(U32).indirect(wa_entries[half]))
+                gather(waq[a], window.bitcast(U32), wa_entries[half])
             hts = [bank(j, [P, H]) for j in range(HALF)]
             for a in range(PASSES):
                 for j in range(HALF):
                     m = half * HALF + j
                     slots = slice(P * m, P * (m + 1))
-                    cols = slice(H * j, H * (j + 1))
+                    cols = block_cols(j, 0, H)
                     nc.tensor.matmul_mx(
                         out=hts[j][:],
                         lhsT=xq[a][:, slots].bitcast(FP8X4),
@@ -201,8 +206,9 @@ def tile_moe_dyl_none_kernel(
 
         width = HALF * N
         wbq = [held([P, width], U32, "wbq%d" % half) for half in range(2)]
+        gather(wbsq_a, wbs[:], wb_entries[0])
         for half in range(2):
-            nc.vector.tensor_copy(wbq[half][:], wbw[:].bitcast(U32).indirect(wb_entries[half]))
+            gather(wbq[half], wbw[:].bitcast(U32), wb_entries[half])
         hq = held([P, SLOTS], U32, "hq")
         hqs = held([P, SLOTS], U8, "hqs")
 
@@ -215,7 +221,7 @@ def tile_moe_dyl_none_kernel(
 
         quantise(grouped_a, slice(0, 4 * P))
         wbsq_b = keep.tile([P, width], U8, tag="hb1", align_bytes=64)
-        nc.vector.tensor_copy(wbsq_b[:], wbs[:].indirect(wb_entries[1]))
+        gather(wbsq_b, wbs[:], wb_entries[1])
         quantise(grouped_b, slice(4 * P, SLOTS))
         ysb = [held([P, SLOTS], F32, "ysb%d" % r) for r in range(ROWBLOCKS)]
         for number, (r, half) in enumerate(((0, 0), (1, 0), (1, 1), (0, 1))):
@@ -224,7 +230,7 @@ def tile_moe_dyl_none_kernel(
             for j in range(HALF):
                 m = half * HALF + j
                 slots = slice(P * m, P * (m + 1))
-                cols = slice(N * j + P * r, N * j + P * (r + 1))
+                cols = block_cols(j, P * r, P)
                 nc.tensor.matmul_mx(
                     out=y[:, P * j : P * (j + 1)],
                     lhsT=wbq[half][:, cols].bitcast(FP8X4),
@@ -267,7 +273,7 @@ def tile_moe_dyl_none_kernel(
             for j in range(2):
                 m = 2 * pair + j
                 slots = slice(P * m, P * (m + 1))
-                cols = slice(N * (m % HALF) + P * SUMMED, N * (m % HALF + 1))
+                cols = block_cols(m % HALF, P * SUMMED, P * DIRECT)
                 nc.tensor.matmul_mx(
                     out=yt[:, j, :],
                     lhsT=hq[:, slots].bitcast(FP8X4),

@@ -160,41 +160,41 @@ def tile_moe_dyl_none_kernel(
 
         grouped_a = held([P, 4 * P, 4], BF16, "grouped_a")
         grouped_b = held([P, 2 * P, 4], BF16, "grouped_b")
-        for half in range(2):
-            waq = [held([P, width], U32, "waq%d_%d" % (half, a)) for a in range(PASSES)]
-            for a in range(PASSES):
-                window = waw[:, E * H * a : E * H * (PASSES if half else a + 1)]
-                gather(waq[a], window.bitcast(U32), wa_entries[half])
-            hts = [bank(j, [P, H]) for j in range(HALF)]
-            for a in range(PASSES):
+        waq = [[held([P, width], U32, "waq%d_%d" % (half, a)) for half in range(2)] for a in range(PASSES)]
+        hts = [bank(number, [P, H]) for number in (0, 1, 2, 3, 6, 7)]
+        for a in range(PASSES):
+            for half in range(2):
+                gather(waq[a][half], waw[:, E * H * a : E * H * (a + 1)].bitcast(U32), wa_entries[half])
                 for j in range(HALF):
                     m = half * HALF + j
                     slots = slice(P * m, P * (m + 1))
                     cols = block_cols(j, 0, H)
                     nc.tensor.matmul_mx(
-                        out=hts[j][:],
+                        out=hts[m][:],
                         lhsT=xq[a][:, slots].bitcast(FP8X4),
                         lhsT_scale=xsq[a][:, slots],
-                        rhs=waq[a][:, cols].bitcast(FP8X4),
+                        rhs=waq[a][half][:, cols].bitcast(FP8X4),
                         rhs_scale=wasq[half][4 * a :, cols],
                         start=(a == 0),
                         stop=(a == PASSES - 1),
                     )
-            for j in range(HALF):
-                m = half * HALF + j
-                ht = hts[j]
-                hb = keep.tile([P, H], BF16, tag="hb%d" % (m % 2), align_bytes=64)
+        for pair in range(HALF):
+            turned = bank(4 + pair % 2, [P, 2, 2, P])
+            for j in range(2):
+                m = 2 * pair + j
+                hb = keep.tile([P, H], BF16, tag="hb%d" % (0, 1, 2, 3, 3, 2)[m], align_bytes=64)
                 nc.scalar.copy(
                     out=hb[:].rearrange("s (u p e) -> s u p e", u=2, e=2),
-                    in_=ht[:].rearrange("s (p u e) -> s u p e", u=2, e=2),
+                    in_=hts[m][:].rearrange("s (p u e) -> s u p e", u=2, e=2),
                 )
-                turned = bank(4 + j, [P, 2, P])
                 for u in range(2):
-                    nc.tensor.transpose(turned[:, u, :], hb[:].bitcast(F32)[:, P * u : P * (u + 1)], ident[:])
-                nc.scalar.copy(
-                    out=(grouped_a, grouped_b)[m // 4][:, P * (m % 4) : P * (m % 4 + 1), :].bitcast(F32),
-                    in_=turned[:].rearrange("p u s -> p s u"),
-                )
+                    nc.tensor.transpose(turned[:, j, u, :], hb[:].bitcast(F32)[:, P * u : P * (u + 1)], ident[:])
+            nc.scalar.copy(
+                out=(grouped_a, grouped_b)[pair // 2][:, 2 * P * (pair % 2) : 2 * P * (pair % 2 + 1), :]
+                .bitcast(F32)
+                .rearrange("p (j s) u -> p j s u", j=2),
+                in_=turned[:].rearrange("p j u s -> p j s u"),
+            )
 
         gate_col = held([P, B], F32, "gate_col")
         for half in range(2):
@@ -220,7 +220,7 @@ def tile_moe_dyl_none_kernel(
             )
 
         quantise(grouped_a, slice(0, 4 * P))
-        wbsq_b = keep.tile([P, width], U8, tag="hb1", align_bytes=64)
+        wbsq_b = keep.tile([P, width], U8, tag="hb2", align_bytes=64)
         gather(wbsq_b, wbs[:], wb_entries[1])
         quantise(grouped_b, slice(4 * P, SLOTS))
         ysb = [held([P, SLOTS], F32, "ysb%d" % r) for r in range(ROWBLOCKS)]

@@ -15,6 +15,8 @@ U8 = mybir.dt.uint8
 FP8X4 = mybir.dt.float8_e4m3fn_x4
 FP4X4 = mybir.dt.float4_e2m1fn_x4
 MULT = mybir.AluOpType.mult
+ADD = mybir.AluOpType.add
+COPY = mybir.ActivationFunctionType.Copy
 
 P = 128
 PASSES = K // 512
@@ -24,8 +26,7 @@ HALF = B // 2
 ROWBLOCKS = N // P
 SUMMED = 2
 DIRECT = ROWBLOCKS - SUMMED
-WA_BYTES = 4 * PASSES * E * H
-COPY = mybir.ActivationFunctionType.Copy
+WIDE = 2 * SLOTS
 
 
 def tile_moe_dyl_none_kernel(
@@ -34,11 +35,13 @@ def tile_moe_dyl_none_kernel(
     nc = tc.nc
     with ExitStack() as ctx:
         keep = ctx.enter_context(tc.tile_pool(name="keep", bufs=1))
-        placed = ctx.enter_context(tc.tile_pool(name="placed", bufs=1))
         psum = ctx.enter_context(tc.psum_pool(name="psum", bufs=1))
 
         def held(shape, dtype, name):
             return keep.tile(shape, dtype, name=name, align_bytes=64)
+
+        def shared(shape, dtype, tag):
+            return keep.tile(shape, dtype, name=tag, tag=tag, align_bytes=64)
 
         def bank(number, shape):
             return psum.tile(shape, F32, name="bank%d" % number, offset=4 * BANK * number)
@@ -64,21 +67,31 @@ def tile_moe_dyl_none_kernel(
         def gather(dst, window, entries):
             nc.vector.tensor_copy(dst[:], window.indirect(entries))
 
-        def block_cols(j, first, count):
-            return slice(H * j + first, H * j + first + count)
+        def mx(acc, lhs, lhs_type, lhs_scale, rhs, rhs_scale, start, stop):
+            nc.tensor.matmul_mx(
+                out=acc,
+                lhsT=lhs.bitcast(lhs_type),
+                lhsT_scale=lhs_scale,
+                rhs=rhs.bitcast(FP8X4),
+                rhs_scale=rhs_scale,
+                start=start,
+                stop=stop,
+            )
 
         tok_list = held([P, SLOTS // 16], U16, "tok_list")
         wa_list = held([P, B * H // 16], U16, "wa_list")
         wb_list = held([P, B * N // 16], U16, "wb_list")
         xw = [held([P, T], I32, "xw%d" % a) for a in range(PASSES)]
-        xs = placed.tile([P, T + 4], U8, name="xs", offset=WA_BYTES - T // 2, align_bytes=64)
-        xs_planes = keep.tile([P, PASSES, T], U8, tag="planes_then_gate", align_bytes=64)
+        xs = held([P, T + 4], U8, "xs")
+        xs_planes = shared([P, PASSES, T], U8, "planes_then_gate")
         was = held([P, E * H + 4], U8, "was")
+        waw = [held([P, E * H], I32, "waw%d" % a) for a in range(PASSES)]
         wbs = held([P, E * N], U8, "wbs")
+        wbw = held([P, E * N], I32, "wbw")
         ww = held([P, PASSES, 2 * N], U8, "ww")
         ws = held([P, PASSES, N], U8, "ws")
         ident = held([P, P], F32, "ident")
-        win = [held([P, T], F32, "win%d" % r) for r in range(ROWBLOCKS)]
+        win = [held([P, T if r < SUMMED else WIDE], F32, "win%d" % r) for r in range(ROWBLOCKS)]
 
         nc.vector.memset(ident[:], 0.0)
         make_identity(nc, ident[:], nomemset=True)
@@ -91,20 +104,20 @@ def tile_moe_dyl_none_kernel(
 
         nc.sync.dma_start(tok_list[:], offs)
         nc.scalar.dma_start(out=xs[:32, :T].bitcast(I32), in_=x_scales.rearrange("a b t -> (a b) t").bitcast(I32))
-        load_words(xw[0][:], x_words[0])
-        load_words(xw[1][:], x_words[1])
+        for a in range(PASSES):
+            load_words(xw[a][:], x_words[a])
         load_scale_rows(was, wa_scales)
         nc.sync.dma_start(wa_list[:], offs2)
         nc.sync.dma_start(out=ww[:].bitcast(I32), in_=w_words.rearrange("a p c -> p a c").bitcast(I32))
         load_planes(ws, w_scales)
         load_planes(xs_planes, x_scales)
-        xs_rows = held([P, SLOTS], U8, "xs_rows")
-        nc.vector.tensor_copy(xs_rows[:], xs[:, :T].indirect(tok_list[:]))
-        waw = placed.tile([P, PASSES * E * H], I32, name="waw", offset=0, align_bytes=64)
-        load_words(waw[:, : E * H], wa_words[0])
-        load_words(waw[:, E * H :], wa_words[1])
+        for a in range(PASSES):
+            load_words(waw[a][:], wa_words[a])
         nc.sync.dma_start(wb_list[:], offs3)
         load_scale_rows(wbs, wb_scales)
+
+        xs_rows = held([P, SLOTS], U8, "xs_rows")
+        gather(xs_rows, xs[:, :T], tok_list[:])
         xsq = [held([P, SLOTS], U8, "xsq%d" % a) for a in range(PASSES)]
         for a in range(PASSES):
             for q in range(4):
@@ -112,7 +125,6 @@ def tile_moe_dyl_none_kernel(
                 nc.sync.dma_start(
                     out=xsq[a][32 * q : 32 * (q + 1), :].bitcast(I32), in_=xs_rows[first : first + 32, :].bitcast(I32)
                 )
-        wbw = placed.tile([P, E * N], I32, name="wbw", offset=WA_BYTES, align_bytes=64)
         load_words(wbw[:], wb_words[0])
 
         for r in range(SUMMED):
@@ -123,66 +135,65 @@ def tile_moe_dyl_none_kernel(
                 scale=0.0,
             )
 
-        base = [held([P, T], F32, "base%d" % r) for r in range(SUMMED)] + win[SUMMED:]
+        def frozen(acc, r, words, planes, cols):
+            for a in range(PASSES):
+                mx(
+                    acc,
+                    ww[:, a, 2 * P * r : 2 * P * (r + 1)],
+                    FP4X4,
+                    ws[:, a, P * r : P * (r + 1)],
+                    words[a][:, cols],
+                    planes[a][:, cols],
+                    a == 0,
+                    a == PASSES - 1,
+                )
 
-        def frozen(r, banks):
+        base = [held([P, T], F32, "base%d" % r) for r in range(SUMMED)] + win[SUMMED:]
+        for r in range(ROWBLOCKS):
             for c in range(T // BANK):
                 toks = slice(BANK * c, BANK * (c + 1))
-                acc = bank(banks[c], [P, BANK])
-                for a in range(PASSES):
-                    nc.tensor.matmul_mx(
-                        out=acc[:],
-                        lhsT=ww[:, a, 2 * P * r : 2 * P * (r + 1)].bitcast(FP4X4),
-                        lhsT_scale=ws[:, a, P * r : P * (r + 1)],
-                        rhs=xw[a][:, toks].bitcast(FP8X4),
-                        rhs_scale=xs_planes[:, a, toks],
-                        start=(a == 0),
-                        stop=(a == PASSES - 1),
-                    )
+                acc = bank(2 * (r % 2) + c, [P, BANK])
+                frozen(acc[:], r, xw, [xs_planes[:, a, :] for a in range(PASSES)], toks)
                 nc.scalar.copy(out=base[r][:, toks], in_=acc[:])
+        gate_sb = shared([P, SLOTS], F32, "planes_then_gate")
+        nc.sync.dma_start(out=gate_sb[:], in_=gate)
 
         xq = [held([P, SLOTS], U32, "xq%d" % a) for a in range(PASSES)]
         for a in range(PASSES):
-            nc.vector.tensor_copy(xq[a][:], xw[a][:].bitcast(U32).indirect(tok_list[:]))
+            gather(xq[a], xw[a][:].bitcast(U32), tok_list[:])
         width = HALF * H
         wa_entries = [wa_list[:, half * width // 16 : (half + 1) * width // 16] for half in range(2)]
+        wb_entries = [wb_list[:, half * width // 16 : (half + 1) * width // 16] for half in range(2)]
         wasq = [held([P, width], U8, "wasq%d" % half) for half in range(2)]
         for half in range(2):
             gather(wasq[half], was[:], wa_entries[half])
 
-        wbsq_a = held([P, width], U8, "wbsq_a")
-        wb_entries = [wb_list[:, half * width // 16 : (half + 1) * width // 16] for half in range(2)]
-
-        for r in range(ROWBLOCKS):
-            frozen(r, (2 * (r % 2), 2 * (r % 2) + 1))
-        gate_sb = keep.tile([P, SLOTS], F32, tag="planes_then_gate", align_bytes=64)
-        nc.sync.dma_start(out=gate_sb[:], in_=gate)
-
-        grouped_a = held([P, 4 * P, 4], BF16, "grouped_a")
-        grouped_b = held([P, 2 * P, 4], BF16, "grouped_b")
-        waq = [[held([P, width], U32, "waq%d_%d" % (half, a)) for half in range(2)] for a in range(PASSES)]
         hts = [bank(number, [P, H]) for number in (0, 1, 2, 3, 6, 7)]
         for a in range(PASSES):
             for half in range(2):
-                gather(waq[a][half], waw[:, E * H * a : E * H * (a + 1)].bitcast(U32), wa_entries[half])
+                waq = held([P, width], U32, "waq%d_%d" % (a, half))
+                gather(waq, waw[a][:].bitcast(U32), wa_entries[half])
                 for j in range(HALF):
                     m = half * HALF + j
                     slots = slice(P * m, P * (m + 1))
-                    cols = block_cols(j, 0, H)
-                    nc.tensor.matmul_mx(
-                        out=hts[m][:],
-                        lhsT=xq[a][:, slots].bitcast(FP8X4),
-                        lhsT_scale=xsq[a][:, slots],
-                        rhs=waq[a][half][:, cols].bitcast(FP8X4),
-                        rhs_scale=wasq[half][4 * a :, cols],
-                        start=(a == 0),
-                        stop=(a == PASSES - 1),
+                    cols = slice(H * j, H * (j + 1))
+                    mx(
+                        hts[m][:],
+                        xq[a][:, slots],
+                        FP8X4,
+                        xsq[a][:, slots],
+                        waq[:, cols],
+                        wasq[half][4 * a :, cols],
+                        a == 0,
+                        a == PASSES - 1,
                     )
+        grouped_a = held([P, 4 * P, 4], BF16, "grouped_a")
+        grouped_b = held([P, 2 * P, 4], BF16, "grouped_b")
         for pair in range(HALF):
             turned = bank(4 + pair % 2, [P, 2, 2, P])
             for j in range(2):
                 m = 2 * pair + j
-                hb = keep.tile([P, H], BF16, tag="hb%d" % (0, 1, 2, 3, 3, 2)[m], align_bytes=64)
+                hb = shared([P, H], BF16, "hb%d" % (0, 1, 2, 3, 3, 2)[m])
                 nc.scalar.copy(
                     out=hb[:].rearrange("s (u p e) -> s u p e", u=2, e=2),
                     in_=hts[m][:].rearrange("s (p u e) -> s u p e", u=2, e=2),
@@ -204,8 +215,8 @@ def tile_moe_dyl_none_kernel(
                 nc.tensor.transpose(turned_gate[:, j, :], gate_sb[:, P * m : P * (m + 1)], ident[:])
             nc.scalar.copy(out=gate_col[:, half * HALF : (half + 1) * HALF], in_=turned_gate[:, :, 0])
 
-        width = HALF * N
         wbq = [held([P, width], U32, "wbq%d" % half) for half in range(2)]
+        wbsq_a = held([P, width], U8, "wbsq_a")
         gather(wbsq_a, wbs[:], wb_entries[0])
         for half in range(2):
             gather(wbq[half], wbw[:].bitcast(U32), wb_entries[half])
@@ -220,25 +231,26 @@ def tile_moe_dyl_none_kernel(
             )
 
         quantise(grouped_a, slice(0, 4 * P))
-        wbsq_b = keep.tile([P, width], U8, tag="hb2", align_bytes=64)
+        wbsq_b = shared([P, width], U8, "hb2")
         gather(wbsq_b, wbs[:], wb_entries[1])
         quantise(grouped_b, slice(4 * P, SLOTS))
+        wbsq = (wbsq_a, wbsq_b)
+
         ysb = [held([P, SLOTS], F32, "ysb%d" % r) for r in range(ROWBLOCKS)]
         for number, (r, half) in enumerate(((0, 0), (1, 0), (1, 1), (0, 1))):
-            wbsq = (wbsq_a, wbsq_b)[half]
             y = bank(number, [P, HALF * P])
             for j in range(HALF):
-                m = half * HALF + j
-                slots = slice(P * m, P * (m + 1))
-                cols = block_cols(j, P * r, P)
-                nc.tensor.matmul_mx(
-                    out=y[:, P * j : P * (j + 1)],
-                    lhsT=wbq[half][:, cols].bitcast(FP8X4),
-                    lhsT_scale=wbsq[:, cols],
-                    rhs=hq[:, slots].bitcast(FP8X4),
-                    rhs_scale=hqs[:, slots],
-                    start=True,
-                    stop=True,
+                slots = slice(P * (half * HALF + j), P * (half * HALF + j + 1))
+                cols = slice(N * j + P * r, N * j + P * (r + 1))
+                mx(
+                    y[:, P * j : P * (j + 1)],
+                    wbq[half][:, cols],
+                    FP8X4,
+                    wbsq[half][:, cols],
+                    hq[:, slots],
+                    hqs[:, slots],
+                    True,
+                    True,
                 )
             part = slice(half * HALF * P, (half + 1) * HALF * P)
             nc.scalar.copy(out=ysb[r][:, part], in_=y[:])
@@ -248,66 +260,50 @@ def tile_moe_dyl_none_kernel(
             elif half == 1:
                 nc.vector.tensor_tensor(win[r][:].indirect(tok_list[:]), ysb[r][:], gate_sb[:], MULT)
 
-        slot_base = [held([P, 2, DIRECT * P], F32, "slot_base%d" % pair) for pair in range(HALF)]
-        for pair in range(HALF):
-            acc = bank(2 + pair % 2, [P, 2, DIRECT * P])
-            for j in range(2):
-                slots = slice(P * (2 * pair + j), P * (2 * pair + j + 1))
-                for d in range(DIRECT):
-                    r = SUMMED + d
-                    for a in range(PASSES):
-                        nc.tensor.matmul_mx(
-                            out=acc[:, j, P * d : P * (d + 1)],
-                            lhsT=xq[a][:, slots].bitcast(FP8X4),
-                            lhsT_scale=xsq[a][:, slots],
-                            rhs=ww[:, a, 2 * P * r : 2 * P * (r + 1)].bitcast(FP4X4),
-                            rhs_scale=ws[:, a, P * r : P * (r + 1)],
-                            start=(a == 0),
-                            stop=(a == PASSES - 1),
-                        )
-            nc.scalar.activation(slot_base[pair][:], acc[:], COPY)
-
         gated = [held([P, DIRECT * P], F32, "gated%d" % m) for m in range(B)]
         for pair in range(HALF):
             yt = bank(4 + pair, [P, 2, DIRECT * P])
             for j in range(2):
                 m = 2 * pair + j
                 slots = slice(P * m, P * (m + 1))
-                cols = block_cols(m % HALF, P * SUMMED, P * DIRECT)
-                nc.tensor.matmul_mx(
-                    out=yt[:, j, :],
-                    lhsT=hq[:, slots].bitcast(FP8X4),
-                    lhsT_scale=hqs[:, slots],
-                    rhs=wbq[m // HALF][:, cols].bitcast(FP8X4),
-                    rhs_scale=(wbsq_a, wbsq_b)[m // HALF][:, cols],
-                    start=True,
-                    stop=True,
+                cols = slice(N * (m % HALF) + P * SUMMED, N * (m % HALF + 1))
+                mx(
+                    yt[:, j, :],
+                    hq[:, slots],
+                    FP8X4,
+                    hqs[:, slots],
+                    wbq[m // HALF][:, cols],
+                    wbsq[m // HALF][:, cols],
+                    True,
+                    True,
                 )
             for j in range(2):
                 m = 2 * pair + j
                 nc.scalar.activation(gated[m][:], yt[:, j, :], COPY, scale=gate_col[:, m : m + 1])
+
+        slot_base = [held([P, SLOTS], F32, "slot_base%d" % d) for d in range(DIRECT)]
         for d in range(DIRECT):
-            cols = slice(P * d, P * (d + 1))
+            r = SUMMED + d
+            wide = bank(2, [P, BANK])
+            frozen(wide[:], r, xq, xsq, slice(0, BANK))
+            nc.scalar.copy(out=slot_base[d][:, :BANK], in_=wide[:])
+            rest = bank(3, [P, SLOTS - BANK])
+            for first in range(BANK, SLOTS, P):
+                frozen(rest[:, first - BANK : first - BANK + P], r, xq, xsq, slice(first, first + P))
+            nc.scalar.copy(out=slot_base[d][:, BANK:], in_=rest[:])
             for half in range(2):
-                total = bank(2 * d + half, [P, HALF * P])
-                for step in range(2):
-                    for j in range(HALF):
-                        m = half * HALF + j
-                        nc.tensor.matmul(
-                            total[:, P * j : P * (j + 1)],
-                            lhsT=(slot_base[m // 2][:, m % 2, cols], gated[m][:, cols])[step],
-                            rhs=ident[:],
-                            is_transpose=True,
-                            start=(step == 0 and j == 0),
-                            stop=(step == 1 and j == HALF - 1),
-                        )
-                nc.scalar.copy(out=ysb[SUMMED + d][:, half * HALF * P : (half + 1) * HALF * P], in_=total[:])
+                turned_y = bank(half, [P, HALF * P])
+                for j in range(HALF):
+                    nc.tensor.transpose(
+                        turned_y[:, P * j : P * (j + 1)], gated[half * HALF + j][:, P * d : P * (d + 1)], ident[:]
+                    )
+                nc.scalar.copy(out=ysb[r][:, half * HALF * P : (half + 1) * HALF * P], in_=turned_y[:])
 
         for r in (2, 3, 1, 0):
             rows = slice(P * r, P * (r + 1))
             if r >= SUMMED:
-                nc.vector.tensor_copy(win[r][:].indirect(tok_list[:]), ysb[r][:])
-                nc.sync.dma_start(out=out[rows, :], in_=win[r][:])
+                nc.vector.tensor_tensor(win[r][:].indirect(tok_list[:]), ysb[r][:], slot_base[r - SUMMED][:], ADD)
+                nc.sync.dma_start(out=out[rows, :], in_=win[r][:, :T])
                 continue
             sum_t = psum.tile([P, T], F32, name="sum_t", offset=4 * BANK * 2)
             for step, term in enumerate((base[r], win[r])):
@@ -323,7 +319,7 @@ def tile_moe_dyl_none_kernel(
             for c in range(T // BANK):
                 toks = slice(BANK * c, BANK * (c + 1))
                 result = held([P, BANK], F32, "result%d_%d" % (r, c))
-                sum_sb = keep.tile([P, BANK], F32, tag="sum_sb%d" % c, align_bytes=64)
+                sum_sb = shared([P, BANK], F32, "sum_sb%d" % c)
                 nc.scalar.copy(out=sum_sb[:], in_=sum_t[:, toks])
                 back = bank(4 + c, [P, BANK])
                 for j in range(BANK // P):

@@ -27,6 +27,7 @@ ROWBLOCKS = N // P
 SUMMED = 2
 DIRECT = ROWBLOCKS - SUMMED
 WIDE = 2 * SLOTS
+SHIFT = 32
 
 
 def tile_moe_dyl_none_kernel(
@@ -84,10 +85,12 @@ def tile_moe_dyl_none_kernel(
         xw = [held([P, T], I32, "xw%d" % a) for a in range(PASSES)]
         xs = held([P, T + 4], U8, "xs")
         xs_planes = shared([P, PASSES, T], U8, "planes_then_gate")
-        was = held([P, E * H + 4], U8, "was")
-        waw = [held([P, E * H], I32, "waw%d" % a) for a in range(PASSES)]
-        wbs = held([P, E * N], U8, "wbs")
-        wbw = held([P, E * N], I32, "wbw")
+        was_tile = held([P, SHIFT + E * H + 4], U8, "was")
+        was = was_tile[:, SHIFT : SHIFT + E * H]
+        waw = [held([P, SHIFT // 4 + E * H], I32, "waw%d" % a)[:, SHIFT // 4 :] for a in range(PASSES)]
+        wbs_tile = held([P, SHIFT + E * N], U8, "wbs")
+        wbs = wbs_tile[:, SHIFT:]
+        wbw = held([P, SHIFT // 4 + E * N], I32, "wbw")[:, SHIFT // 4 :]
         ww = held([P, PASSES, 2 * N], U8, "ww")
         ws = held([P, PASSES, N], U8, "ws")
         ident = held([P, P], F32, "ident")
@@ -97,10 +100,10 @@ def tile_moe_dyl_none_kernel(
         make_identity(nc, ident[:], nomemset=True)
         nc.vector.memset(xs[32:64, :].bitcast(I32), 0)
         nc.vector.memset(xs[64:, :].bitcast(I32), 0)
-        nc.vector.memset(was[:].bitcast(I32), 0)
+        nc.vector.memset(was_tile[:].bitcast(I32), 0)
         nc.gpsimd.memset(ws[:].rearrange("p a n -> p (a n)").bitcast(I32), 0)
         nc.gpsimd.memset(xs_planes[:].rearrange("p a n -> p (a n)").bitcast(I32), 0)
-        nc.gpsimd.memset(wbs[:].bitcast(I32), 0)
+        nc.gpsimd.memset(wbs_tile[:].bitcast(I32), 0)
 
         nc.sync.dma_start(tok_list[:], offs)
         nc.scalar.dma_start(out=xs[:32, :T].bitcast(I32), in_=x_scales.rearrange("a b t -> (a b) t").bitcast(I32))

@@ -96,14 +96,13 @@ def tile_moe_dyl_none_kernel(
         ident = held([P, P], F32, "ident")
         win = [held([P, T if r < SUMMED else WIDE], F32, "win%d" % r) for r in range(ROWBLOCKS)]
 
-        nc.vector.memset(ident[:], 0.0)
-        make_identity(nc, ident[:], nomemset=True)
-        nc.vector.memset(xs[32:64, :].bitcast(I32), 0)
-        nc.vector.memset(xs[64:, :].bitcast(I32), 0)
         nc.vector.memset(was_tile[:].bitcast(I32), 0)
         nc.gpsimd.memset(ws[:].rearrange("p a n -> p (a n)").bitcast(I32), 0)
         nc.gpsimd.memset(xs_planes[:].rearrange("p a n -> p (a n)").bitcast(I32), 0)
-        nc.gpsimd.memset(wbs_tile[:].bitcast(I32), 0)
+        nc.gpsimd.memset(xs[64:, :].bitcast(I32), 0)
+        nc.vector.memset(ident[:], 0.0)
+        make_identity(nc, ident[:], nomemset=True)
+        nc.vector.memset(xs[32:64, :].bitcast(I32), 0)
 
         nc.sync.dma_start(tok_list[:], offs)
         nc.scalar.dma_start(out=xs[:32, :T].bitcast(I32), in_=x_scales.rearrange("a b t -> (a b) t").bitcast(I32))
@@ -117,7 +116,11 @@ def tile_moe_dyl_none_kernel(
         for a in range(PASSES):
             load_words(waw[a][:], wa_words[a])
         nc.sync.dma_start(wb_list[:], offs3)
-        load_scale_rows(wbs, wb_scales)
+        for q in range(4):
+            nc.sync.dma_start(
+                out=wbs[32 * q : 32 * (q + 1), :].bitcast(I32),
+                in_=wb_scales[:, 4 * q : 4 * q + 4, :].bitcast(I32).to_broadcast([8, 4, E * N // 4]),
+            )
 
         xs_rows = held([P, SLOTS], U8, "xs_rows")
         gather(xs_rows, xs[:, :T], tok_list[:])

@@ -84,7 +84,7 @@ def tile_moe_dyl_none_kernel(
         wb_list = held([P, B * N // 16], U16, "wb_list")
         xw = [held([P, T], I32, "xw%d" % a) for a in range(PASSES)]
         xs = held([P, T + 4], U8, "xs")
-        xs_planes = shared([P, PASSES, T], U8, "planes_then_gate")
+        xs_planes = held([P, PASSES, T], U8, "xs_planes")
         was_tile = held([P, SHIFT + E * H + 4], U8, "was")
         was = was_tile[:, SHIFT : SHIFT + E * H]
         waw = [held([P, SHIFT // 4 + E * H], I32, "waw%d" % a)[:, SHIFT // 4 :] for a in range(PASSES)]
@@ -110,11 +110,11 @@ def tile_moe_dyl_none_kernel(
             load_words(xw[a][:], x_words[a])
         load_scale_rows(was, wa_scales)
         nc.sync.dma_start(wa_list[:], offs2)
+        load_words(waw[0][:], wa_words[0])
         nc.sync.dma_start(out=ww[:].bitcast(I32), in_=w_words.rearrange("a p c -> p a c").bitcast(I32))
         load_planes(ws, w_scales)
         load_planes(xs_planes, x_scales)
-        for a in range(PASSES):
-            load_words(waw[a][:], wa_words[a])
+        load_words(waw[1][:], wa_words[1])
         nc.sync.dma_start(wb_list[:], offs3)
         for q in range(4):
             nc.sync.dma_start(
@@ -132,6 +132,8 @@ def tile_moe_dyl_none_kernel(
                     out=xsq[a][32 * q : 32 * (q + 1), :].bitcast(I32), in_=xs_rows[first : first + 32, :].bitcast(I32)
                 )
         load_words(wbw[:], wb_words[0])
+        gate_sb = held([P, SLOTS], F32, "gate_sb")
+        nc.sync.dma_start(out=gate_sb[:], in_=gate)
 
         for r in range(SUMMED):
             nc.scalar.activation(
@@ -155,14 +157,16 @@ def tile_moe_dyl_none_kernel(
                 )
 
         base = [held([P, T], F32, "base%d" % r) for r in range(SUMMED)] + win[SUMMED:]
-        for r in range(ROWBLOCKS):
+
+        def frozen_rows(r, banks):
             for c in range(T // BANK):
                 toks = slice(BANK * c, BANK * (c + 1))
-                acc = bank(2 * (r % 2) + c, [P, BANK])
+                acc = bank(banks[c], [P, BANK])
                 frozen(acc[:], r, xw, [xs_planes[:, a, :] for a in range(PASSES)], toks)
                 nc.scalar.copy(out=base[r][:, toks], in_=acc[:])
-        gate_sb = shared([P, SLOTS], F32, "planes_then_gate")
-        nc.sync.dma_start(out=gate_sb[:], in_=gate)
+
+        frozen_rows(2, (0, 1))
+        frozen_rows(3, (2, 3))
 
         xq = [held([P, SLOTS], U32, "xq%d" % a) for a in range(PASSES)]
         for a in range(PASSES):
@@ -220,6 +224,8 @@ def tile_moe_dyl_none_kernel(
                 m = half * HALF + j
                 nc.tensor.transpose(turned_gate[:, j, :], gate_sb[:, P * m : P * (m + 1)], ident[:])
             nc.scalar.copy(out=gate_col[:, half * HALF : (half + 1) * HALF], in_=turned_gate[:, :, 0])
+
+        frozen_rows(1, (5, 4))
 
         wbq = [held([P, width], U32, "wbq%d" % half) for half in range(2)]
         wbsq_a = held([P, width], U8, "wbsq_a")
@@ -304,6 +310,8 @@ def tile_moe_dyl_none_kernel(
                         turned_y[:, P * j : P * (j + 1)], gated[half * HALF + j][:, P * d : P * (d + 1)], ident[:]
                     )
                 nc.scalar.copy(out=ysb[r][:, half * HALF * P : (half + 1) * HALF * P], in_=turned_y[:])
+
+        frozen_rows(0, (6, 7))
 
         for r in (2, 3, 1, 0):
             rows = slice(P * r, P * (r + 1))

@@ -58,8 +58,8 @@ def tile_moe_dyl_none_kernel(
                     in_=scales[:, 4 * q : 4 * q + 4, :].bitcast(I32),
                 )
 
-        def load_planes(planes, scales):
-            for q in range(4):
+        def load_planes(planes, scales, quadrants):
+            for q in quadrants:
                 nc.sync.dma_start(
                     out=planes[32 * q : 32 * q + 4, :, :].bitcast(I32),
                     in_=scales[:, 4 * q : 4 * q + 4, :].rearrange("a r n -> r a n").bitcast(I32),
@@ -110,10 +110,11 @@ def tile_moe_dyl_none_kernel(
             load_words(xw[a][:], x_words[a])
         load_scale_rows(was, wa_scales)
         nc.sync.dma_start(wa_list[:], offs2)
-        load_words(waw[0][:], wa_words[0])
         nc.sync.dma_start(out=ww[:].bitcast(I32), in_=w_words.rearrange("a p c -> p a c").bitcast(I32))
-        load_planes(ws, w_scales)
-        load_planes(xs_planes, x_scales)
+        load_planes(ws, w_scales, range(2))
+        load_words(waw[0][:], wa_words[0])
+        load_planes(ws, w_scales, range(2, 4))
+        load_planes(xs_planes, x_scales, range(4))
         load_words(waw[1][:], wa_words[1])
         nc.sync.dma_start(wb_list[:], offs3)
         for q in range(4):

@@ -110,29 +110,33 @@ def tile_moe_dyl_none_kernel(
             load_words(xw[a][:], x_words[a])
         load_scale_rows(was, wa_scales)
         nc.sync.dma_start(wa_list[:], offs2)
-        nc.sync.dma_start(out=ww[:].bitcast(I32), in_=w_words.rearrange("a p c -> p a c").bitcast(I32))
-        load_planes(ws, w_scales, range(2))
+        load_planes(ws, w_scales, range(3))
         load_words(waw[0][:], wa_words[0])
-        load_planes(ws, w_scales, range(2, 4))
+        nc.sync.dma_start(out=ww[:].bitcast(I32), in_=w_words.rearrange("a p c -> p a c").bitcast(I32))
+        load_planes(ws, w_scales, range(3, 4))
         load_planes(xs_planes, x_scales, range(4))
         load_words(waw[1][:], wa_words[1])
         nc.sync.dma_start(wb_list[:], offs3)
-        for q in range(4):
-            nc.sync.dma_start(
-                out=wbs[32 * q : 32 * (q + 1), :].bitcast(I32),
-                in_=wb_scales[:, 4 * q : 4 * q + 4, :].bitcast(I32).to_broadcast([8, 4, E * N // 4]),
-            )
 
         xs_rows = held([P, SLOTS], U8, "xs_rows")
         gather(xs_rows, xs[:, :T], tok_list[:])
         xsq = [held([P, SLOTS], U8, "xsq%d" % a) for a in range(PASSES)]
-        for a in range(PASSES):
+
+        def move_rows(a):
             for q in range(4):
                 first = 16 * a + 4 * q
                 nc.sync.dma_start(
                     out=xsq[a][32 * q : 32 * (q + 1), :].bitcast(I32), in_=xs_rows[first : first + 32, :].bitcast(I32)
                 )
+
+        move_rows(0)
         load_words(wbw[:], wb_words[0])
+        move_rows(1)
+        for q in range(4):
+            nc.sync.dma_start(
+                out=wbs[32 * q : 32 * (q + 1), :].bitcast(I32),
+                in_=wb_scales[:, 4 * q : 4 * q + 4, :].bitcast(I32).to_broadcast([8, 4, E * N // 4]),
+            )
         gate_sb = held([P, SLOTS], F32, "gate_sb")
         nc.sync.dma_start(out=gate_sb[:], in_=gate)
 
@@ -230,9 +234,9 @@ def tile_moe_dyl_none_kernel(
 
         wbq = [held([P, width], U32, "wbq%d" % half) for half in range(2)]
         wbsq_a = held([P, width], U8, "wbsq_a")
-        gather(wbsq_a, wbs[:], wb_entries[0])
         for half in range(2):
             gather(wbq[half], wbw[:].bitcast(U32), wb_entries[half])
+        gather(wbsq_a, wbs[:], wb_entries[0])
         hq = held([P, SLOTS], U32, "hq")
         hqs = held([P, SLOTS], U8, "hqs")
 

@@ -22,12 +22,9 @@ P = 128
 PASSES = K // 512
 SLOTS = P * B
 BANK = 512
-HALF = B // 2
-ROWBLOCKS = N // P
-SUMMED = 2
-DIRECT = ROWBLOCKS - SUMMED
-WIDE = 2 * SLOTS
-SHIFT = 32
+PAIR = 2 * P
+KIB = 1024
+LOWERED = 112
 
 
 def tile_moe_dyl_none_kernel(
@@ -36,6 +33,7 @@ def tile_moe_dyl_none_kernel(
     nc = tc.nc
     with ExitStack() as ctx:
         keep = ctx.enter_context(tc.tile_pool(name="keep", bufs=1))
+        reuse = ctx.enter_context(tc.tile_pool(name="reuse", bufs=1))
         psum = ctx.enter_context(tc.psum_pool(name="psum", bufs=1))
 
         def held(shape, dtype, name):
@@ -44,36 +42,38 @@ def tile_moe_dyl_none_kernel(
         def shared(shape, dtype, tag):
             return keep.tile(shape, dtype, name=tag, tag=tag, align_bytes=64)
 
+        def placed(shape, dtype, name, offset):
+            return reuse.tile(shape, dtype, name=name, offset=offset, align_bytes=64)
+
         def bank(number, shape):
             return psum.tile(shape, F32, name="bank%d" % number, offset=4 * BANK * number)
+
+        def clear(region):
+            nc.vector.memset(region.bitcast(I32), 0)
 
         def load_words(tile, words):
             nc.sync.dma_start(out=tile, in_=words.rearrange("p c d -> p (c d)").bitcast(I32))
 
-        def load_scale_rows(plane, scales):
+        def load_scale_rows(queue, plane, scales):
             rows = 4 * scales.shape[0]
             for q in range(4):
-                nc.sync.dma_start(
-                    out=plane[32 * q : 32 * q + rows, : scales.shape[2]].bitcast(I32),
+                queue.dma_start(
+                    out=plane[32 * q : 32 * q + rows, :].bitcast(I32),
                     in_=scales[:, 4 * q : 4 * q + 4, :].bitcast(I32),
                 )
 
-        def load_planes(planes, scales, quadrants):
-            for q in quadrants:
-                nc.sync.dma_start(
-                    out=planes[32 * q : 32 * q + 4, :, :].bitcast(I32),
-                    in_=scales[:, 4 * q : 4 * q + 4, :].rearrange("a r n -> r a n").bitcast(I32),
-                )
+        def lower(dst, src):
+            nc.scalar.dma_start(out=dst[:LOWERED, :].bitcast(I32), in_=src[4 : 4 + LOWERED, :].bitcast(I32))
 
         def gather(dst, window, entries):
             nc.vector.tensor_copy(dst[:], window.indirect(entries))
 
-        def mx(acc, lhs, lhs_type, lhs_scale, rhs, rhs_scale, start, stop):
+        def mx(acc, lhs, lhs_type, lhs_scale, rhs, rhs_type, rhs_scale, start, stop):
             nc.tensor.matmul_mx(
                 out=acc,
                 lhsT=lhs.bitcast(lhs_type),
                 lhsT_scale=lhs_scale,
-                rhs=rhs.bitcast(FP8X4),
+                rhs=rhs.bitcast(rhs_type),
                 rhs_scale=rhs_scale,
                 start=start,
                 stop=stop,
@@ -83,64 +83,86 @@ def tile_moe_dyl_none_kernel(
         wa_list = held([P, B * H // 16], U16, "wa_list")
         wb_list = held([P, B * N // 16], U16, "wb_list")
         xw = [held([P, T], I32, "xw%d" % a) for a in range(PASSES)]
-        xs = held([P, T + 4], U8, "xs")
-        xs_planes = held([P, PASSES, T], U8, "xs_planes")
-        was_tile = held([P, SHIFT + E * H + 4], U8, "was")
-        was = was_tile[:, SHIFT : SHIFT + E * H]
-        waw = [held([P, SHIFT // 4 + E * H], I32, "waw%d" % a)[:, SHIFT // 4 :] for a in range(PASSES)]
-        wbs_tile = held([P, SHIFT + E * N], U8, "wbs")
-        wbs = wbs_tile[:, SHIFT:]
-        wbw = held([P, SHIFT // 4 + E * N], I32, "wbw")[:, SHIFT // 4 :]
+        xs = held([P, T], U8, "xs")
+        xs_low = held([P, T], U8, "xs_low")
+        xsq = held([P, SLOTS], U8, "xsq")
+        xsq_low = held([P, SLOTS], U8, "xsq_low")
+        was = held([P, E * H], U8, "was")
+        waw = [held([P, E * H], I32, "waw%d" % a) for a in range(PASSES)]
+        wbs = held([P, E * N], U8, "wbs")
+        wbw = held([P, E * N], I32, "wbw")
         ww = held([P, PASSES, 2 * N], U8, "ww")
         ws = held([P, PASSES, N], U8, "ws")
         ident = held([P, P], F32, "ident")
-        win = [held([P, T if r < SUMMED else WIDE], F32, "win%d" % r) for r in range(ROWBLOCKS)]
+        gate_sb = held([P, SLOTS], F32, "gate_sb")
+        gate_col = held([P, B], F32, "gate_col")
+        gate_rows = placed([P, P], F32, "gate_rows", 28 * KIB - 256)
 
-        nc.vector.memset(was_tile[:].bitcast(I32), 0)
-        nc.gpsimd.memset(ws[:].rearrange("p a n -> p (a n)").bitcast(I32), 0)
-        nc.gpsimd.memset(xs_planes[:].rearrange("p a n -> p (a n)").bitcast(I32), 0)
-        nc.gpsimd.memset(xs[64:, :].bitcast(I32), 0)
-        nc.vector.memset(ident[:], 0.0)
+        clear(xs[:])
+        clear(was[:])
+        clear(ws[:].rearrange("p a n -> p (a n)"))
+        clear(xs_low[96:, :])
+        clear(wbs[:])
+        clear(xsq_low[96:, :])
+        nc.gpsimd.memset(ident[:], 0.0)
         make_identity(nc, ident[:], nomemset=True)
-        nc.vector.memset(xs[32:64, :].bitcast(I32), 0)
 
         nc.sync.dma_start(tok_list[:], offs)
-        nc.scalar.dma_start(out=xs[:32, :T].bitcast(I32), in_=x_scales.rearrange("a b t -> (a b) t").bitcast(I32))
-        for a in range(PASSES):
-            load_words(xw[a][:], x_words[a])
-        load_scale_rows(was, wa_scales)
+        load_words(xw[0][:], x_words[0])
+        load_words(xw[1][:], x_words[1])
         nc.sync.dma_start(wa_list[:], offs2)
-        load_planes(ws, w_scales, range(3))
-        load_words(waw[0][:], wa_words[0])
+        load_scale_rows(nc.scalar, xs, x_scales)
         nc.sync.dma_start(out=ww[:].bitcast(I32), in_=w_words.rearrange("a p c -> p a c").bitcast(I32))
-        load_planes(ws, w_scales, range(3, 4))
-        load_planes(xs_planes, x_scales, range(4))
+        load_words(waw[0][:], wa_words[0])
+        load_scale_rows(nc.scalar, was, wa_scales)
         load_words(waw[1][:], wa_words[1])
-        nc.sync.dma_start(wb_list[:], offs3)
-
-        xs_rows = held([P, SLOTS], U8, "xs_rows")
-        gather(xs_rows, xs[:, :T], tok_list[:])
-        xsq = [held([P, SLOTS], U8, "xsq%d" % a) for a in range(PASSES)]
-
-        def move_rows(a):
-            for q in range(4):
-                first = 16 * a + 4 * q
-                nc.sync.dma_start(
-                    out=xsq[a][32 * q : 32 * (q + 1), :].bitcast(I32), in_=xs_rows[first : first + 32, :].bitcast(I32)
-                )
-
-        move_rows(0)
-        load_words(wbw[:], wb_words[0])
-        move_rows(1)
         for q in range(4):
-            nc.sync.dma_start(
-                out=wbs[32 * q : 32 * (q + 1), :].bitcast(I32),
-                in_=wb_scales[:, 4 * q : 4 * q + 4, :].bitcast(I32).to_broadcast([8, 4, E * N // 4]),
+            nc.scalar.dma_start(
+                out=ws[32 * q : 32 * q + 4, :, :].bitcast(I32),
+                in_=w_scales[:, 4 * q : 4 * q + 4, :].rearrange("a r n -> r a n").bitcast(I32),
             )
-        gate_sb = held([P, SLOTS], F32, "gate_sb")
+        lower(xs_low, xs)
+        nc.sync.dma_start(wb_list[:], offs3)
+        load_scale_rows(nc.sync, wbs, wb_scales)
+        load_words(wbw[:], wb_words[0])
+        nc.scalar.dma_start(out=gate_rows[:], in_=gate.rearrange("p (m s) -> (p m) s", s=P)[:P, :])
         nc.sync.dma_start(out=gate_sb[:], in_=gate)
 
-        for r in range(SUMMED):
+        xq = [held([P, SLOTS], U32, "xq%d" % a) for a in range(PASSES)]
+        for a in range(PASSES):
+            gather(xq[a], xw[a][:].bitcast(U32), tok_list[:])
+        gather(xsq, xs[:], tok_list[:])
+        lower(xsq_low, xsq)
+
+        turned_gate = bank(6, [P, P])
+        nc.tensor.transpose(turned_gate[:], gate_rows[:], ident[:])
+        nc.scalar.copy(out=gate_col[:], in_=turned_gate[:, :B])
+
+        win = [placed([P, T], F32, "win%d" % r, (24 + 4 * r) * KIB) for r in range(2)]
+        win = win + [held([P, T], F32, "win%d" % r) for r in range(2, 4)]
+
+        def frozen(r, c, number):
+            acc = bank(number, [P, BANK])
+            toks = slice(BANK * c, BANK * (c + 1))
+            for a in range(PASSES):
+                mx(
+                    acc[:],
+                    ww[:, a, 2 * P * r : 2 * P * (r + 1)],
+                    FP4X4,
+                    ws[:, a, P * r : P * (r + 1)],
+                    xw[a][:, toks],
+                    FP8X4,
+                    (xs, xs_low)[a][:, toks],
+                    a == 0,
+                    a == PASSES - 1,
+                )
+            return acc
+
+        for r, banks in ((2, (2, 3)), (3, (0, 1))):
+            for c in range(2):
+                acc = frozen(r, c, banks[c])
+                nc.scalar.copy(out=win[r][:, BANK * c : BANK * (c + 1)], in_=acc[:])
+        for r in range(2):
             nc.scalar.activation(
                 win[r][:].rearrange("p (a b) -> p a b", b=P),
                 ident[:].unsqueeze(1).to_broadcast([P, T // P, P]),
@@ -148,200 +170,216 @@ def tile_moe_dyl_none_kernel(
                 scale=0.0,
             )
 
-        def frozen(acc, r, words, planes, cols):
+        def columns_of(entries, g):
+            return entries[:, g * 2 * H // 16 : (g + 1) * 2 * H // 16]
+
+        def tokens_of(g):
+            return tok_list[:, g * PAIR // 16 : (g + 1) * PAIR // 16]
+
+        def wa_scales_of(g):
+            wasq = shared([P, 2 * H], U8, "wasq")
+            gather(wasq, was[:], columns_of(wa_list, g))
+            return wasq
+
+        def first_product(g, wasq, waq):
+            hts = [bank(j, [P, H]) for j in range(2)]
             for a in range(PASSES):
-                mx(
-                    acc,
-                    ww[:, a, 2 * P * r : 2 * P * (r + 1)],
-                    FP4X4,
-                    ws[:, a, P * r : P * (r + 1)],
-                    words[a][:, cols],
-                    planes[a][:, cols],
-                    a == 0,
-                    a == PASSES - 1,
-                )
-
-        base = [held([P, T], F32, "base%d" % r) for r in range(SUMMED)] + win[SUMMED:]
-
-        def frozen_rows(r, banks):
-            for c in range(T // BANK):
-                toks = slice(BANK * c, BANK * (c + 1))
-                acc = bank(banks[c], [P, BANK])
-                frozen(acc[:], r, xw, [xs_planes[:, a, :] for a in range(PASSES)], toks)
-                nc.scalar.copy(out=base[r][:, toks], in_=acc[:])
-
-        frozen_rows(2, (0, 1))
-        frozen_rows(3, (2, 3))
-
-        xq = [held([P, SLOTS], U32, "xq%d" % a) for a in range(PASSES)]
-        for a in range(PASSES):
-            gather(xq[a], xw[a][:].bitcast(U32), tok_list[:])
-        width = HALF * H
-        wa_entries = [wa_list[:, half * width // 16 : (half + 1) * width // 16] for half in range(2)]
-        wb_entries = [wb_list[:, half * width // 16 : (half + 1) * width // 16] for half in range(2)]
-        wasq = [held([P, width], U8, "wasq%d" % half) for half in range(2)]
-        for half in range(2):
-            gather(wasq[half], was[:], wa_entries[half])
-
-        hts = [bank(number, [P, H]) for number in (0, 1, 2, 3, 6, 7)]
-        for a in range(PASSES):
-            for half in range(2):
-                waq = held([P, width], U32, "waq%d_%d" % (a, half))
-                gather(waq, waw[a][:].bitcast(U32), wa_entries[half])
-                for j in range(HALF):
-                    m = half * HALF + j
-                    slots = slice(P * m, P * (m + 1))
+                gather(waq[a], waw[a][:].bitcast(U32), columns_of(wa_list, g))
+                for j in range(2):
+                    slots = slice(PAIR * g + P * j, PAIR * g + P * (j + 1))
                     cols = slice(H * j, H * (j + 1))
                     mx(
-                        hts[m][:],
+                        hts[j][:],
                         xq[a][:, slots],
                         FP8X4,
-                        xsq[a][:, slots],
-                        waq[:, cols],
-                        wasq[half][4 * a :, cols],
+                        xsq[4 * a :, slots],
+                        waq[a][:, cols],
+                        FP8X4,
+                        wasq[4 * a :, cols],
                         a == 0,
                         a == PASSES - 1,
                     )
-        grouped_a = held([P, 4 * P, 4], BF16, "grouped_a")
-        grouped_b = held([P, 2 * P, 4], BF16, "grouped_b")
-        for pair in range(HALF):
-            turned = bank(4 + pair % 2, [P, 2, 2, P])
+            return hts
+
+        def turn_h(hts, hbs, grouped):
+            turned = bank(2, [P, 2, 2, P])
             for j in range(2):
-                m = 2 * pair + j
-                hb = shared([P, H], BF16, "hb%d" % (0, 1, 2, 3, 3, 2)[m])
                 nc.scalar.copy(
-                    out=hb[:].rearrange("s (u p e) -> s u p e", u=2, e=2),
-                    in_=hts[m][:].rearrange("s (p u e) -> s u p e", u=2, e=2),
+                    out=hbs[j][:].rearrange("s (u p e) -> s u p e", u=2, e=2),
+                    in_=hts[j][:].rearrange("s (p u e) -> s u p e", u=2, e=2),
                 )
                 for u in range(2):
-                    nc.tensor.transpose(turned[:, j, u, :], hb[:].bitcast(F32)[:, P * u : P * (u + 1)], ident[:])
+                    nc.tensor.transpose(turned[:, j, u, :], hbs[j][:].bitcast(F32)[:, P * u : P * (u + 1)], ident[:])
             nc.scalar.copy(
-                out=(grouped_a, grouped_b)[pair // 2][:, 2 * P * (pair % 2) : 2 * P * (pair % 2 + 1), :]
-                .bitcast(F32)
-                .rearrange("p (j s) u -> p j s u", j=2),
+                out=grouped[:].bitcast(F32).rearrange("p (j s) u -> p j s u", j=2),
                 in_=turned[:].rearrange("p j u s -> p j s u"),
             )
 
-        gate_col = held([P, B], F32, "gate_col")
-        for half in range(2):
-            turned_gate = bank((7, 3)[half], [P, HALF, P])
-            for j in range(HALF):
-                m = half * HALF + j
-                nc.tensor.transpose(turned_gate[:, j, :], gate_sb[:, P * m : P * (m + 1)], ident[:])
-            nc.scalar.copy(out=gate_col[:, half * HALF : (half + 1) * HALF], in_=turned_gate[:, :, 0])
+        def slot_base(g, number):
+            acc = bank(number, [P, 2, PAIR])
+            for j in range(2):
+                slots = slice(PAIR * g + P * j, PAIR * g + P * (j + 1))
+                for a in range(PASSES):
+                    mx(
+                        acc[:, j, :],
+                        xq[a][:, slots],
+                        FP8X4,
+                        (xsq, xsq_low)[a][:, slots],
+                        ww[:, a, 2 * PAIR :],
+                        FP4X4,
+                        ws[:, a, PAIR:],
+                        a == 0,
+                        a == PASSES - 1,
+                    )
+            sb = held([P, 2, PAIR], F32, "sb%d" % g)
+            nc.scalar.copy(out=sb[:], in_=acc[:])
+            return sb
 
-        frozen_rows(1, (5, 4))
+        def wb_of(g):
+            wbsq = shared([P, 2 * N], U8, "wbsq")
+            gather(wbsq, wbs[:], columns_of(wb_list, g))
+            wbq = shared([P, 2 * N], U32, "wbq")
+            gather(wbq, wbw[:].bitcast(U32), columns_of(wb_list, g))
+            return wbq, wbsq
 
-        wbq = [held([P, width], U32, "wbq%d" % half) for half in range(2)]
-        wbsq_a = held([P, width], U8, "wbsq_a")
-        for half in range(2):
-            gather(wbq[half], wbw[:].bitcast(U32), wb_entries[half])
-        gather(wbsq_a, wbs[:], wb_entries[0])
-        hq = held([P, SLOTS], U32, "hq")
-        hqs = held([P, SLOTS], U8, "hqs")
-
-        def quantise(grouped, slots):
+        def quantise(g, grouped, hq):
+            hqs = held([P, PAIR], U8, "hqs%d" % g)
             nc.vector.quantize_mx(
-                out=hq[:, slots].bitcast(FP8X4),
-                scales=hqs[:, slots],
-                in_=grouped[:].rearrange("p s t -> p (s t)"),
+                out=hq[:].bitcast(FP8X4), scales=hqs[:], in_=grouped[:].rearrange("p s t -> p (s t)")
+            )
+            return hq, hqs
+
+        def y_by_slot(acc, h, wb, j, first, count):
+            slots = slice(P * j, P * (j + 1))
+            cols = slice(N * j + first, N * j + first + count)
+            mx(acc, h[0][:, slots], FP8X4, h[1][:, slots], wb[0][:, cols], FP8X4, wb[1][:, cols], True, True)
+
+        def y_by_row(acc, h, wb, r):
+            for j in range(2):
+                slots = slice(P * j, P * (j + 1))
+                cols = slice(N * j + P * r, N * j + P * (r + 1))
+                mx(acc[:, slots], wb[0][:, cols], FP8X4, wb[1][:, cols], h[0][:, slots], FP8X4, h[1][:, slots], True, True)
+
+        def gate_slots(dst, acc, m):
+            nc.scalar.activation(dst, acc, COPY, scale=gate_col[:, m : m + 1])
+
+        def turn_sums(number, sb, gated):
+            acc = bank(number, [P, 2, PAIR])
+            for step in range(2):
+                for d in range(2):
+                    for j in range(2):
+                        term = (sb[:, j, :], gated[j])[step]
+                        nc.tensor.matmul(
+                            acc[:, d, P * j : P * (j + 1)],
+                            lhsT=term[:, P * d : P * (d + 1)],
+                            rhs=ident[:],
+                            is_transpose=True,
+                            start=(step, d, j) == (0, 0, 0),
+                            stop=(step, d, j) == (1, 1, 1),
+                        )
+            return acc
+
+        def scatter_values(r, g, values):
+            nc.scalar.activation(win[r][:].indirect(tokens_of(g)), values, COPY)
+
+        def scatter_gated(r, g, values):
+            nc.vector.tensor_tensor(
+                win[r][:].indirect(tokens_of(g)), values, gate_sb[:, PAIR * g : PAIR * (g + 1)], MULT
             )
 
-        quantise(grouped_a, slice(0, 4 * P))
-        wbsq_b = shared([P, width], U8, "hb2")
-        gather(wbsq_b, wbs[:], wb_entries[1])
-        quantise(grouped_b, slice(4 * P, SLOTS))
-        wbsq = (wbsq_a, wbsq_b)
-
-        ysb = [held([P, SLOTS], F32, "ysb%d" % r) for r in range(ROWBLOCKS)]
-        for number, (r, half) in enumerate(((0, 0), (1, 0), (1, 1), (0, 1))):
-            y = bank(number, [P, HALF * P])
-            for j in range(HALF):
-                slots = slice(P * (half * HALF + j), P * (half * HALF + j + 1))
-                cols = slice(N * j + P * r, N * j + P * (r + 1))
-                mx(
-                    y[:, P * j : P * (j + 1)],
-                    wbq[half][:, cols],
-                    FP8X4,
-                    wbsq[half][:, cols],
-                    hq[:, slots],
-                    hqs[:, slots],
-                    True,
-                    True,
-                )
-            part = slice(half * HALF * P, (half + 1) * HALF * P)
-            nc.scalar.copy(out=ysb[r][:, part], in_=y[:])
-            if r == 0:
-                entries = tok_list[:, part.start // 16 : part.stop // 16]
-                nc.vector.tensor_tensor(win[r][:].indirect(entries), ysb[r][:, part], gate_sb[:, part], MULT)
-            elif half == 1:
-                nc.vector.tensor_tensor(win[r][:].indirect(tok_list[:]), ysb[r][:], gate_sb[:], MULT)
-
-        gated = [held([P, DIRECT * P], F32, "gated%d" % m) for m in range(B)]
-        for pair in range(HALF):
-            yt = bank(4 + pair, [P, 2, DIRECT * P])
-            for j in range(2):
-                m = 2 * pair + j
-                slots = slice(P * m, P * (m + 1))
-                cols = slice(N * (m % HALF) + P * SUMMED, N * (m % HALF + 1))
-                mx(
-                    yt[:, j, :],
-                    hq[:, slots],
-                    FP8X4,
-                    hqs[:, slots],
-                    wbq[m // HALF][:, cols],
-                    wbsq[m // HALF][:, cols],
-                    True,
-                    True,
-                )
-            for j in range(2):
-                m = 2 * pair + j
-                nc.scalar.activation(gated[m][:], yt[:, j, :], COPY, scale=gate_col[:, m : m + 1])
-
-        slot_base = [held([P, SLOTS], F32, "slot_base%d" % d) for d in range(DIRECT)]
-        for d in range(DIRECT):
-            r = SUMMED + d
-            wide = bank(2, [P, BANK])
-            frozen(wide[:], r, xq, xsq, slice(0, BANK))
-            nc.scalar.copy(out=slot_base[d][:, :BANK], in_=wide[:])
-            rest = bank(3, [P, SLOTS - BANK])
-            for first in range(BANK, SLOTS, P):
-                frozen(rest[:, first - BANK : first - BANK + P], r, xq, xsq, slice(first, first + P))
-            nc.scalar.copy(out=slot_base[d][:, BANK:], in_=rest[:])
-            for half in range(2):
-                turned_y = bank(half, [P, HALF * P])
-                for j in range(HALF):
-                    nc.tensor.transpose(
-                        turned_y[:, P * j : P * (j + 1)], gated[half * HALF + j][:, P * d : P * (d + 1)], ident[:]
-                    )
-                nc.scalar.copy(out=ysb[r][:, half * HALF * P : (half + 1) * HALF * P], in_=turned_y[:])
-
-        frozen_rows(0, (6, 7))
-
-        for r in (2, 3, 1, 0):
-            rows = slice(P * r, P * (r + 1))
-            if r >= SUMMED:
-                nc.vector.tensor_tensor(win[r][:].indirect(tok_list[:]), ysb[r][:], slot_base[r - SUMMED][:], ADD)
-                nc.sync.dma_start(out=out[rows, :], in_=win[r][:, :T])
-                continue
-            sum_t = psum.tile([P, T], F32, name="sum_t", offset=4 * BANK * 2)
-            for step, term in enumerate((base[r], win[r])):
-                for j in range(T // P):
-                    nc.tensor.matmul(
-                        sum_t[:, P * j : P * (j + 1)],
-                        lhsT=term[:, P * j : P * (j + 1)],
-                        rhs=ident[:],
-                        is_transpose=True,
-                        start=(step == 0 and j % 4 == 0),
-                        stop=(step == 1 and j % 4 == 3),
-                    )
-            for c in range(T // BANK):
+        def add_and_store(r, banks):
+            for c in range(2):
                 toks = slice(BANK * c, BANK * (c + 1))
+                acc = frozen(r, c, banks[c])
                 result = held([P, BANK], F32, "result%d_%d" % (r, c))
-                sum_sb = shared([P, BANK], F32, "sum_sb%d" % c)
-                nc.scalar.copy(out=sum_sb[:], in_=sum_t[:, toks])
-                back = bank(4 + c, [P, BANK])
-                for j in range(BANK // P):
-                    nc.tensor.transpose(back[:, P * j : P * (j + 1)], sum_sb[:, P * j : P * (j + 1)], ident[:])
-                nc.scalar.copy(out=result[:], in_=back[:])
-                nc.scalar.dma_start(out=out[rows, toks], in_=result[:])
+                nc.vector.tensor_tensor(result[:], acc[:], win[r][:, toks], ADD)
+                nc.sync.dma_start(out=out[P * r : P * (r + 1), toks], in_=result[:])
+
+        wasq = wa_scales_of(0)
+        hts = first_product(0, wasq, [held([P, 2 * H], U32, "waq_a%d" % a) for a in range(PASSES)])
+        grouped_a = placed([P, PAIR, 4], BF16, "grouped_a", 4 * KIB - 512)
+        turn_h(hts, [held([P, H], BF16, "hb_a%d" % j) for j in range(2)], grouped_a)
+        wb = wb_of(0)
+        wasq = wa_scales_of(1)
+        h = quantise(0, grouped_a, held([P, PAIR], U32, "hq_a"))
+        sb_a = slot_base(0, 1)
+        sb_b = slot_base(1, 2)
+        gated_a = [held([P, 3 * P], F32, "gated_a%d" % j) for j in range(2)]
+        for j in range(2):
+            acc = bank(j, [P, 3 * P])
+            y_by_slot(acc[:, :P], h, wb, j, P, P)
+            y_by_slot(acc[:, P:], h, wb, j, PAIR, PAIR)
+            gate_slots(gated_a[j][:], acc[:], j)
+        y0_a = bank(7, [P, PAIR])
+        y_by_row(y0_a, h, wb, 0)
+        turned_1 = bank(6, [P, PAIR])
+        for j in range(2):
+            nc.tensor.transpose(turned_1[:, P * j : P * (j + 1)], gated_a[j][:, :P], ident[:])
+        v1_a = held([P, PAIR], F32, "v1_a")
+        nc.scalar.copy(out=v1_a[:], in_=turned_1[:])
+        sb_c = slot_base(2, 2)
+
+        hts = first_product(1, wasq, [placed([P, 2 * H], U32, "waq_b%d" % a, 5 * KIB * a) for a in range(PASSES)])
+        wb = wb_of(1)
+        grouped_b = placed([P, PAIR, 4], BF16, "grouped_b", 13 * KIB - 512)
+        turn_h(hts, [held([P, H], BF16, "hb_b0"), placed([P, H], BF16, "hb_b1", 18 * KIB)], grouped_b)
+        scatter_values(1, 0, v1_a[:])
+        wasq = wa_scales_of(2)
+        h = quantise(1, grouped_b, held([P, PAIR], U32, "hq_b"))
+        sums = turn_sums(4, sb_a, [gated_a[j][:, P:] for j in range(2)])
+        v23_a = placed([P, 2, PAIR], F32, "v23_a", 18 * KIB)
+        nc.scalar.copy(out=v23_a[:], in_=sums[:])
+        for d in range(2):
+            scatter_values(2 + d, 0, v23_a[:, d, :])
+        yt_b = bank(3, [P, 2, PAIR])
+        for j in range(2):
+            y_by_slot(yt_b[:, j, :], h, wb, j, PAIR, PAIR)
+        y01_b = bank(5, [P, 2, PAIR])
+        for r in range(2):
+            y_by_row(y01_b[:, r, :], h, wb, r)
+        ysb_a = placed([P, PAIR], F32, "ysb_a", 13 * KIB)
+        nc.scalar.copy(out=ysb_a[:], in_=y0_a[:])
+
+        hts = first_product(
+            2, wasq, [placed([P, 2 * H], U32, "waq_c%d" % a, (9 + 5 * a) * KIB) for a in range(PASSES)]
+        )
+        wb = wb_of(2)
+        gated_b = [placed([P, PAIR], F32, "gated_b%d" % j, (16 + j) * KIB) for j in range(2)]
+        for j in range(2):
+            gate_slots(gated_b[j][:], yt_b[:, j, :], 2 + j)
+        grouped_c = held([P, PAIR, 4], BF16, "grouped_c")
+        turn_h(hts, [held([P, H], BF16, "hb_c0"), placed([P, H], BF16, "hb_c1", 22 * KIB - 512)], grouped_c)
+        scatter_gated(0, 0, ysb_a[:])
+        h = quantise(2, grouped_c, placed([P, PAIR], U32, "hq_c", 23 * KIB))
+        sums = turn_sums(4, sb_b, [gated_b[j][:] for j in range(2)])
+        ysb_b = placed([P, 2, PAIR], F32, "ysb_b", 20 * KIB)
+        nc.scalar.copy(out=ysb_b[:], in_=y01_b[:])
+        v2_b = placed([P, PAIR], F32, "v2_b", 22 * KIB)
+        nc.scalar.copy(out=v2_b[:], in_=sums[:, 0, :])
+        scatter_values(2, 1, v2_b[:])
+        for r in range(2):
+            scatter_gated(r, 1, ysb_b[:, r, :])
+        y01_c = bank(5, [P, 2, PAIR])
+        for r in range(2):
+            y_by_row(y01_c[:, r, :], h, wb, r)
+        yt_c = bank(3, [P, 2, PAIR])
+        for j in range(2):
+            y_by_slot(yt_c[:, j, :], h, wb, j, PAIR, PAIR)
+        ysb_c = held([P, 2, PAIR], F32, "ysb_c")
+        nc.scalar.copy(out=ysb_c[:], in_=y01_c[:])
+        gated_c = [held([P, PAIR], F32, "gated_c%d" % j) for j in range(2)]
+        for j in range(2):
+            gate_slots(gated_c[j][:], yt_c[:, j, :], 4 + j)
+        v3_b = placed([P, PAIR], F32, "v3_b", 23 * KIB)
+        nc.scalar.copy(out=v3_b[:], in_=sums[:, 1, :])
+        scatter_values(3, 1, v3_b[:])
+        sums = turn_sums(2, sb_c, [gated_c[j][:] for j in range(2)])
+        v23_c = held([P, 2, PAIR], F32, "v23_c")
+        nc.scalar.copy(out=v23_c[:], in_=sums[:])
+        scatter_gated(1, 2, ysb_c[:, 1, :])
+        add_and_store(1, (0, 1))
+        scatter_gated(0, 2, ysb_c[:, 0, :])
+        add_and_store(0, (6, 7))
+        for d in range(2):
+            scatter_values(2 + d, 2, v23_c[:, d, :])
+            nc.scalar.dma_start(out=out[P * (2 + d) : P * (3 + d), :], in_=win[2 + d][:])

@@ -51,19 +51,19 @@ def tile_moe_dyl_none_kernel(
         def clear(region):
             nc.vector.memset(region.bitcast(I32), 0)
 
-        def load_words(tile, words):
-            nc.sync.dma_start(out=tile, in_=words.rearrange("p c d -> p (c d)").bitcast(I32))
+        def load_words(queue, tile, words):
+            queue.dma_start(out=tile, in_=words.rearrange("p c d -> p (c d)").bitcast(I32))
 
-        def load_scale_rows(queue, plane, scales):
+        def load_scale_rows(queues, plane, scales):
             rows = 4 * scales.shape[0]
             for q in range(4):
-                queue.dma_start(
+                queues[q].dma_start(
                     out=plane[32 * q : 32 * q + rows, :].bitcast(I32),
                     in_=scales[:, 4 * q : 4 * q + 4, :].bitcast(I32),
                 )
 
-        def lower(dst, src):
-            nc.scalar.dma_start(out=dst[:LOWERED, :].bitcast(I32), in_=src[4 : 4 + LOWERED, :].bitcast(I32))
+        def lower(queue, dst, src):
+            queue.dma_start(out=dst[:LOWERED, :].bitcast(I32), in_=src[4 : 4 + LOWERED, :].bitcast(I32))
 
         def gather(dst, window, entries):
             nc.vector.tensor_copy(dst[:], window.indirect(entries))
@@ -96,11 +96,11 @@ def tile_moe_dyl_none_kernel(
         ident = held([P, P], F32, "ident")
         gate_sb = held([P, SLOTS], F32, "gate_sb")
         gate_col = held([P, B], F32, "gate_col")
-        gate_rows = placed([P, P], F32, "gate_rows", 28 * KIB - 256)
+        gate_rows = held([P, P], F32, "gate_rows")
 
         clear(xs[:])
-        clear(was[:])
         clear(ws[:].rearrange("p a n -> p (a n)"))
+        clear(was[:])
         clear(xs_low[96:, :])
         clear(wbs[:])
         clear(xsq_low[96:, :])
@@ -108,38 +108,33 @@ def tile_moe_dyl_none_kernel(
         make_identity(nc, ident[:], nomemset=True)
 
         nc.sync.dma_start(tok_list[:], offs)
-        load_words(xw[0][:], x_words[0])
-        load_words(xw[1][:], x_words[1])
+        load_words(nc.scalar, xw[0][:], x_words[0])
         nc.sync.dma_start(wa_list[:], offs2)
-        load_scale_rows(nc.scalar, xs, x_scales)
+        load_words(nc.sync, xw[1][:], x_words[1])
+        load_scale_rows((nc.scalar, nc.scalar, nc.sync, nc.scalar), xs, x_scales)
+        load_scale_rows((nc.sync, nc.scalar, nc.sync, nc.scalar), was, wa_scales)
         nc.sync.dma_start(out=ww[:].bitcast(I32), in_=w_words.rearrange("a p c -> p a c").bitcast(I32))
-        load_words(waw[0][:], wa_words[0])
-        load_scale_rows(nc.scalar, was, wa_scales)
-        load_words(waw[1][:], wa_words[1])
+        lower(nc.scalar, xs_low, xs)
         for q in range(4):
-            nc.scalar.dma_start(
+            nc.gpsimd.dma_start(
                 out=ws[32 * q : 32 * q + 4, :, :].bitcast(I32),
                 in_=w_scales[:, 4 * q : 4 * q + 4, :].rearrange("a r n -> r a n").bitcast(I32),
             )
-        lower(xs_low, xs)
+        load_words(nc.sync, waw[0][:], wa_words[0])
+        load_words(nc.sync, waw[1][:], wa_words[1])
         nc.sync.dma_start(wb_list[:], offs3)
-        load_scale_rows(nc.sync, wbs, wb_scales)
-        load_words(wbw[:], wb_words[0])
-        nc.scalar.dma_start(out=gate_rows[:], in_=gate.rearrange("p (m s) -> (p m) s", s=P)[:P, :])
-        nc.sync.dma_start(out=gate_sb[:], in_=gate)
+        load_scale_rows([nc.sync] * 4, wbs, wb_scales)
+        load_words(nc.sync, wbw[:], wb_words[0])
+        nc.sync.dma_start(out=gate_rows[:], in_=gate.rearrange("p (m s) -> (p m) s", s=P)[:P, :])
 
         xq = [held([P, SLOTS], U32, "xq%d" % a) for a in range(PASSES)]
         for a in range(PASSES):
             gather(xq[a], xw[a][:].bitcast(U32), tok_list[:])
         gather(xsq, xs[:], tok_list[:])
-        lower(xsq_low, xsq)
+        lower(nc.sync, xsq_low, xsq)
+        nc.sync.dma_start(out=gate_sb[:], in_=gate)
 
-        turned_gate = bank(6, [P, P])
-        nc.tensor.transpose(turned_gate[:], gate_rows[:], ident[:])
-        nc.scalar.copy(out=gate_col[:], in_=turned_gate[:, :B])
-
-        win = [placed([P, T], F32, "win%d" % r, (24 + 4 * r) * KIB) for r in range(2)]
-        win = win + [held([P, T], F32, "win%d" % r) for r in range(2, 4)]
+        win = [held([P, T], F32, "win%d" % r) for r in range(4)]
 
         def frozen(r, c, number):
             acc = bank(number, [P, BANK])
@@ -158,7 +153,7 @@ def tile_moe_dyl_none_kernel(
                 )
             return acc
 
-        for r, banks in ((2, (2, 3)), (3, (0, 1))):
+        for r, banks in ((2, (0, 1)), (3, (3, 4))):
             for c in range(2):
                 acc = frozen(r, c, banks[c])
                 nc.scalar.copy(out=win[r][:, BANK * c : BANK * (c + 1)], in_=acc[:])
@@ -299,10 +294,13 @@ def tile_moe_dyl_none_kernel(
         hts = first_product(0, wasq, [held([P, 2 * H], U32, "waq_a%d" % a) for a in range(PASSES)])
         grouped_a = placed([P, PAIR, 4], BF16, "grouped_a", 4 * KIB - 512)
         turn_h(hts, [held([P, H], BF16, "hb_a%d" % j) for j in range(2)], grouped_a)
+        turned_gate = bank(2, [P, P])
+        nc.tensor.transpose(turned_gate[:], gate_rows[:], ident[:])
+        nc.scalar.copy(out=gate_col[:], in_=turned_gate[:, :B])
         wb = wb_of(0)
         wasq = wa_scales_of(1)
         h = quantise(0, grouped_a, held([P, PAIR], U32, "hq_a"))
-        sb_a = slot_base(0, 1)
+        sb_a = slot_base(0, 2)
         sb_b = slot_base(1, 2)
         gated_a = [held([P, 3 * P], F32, "gated_a%d" % j) for j in range(2)]
         for j in range(2):
@@ -317,13 +315,13 @@ def tile_moe_dyl_none_kernel(
             nc.tensor.transpose(turned_1[:, P * j : P * (j + 1)], gated_a[j][:, :P], ident[:])
         v1_a = held([P, PAIR], F32, "v1_a")
         nc.scalar.copy(out=v1_a[:], in_=turned_1[:])
-        sb_c = slot_base(2, 2)
 
         hts = first_product(1, wasq, [placed([P, 2 * H], U32, "waq_b%d" % a, 5 * KIB * a) for a in range(PASSES)])
         wb = wb_of(1)
         grouped_b = placed([P, PAIR, 4], BF16, "grouped_b", 13 * KIB - 512)
         turn_h(hts, [held([P, H], BF16, "hb_b0"), placed([P, H], BF16, "hb_b1", 18 * KIB)], grouped_b)
         scatter_values(1, 0, v1_a[:])
+        sb_c = slot_base(2, 2)
         wasq = wa_scales_of(2)
         h = quantise(1, grouped_b, held([P, PAIR], U32, "hq_b"))
         sums = turn_sums(4, sb_a, [gated_a[j][:, P:] for j in range(2)])
@@ -344,17 +342,17 @@ def tile_moe_dyl_none_kernel(
             2, wasq, [placed([P, 2 * H], U32, "waq_c%d" % a, (9 + 5 * a) * KIB) for a in range(PASSES)]
         )
         wb = wb_of(2)
+        grouped_c = held([P, PAIR, 4], BF16, "grouped_c")
+        turn_h(hts, [held([P, H], BF16, "hb_c%d" % j) for j in range(2)], grouped_c)
         gated_b = [placed([P, PAIR], F32, "gated_b%d" % j, (16 + j) * KIB) for j in range(2)]
         for j in range(2):
             gate_slots(gated_b[j][:], yt_b[:, j, :], 2 + j)
-        grouped_c = held([P, PAIR, 4], BF16, "grouped_c")
-        turn_h(hts, [held([P, H], BF16, "hb_c0"), placed([P, H], BF16, "hb_c1", 22 * KIB - 512)], grouped_c)
         scatter_gated(0, 0, ysb_a[:])
         h = quantise(2, grouped_c, placed([P, PAIR], U32, "hq_c", 23 * KIB))
         sums = turn_sums(4, sb_b, [gated_b[j][:] for j in range(2)])
-        ysb_b = placed([P, 2, PAIR], F32, "ysb_b", 20 * KIB)
+        ysb_b = placed([P, 2, PAIR], F32, "ysb_b", 16 * KIB)
         nc.scalar.copy(out=ysb_b[:], in_=y01_b[:])
-        v2_b = placed([P, PAIR], F32, "v2_b", 22 * KIB)
+        v2_b = held([P, PAIR], F32, "v2_b")
         nc.scalar.copy(out=v2_b[:], in_=sums[:, 0, :])
         scatter_values(2, 1, v2_b[:])
         for r in range(2):

@@ -86,7 +86,6 @@ def tile_moe_dyl_none_kernel(
         xs = held([P, T], U8, "xs")
         xs_low = held([P, T], U8, "xs_low")
         xsq = held([P, SLOTS], U8, "xsq")
-        xsq_low = held([P, SLOTS], U8, "xsq_low")
         was = held([P, E * H], U8, "was")
         waw = [held([P, E * H], I32, "waw%d" % a) for a in range(PASSES)]
         wbs = held([P, E * N], U8, "wbs")
@@ -95,75 +94,55 @@ def tile_moe_dyl_none_kernel(
         ws = held([P, PASSES, N], U8, "ws")
         ident = held([P, P], F32, "ident")
         gate_sb = held([P, SLOTS], F32, "gate_sb")
-        gate_col = held([P, B], F32, "gate_col")
-        gate_rows = held([P, P], F32, "gate_rows")
+        zeros = held([P, P], F32, "zeros")
+        win = [held([P, T], F32, "win%d" % r) for r in range(4)]
 
+        def clear_window(r, first, last):
+            nc.scalar.activation(
+                win[r][:, P * first : P * last].rearrange("p (a b) -> p a b", b=P),
+                zeros[:].unsqueeze(1).to_broadcast([P, last - first, P]),
+                COPY,
+            )
+
+        nc.vector.memset(zeros[:], 0.0)
+        clear_window(0, 0, 1)
         clear(xs[:])
-        clear(ws[:].rearrange("p a n -> p (a n)"))
         clear(was[:])
-        clear(xs_low[96:, :])
         clear(wbs[:])
-        clear(xsq_low[96:, :])
+        nc.vector.memset(win[3][:], 0.0)
+        clear(ws[:].rearrange("p a n -> p (a n)"))
+        clear(xs_low[96:, :])
         nc.gpsimd.memset(ident[:], 0.0)
         make_identity(nc, ident[:], nomemset=True)
 
         nc.sync.dma_start(tok_list[:], offs)
-        load_words(nc.scalar, xw[0][:], x_words[0])
-        nc.sync.dma_start(wa_list[:], offs2)
+        load_words(nc.sync, xw[0][:], x_words[0])
         load_words(nc.sync, xw[1][:], x_words[1])
-        load_scale_rows((nc.scalar, nc.scalar, nc.sync, nc.scalar), xs, x_scales)
-        load_scale_rows((nc.sync, nc.scalar, nc.sync, nc.scalar), was, wa_scales)
+        nc.sync.dma_start(wa_list[:], offs2)
+        load_scale_rows([nc.scalar] * 4, xs, x_scales)
+        load_words(nc.sync, waw[0][:], wa_words[0])
+        load_words(nc.sync, waw[1][:], wa_words[1])
+        load_scale_rows([nc.scalar] * 4, was, wa_scales)
+        nc.sync.dma_start(wb_list[:], offs3)
+        load_words(nc.sync, wbw[:], wb_words[0])
+        load_scale_rows([nc.scalar] * 4, wbs, wb_scales)
+        nc.sync.dma_start(out=gate_sb[:], in_=gate)
         nc.sync.dma_start(out=ww[:].bitcast(I32), in_=w_words.rearrange("a p c -> p a c").bitcast(I32))
-        lower(nc.scalar, xs_low, xs)
         for q in range(4):
-            nc.gpsimd.dma_start(
+            nc.sync.dma_start(
                 out=ws[32 * q : 32 * q + 4, :, :].bitcast(I32),
                 in_=w_scales[:, 4 * q : 4 * q + 4, :].rearrange("a r n -> r a n").bitcast(I32),
             )
-        load_words(nc.sync, waw[0][:], wa_words[0])
-        load_words(nc.sync, waw[1][:], wa_words[1])
-        nc.sync.dma_start(wb_list[:], offs3)
-        load_scale_rows([nc.sync] * 4, wbs, wb_scales)
-        load_words(nc.sync, wbw[:], wb_words[0])
-        nc.sync.dma_start(out=gate_rows[:], in_=gate.rearrange("p (m s) -> (p m) s", s=P)[:P, :])
+        lower(nc.sync, xs_low, xs)
 
         xq = [held([P, SLOTS], U32, "xq%d" % a) for a in range(PASSES)]
         for a in range(PASSES):
             gather(xq[a], xw[a][:].bitcast(U32), tok_list[:])
         gather(xsq, xs[:], tok_list[:])
-        lower(nc.sync, xsq_low, xsq)
-        nc.sync.dma_start(out=gate_sb[:], in_=gate)
 
-        win = [held([P, T], F32, "win%d" % r) for r in range(4)]
-
-        def frozen(r, c, number):
-            acc = bank(number, [P, BANK])
-            toks = slice(BANK * c, BANK * (c + 1))
-            for a in range(PASSES):
-                mx(
-                    acc[:],
-                    ww[:, a, 2 * P * r : 2 * P * (r + 1)],
-                    FP4X4,
-                    ws[:, a, P * r : P * (r + 1)],
-                    xw[a][:, toks],
-                    FP8X4,
-                    (xs, xs_low)[a][:, toks],
-                    a == 0,
-                    a == PASSES - 1,
-                )
-            return acc
-
-        for r, banks in ((2, (0, 1)), (3, (3, 4))):
-            for c in range(2):
-                acc = frozen(r, c, banks[c])
-                nc.scalar.copy(out=win[r][:, BANK * c : BANK * (c + 1)], in_=acc[:])
-        for r in range(2):
-            nc.scalar.activation(
-                win[r][:].rearrange("p (a b) -> p a b", b=P),
-                ident[:].unsqueeze(1).to_broadcast([P, T // P, P]),
-                COPY,
-                scale=0.0,
-            )
+        clear_window(0, 1, T // P)
+        for r in (1, 2):
+            clear_window(r, 0, T // P)
 
         def columns_of(entries, g):
             return entries[:, g * 2 * H // 16 : (g + 1) * 2 * H // 16]
@@ -176,28 +155,25 @@ def tile_moe_dyl_none_kernel(
             gather(wasq, was[:], columns_of(wa_list, g))
             return wasq
 
-        def first_product(g, wasq, waq):
-            hts = [bank(j, [P, H]) for j in range(2)]
-            for a in range(PASSES):
-                gather(waq[a], waw[a][:].bitcast(U32), columns_of(wa_list, g))
-                for j in range(2):
-                    slots = slice(PAIR * g + P * j, PAIR * g + P * (j + 1))
-                    cols = slice(H * j, H * (j + 1))
-                    mx(
-                        hts[j][:],
-                        xq[a][:, slots],
-                        FP8X4,
-                        xsq[4 * a :, slots],
-                        waq[a][:, cols],
-                        FP8X4,
-                        wasq[4 * a :, cols],
-                        a == 0,
-                        a == PASSES - 1,
-                    )
-            return hts
+        def first_pass(g, a, hts, wasq, waq):
+            gather(waq, waw[a][:].bitcast(U32), columns_of(wa_list, g))
+            for j in range(2):
+                slots = slice(PAIR * g + P * j, PAIR * g + P * (j + 1))
+                cols = slice(H * j, H * (j + 1))
+                mx(
+                    hts[j][:],
+                    xq[a][:, slots],
+                    FP8X4,
+                    xsq[4 * a :, slots],
+                    waq[:, cols],
+                    FP8X4,
+                    wasq[4 * a :, cols],
+                    a == 0,
+                    a == PASSES - 1,
+                )
 
-        def turn_h(hts, hbs, grouped):
-            turned = bank(2, [P, 2, 2, P])
+        def turn_h(hts, hbs, number, grouped):
+            turned = bank(number, [P, 2, 2, P])
             for j in range(2):
                 nc.scalar.copy(
                     out=hbs[j][:].rearrange("s (u p e) -> s u p e", u=2, e=2),
@@ -209,26 +185,6 @@ def tile_moe_dyl_none_kernel(
                 out=grouped[:].bitcast(F32).rearrange("p (j s) u -> p j s u", j=2),
                 in_=turned[:].rearrange("p j u s -> p j s u"),
             )
-
-        def slot_base(g, number):
-            acc = bank(number, [P, 2, PAIR])
-            for j in range(2):
-                slots = slice(PAIR * g + P * j, PAIR * g + P * (j + 1))
-                for a in range(PASSES):
-                    mx(
-                        acc[:, j, :],
-                        xq[a][:, slots],
-                        FP8X4,
-                        (xsq, xsq_low)[a][:, slots],
-                        ww[:, a, 2 * PAIR :],
-                        FP4X4,
-                        ws[:, a, PAIR:],
-                        a == 0,
-                        a == PASSES - 1,
-                    )
-            sb = held([P, 2, PAIR], F32, "sb%d" % g)
-            nc.scalar.copy(out=sb[:], in_=acc[:])
-            return sb
 
         def wb_of(g):
             wbsq = shared([P, 2 * N], U8, "wbsq")
@@ -244,140 +200,107 @@ def tile_moe_dyl_none_kernel(
             )
             return hq, hqs
 
-        def y_by_slot(acc, h, wb, j, first, count):
-            slots = slice(P * j, P * (j + 1))
-            cols = slice(N * j + first, N * j + first + count)
-            mx(acc, h[0][:, slots], FP8X4, h[1][:, slots], wb[0][:, cols], FP8X4, wb[1][:, cols], True, True)
+        def second_product(banks, h, wb):
+            ys = [bank(number, [P, 2, PAIR]) for number in banks]
+            for r in range(4):
+                for j in range(2):
+                    slots = slice(P * j, P * (j + 1))
+                    cols = slice(N * j + P * r, N * j + P * (r + 1))
+                    mx(
+                        ys[r // 2][:, r % 2, slots],
+                        wb[0][:, cols],
+                        FP8X4,
+                        wb[1][:, cols],
+                        h[0][:, slots],
+                        FP8X4,
+                        h[1][:, slots],
+                        True,
+                        True,
+                    )
+            return ys
 
-        def y_by_row(acc, h, wb, r):
-            for j in range(2):
-                slots = slice(P * j, P * (j + 1))
-                cols = slice(N * j + P * r, N * j + P * (r + 1))
-                mx(acc[:, slots], wb[0][:, cols], FP8X4, wb[1][:, cols], h[0][:, slots], FP8X4, h[1][:, slots], True, True)
+        def gated(g, dst, y):
+            weights = gate_sb[:, PAIR * g : PAIR * (g + 1)]
+            nc.vector.tensor_tensor(dst, y, weights.unsqueeze(1).to_broadcast([P, y.shape[1], PAIR]), MULT)
 
-        def gate_slots(dst, acc, m):
-            nc.scalar.activation(dst, acc, COPY, scale=gate_col[:, m : m + 1])
-
-        def turn_sums(number, sb, gated):
-            acc = bank(number, [P, 2, PAIR])
-            for step in range(2):
-                for d in range(2):
-                    for j in range(2):
-                        term = (sb[:, j, :], gated[j])[step]
-                        nc.tensor.matmul(
-                            acc[:, d, P * j : P * (j + 1)],
-                            lhsT=term[:, P * d : P * (d + 1)],
-                            rhs=ident[:],
-                            is_transpose=True,
-                            start=(step, d, j) == (0, 0, 0),
-                            stop=(step, d, j) == (1, 1, 1),
-                        )
-            return acc
-
-        def scatter_values(r, g, values):
+        def scatter_on_scalar(r, g, values):
             nc.scalar.activation(win[r][:].indirect(tokens_of(g)), values, COPY)
 
-        def scatter_gated(r, g, values):
-            nc.vector.tensor_tensor(
-                win[r][:].indirect(tokens_of(g)), values, gate_sb[:, PAIR * g : PAIR * (g + 1)], MULT
-            )
+        def scatter_on_vector(r, g, values):
+            nc.vector.tensor_copy(win[r][:].indirect(tokens_of(g)), values)
 
         def add_and_store(r, banks):
             for c in range(2):
                 toks = slice(BANK * c, BANK * (c + 1))
-                acc = frozen(r, c, banks[c])
+                acc = bank(banks[c], [P, BANK])
+                for a in range(PASSES):
+                    mx(
+                        acc[:],
+                        ww[:, a, 2 * P * r : 2 * P * (r + 1)],
+                        FP4X4,
+                        ws[:, a, P * r : P * (r + 1)],
+                        xw[a][:, toks],
+                        FP8X4,
+                        (xs, xs_low)[a][:, toks],
+                        a == 0,
+                        a == PASSES - 1,
+                    )
                 result = held([P, BANK], F32, "result%d_%d" % (r, c))
                 nc.vector.tensor_tensor(result[:], acc[:], win[r][:, toks], ADD)
                 nc.sync.dma_start(out=out[P * r : P * (r + 1), toks], in_=result[:])
 
         wasq = wa_scales_of(0)
-        hts = first_product(0, wasq, [held([P, 2 * H], U32, "waq_a%d" % a) for a in range(PASSES)])
-        grouped_a = placed([P, PAIR, 4], BF16, "grouped_a", 4 * KIB - 512)
-        turn_h(hts, [held([P, H], BF16, "hb_a%d" % j) for j in range(2)], grouped_a)
-        turned_gate = bank(2, [P, P])
-        nc.tensor.transpose(turned_gate[:], gate_rows[:], ident[:])
-        nc.scalar.copy(out=gate_col[:], in_=turned_gate[:, :B])
+        hts = [bank(j, [P, H]) for j in range(2)]
+        for a in range(PASSES):
+            first_pass(0, a, hts, wasq, held([P, 2 * H], U32, "waq_a%d" % a))
+        grouped = placed([P, PAIR, 4], BF16, "grouped_a", 0)
+        turn_h(hts, [held([P, H], BF16, "hb_a%d" % j) for j in range(2)], 2, grouped)
         wb = wb_of(0)
         wasq = wa_scales_of(1)
-        h = quantise(0, grouped_a, held([P, PAIR], U32, "hq_a"))
-        sb_a = slot_base(0, 2)
-        sb_b = slot_base(1, 2)
-        gated_a = [held([P, 3 * P], F32, "gated_a%d" % j) for j in range(2)]
-        for j in range(2):
-            acc = bank(j, [P, 3 * P])
-            y_by_slot(acc[:, :P], h, wb, j, P, P)
-            y_by_slot(acc[:, P:], h, wb, j, PAIR, PAIR)
-            gate_slots(gated_a[j][:], acc[:], j)
-        y0_a = bank(7, [P, PAIR])
-        y_by_row(y0_a, h, wb, 0)
-        turned_1 = bank(6, [P, PAIR])
-        for j in range(2):
-            nc.tensor.transpose(turned_1[:, P * j : P * (j + 1)], gated_a[j][:, :P], ident[:])
-        v1_a = held([P, PAIR], F32, "v1_a")
-        nc.scalar.copy(out=v1_a[:], in_=turned_1[:])
+        h = quantise(0, grouped, placed([P, PAIR], U32, "hq_a", 4 * KIB))
+        y_a = second_product((7, 4), h, wb)
 
-        hts = first_product(1, wasq, [placed([P, 2 * H], U32, "waq_b%d" % a, 5 * KIB * a) for a in range(PASSES)])
+        hts = [bank(j, [P, H]) for j in range(2)]
+        first_pass(1, 0, hts, wasq, placed([P, 2 * H], U32, "waq_b0", 0))
+        v01_a = held([P, 2, PAIR], F32, "v01_a")
+        gated(0, v01_a[:], y_a[0][:])
+        first_pass(1, 1, hts, wasq, placed([P, 2 * H], U32, "waq_b1", 4 * KIB))
         wb = wb_of(1)
-        grouped_b = placed([P, PAIR, 4], BF16, "grouped_b", 13 * KIB - 512)
-        turn_h(hts, [held([P, H], BF16, "hb_b0"), placed([P, H], BF16, "hb_b1", 18 * KIB)], grouped_b)
-        scatter_values(1, 0, v1_a[:])
-        sb_c = slot_base(2, 2)
         wasq = wa_scales_of(2)
-        h = quantise(1, grouped_b, held([P, PAIR], U32, "hq_b"))
-        sums = turn_sums(4, sb_a, [gated_a[j][:, P:] for j in range(2)])
-        v23_a = placed([P, 2, PAIR], F32, "v23_a", 18 * KIB)
-        nc.scalar.copy(out=v23_a[:], in_=sums[:])
-        for d in range(2):
-            scatter_values(2 + d, 0, v23_a[:, d, :])
-        yt_b = bank(3, [P, 2, PAIR])
-        for j in range(2):
-            y_by_slot(yt_b[:, j, :], h, wb, j, PAIR, PAIR)
-        y01_b = bank(5, [P, 2, PAIR])
+        grouped = placed([P, PAIR, 4], BF16, "grouped_b", 8 * KIB)
+        turn_h(hts, [held([P, H], BF16, "hb_b0"), placed([P, H], BF16, "hb_b1", 16 * KIB)], 3, grouped)
         for r in range(2):
-            y_by_row(y01_b[:, r, :], h, wb, r)
-        ysb_a = placed([P, PAIR], F32, "ysb_a", 13 * KIB)
-        nc.scalar.copy(out=ysb_a[:], in_=y0_a[:])
+            scatter_on_scalar(r, 0, v01_a[:, r, :])
+        v23_a = placed([P, 2, PAIR], F32, "v23_a", 16 * KIB)
+        gated(0, v23_a[:], y_a[1][:])
+        h = quantise(1, grouped, placed([P, PAIR], U32, "hq_b", 12 * KIB))
+        for r in range(2):
+            scatter_on_scalar(2 + r, 0, v23_a[:, r, :])
+        y_b = second_product((5, 6), h, wb)
 
-        hts = first_product(
-            2, wasq, [placed([P, 2 * H], U32, "waq_c%d" % a, (9 + 5 * a) * KIB) for a in range(PASSES)]
-        )
+        hts = [bank(j, [P, H]) for j in range(2)]
+        first_pass(2, 0, hts, wasq, placed([P, 2 * H], U32, "waq_c0", 8 * KIB))
+        v0_b = held([P, 1, PAIR], F32, "v0_b")
+        gated(1, v0_b[:], y_b[0][:, :1, :])
+        first_pass(2, 1, hts, wasq, placed([P, 2 * H], U32, "waq_c1", 12 * KIB))
         wb = wb_of(2)
-        grouped_c = held([P, PAIR, 4], BF16, "grouped_c")
-        turn_h(hts, [held([P, H], BF16, "hb_c%d" % j) for j in range(2)], grouped_c)
-        gated_b = [placed([P, PAIR], F32, "gated_b%d" % j, (16 + j) * KIB) for j in range(2)]
-        for j in range(2):
-            gate_slots(gated_b[j][:], yt_b[:, j, :], 2 + j)
-        scatter_gated(0, 0, ysb_a[:])
-        h = quantise(2, grouped_c, placed([P, PAIR], U32, "hq_c", 23 * KIB))
-        sums = turn_sums(4, sb_b, [gated_b[j][:] for j in range(2)])
-        ysb_b = placed([P, 2, PAIR], F32, "ysb_b", 16 * KIB)
-        nc.scalar.copy(out=ysb_b[:], in_=y01_b[:])
-        v2_b = held([P, PAIR], F32, "v2_b")
-        nc.scalar.copy(out=v2_b[:], in_=sums[:, 0, :])
-        scatter_values(2, 1, v2_b[:])
-        for r in range(2):
-            scatter_gated(r, 1, ysb_b[:, r, :])
-        y01_c = bank(5, [P, 2, PAIR])
-        for r in range(2):
-            y_by_row(y01_c[:, r, :], h, wb, r)
-        yt_c = bank(3, [P, 2, PAIR])
-        for j in range(2):
-            y_by_slot(yt_c[:, j, :], h, wb, j, PAIR, PAIR)
-        ysb_c = held([P, 2, PAIR], F32, "ysb_c")
-        nc.scalar.copy(out=ysb_c[:], in_=y01_c[:])
-        gated_c = [held([P, PAIR], F32, "gated_c%d" % j) for j in range(2)]
-        for j in range(2):
-            gate_slots(gated_c[j][:], yt_c[:, j, :], 4 + j)
-        v3_b = placed([P, PAIR], F32, "v3_b", 23 * KIB)
-        nc.scalar.copy(out=v3_b[:], in_=sums[:, 1, :])
-        scatter_values(3, 1, v3_b[:])
-        sums = turn_sums(2, sb_c, [gated_c[j][:] for j in range(2)])
-        v23_c = held([P, 2, PAIR], F32, "v23_c")
-        nc.scalar.copy(out=v23_c[:], in_=sums[:])
-        scatter_gated(1, 2, ysb_c[:, 1, :])
-        add_and_store(1, (0, 1))
-        scatter_gated(0, 2, ysb_c[:, 0, :])
-        add_and_store(0, (6, 7))
-        for d in range(2):
-            scatter_values(2 + d, 2, v23_c[:, d, :])
-            nc.scalar.dma_start(out=out[P * (2 + d) : P * (3 + d), :], in_=win[2 + d][:])
+        grouped = held([P, PAIR, 4], BF16, "grouped_c")
+        turn_h(hts, [held([P, H], BF16, "hb_c0"), placed([P, H], BF16, "hb_c1", 19 * KIB - 512)], 2, grouped)
+        scatter_on_scalar(0, 1, v0_b[:, 0, :])
+        v1_b = placed([P, 1, PAIR], F32, "v1_b", 18 * KIB)
+        gated(1, v1_b[:], y_b[0][:, 1:, :])
+        v23_b = placed([P, 2, PAIR], F32, "v23_b", 19 * KIB)
+        gated(1, v23_b[:], y_b[1][:])
+        h = quantise(2, grouped, held([P, PAIR], U32, "hq_c"))
+        scatter_on_scalar(1, 1, v1_b[:, 0, :])
+        scatter_on_scalar(2, 1, v23_b[:, 0, :])
+        scatter_on_vector(3, 1, v23_b[:, 1, :])
+        y_c = second_product((0, 4), h, wb)
+        v_c = [held([P, 2, PAIR], F32, "v_c%d" % half) for half in range(2)]
+        for half in range(2):
+            gated(2, v_c[half][:], y_c[half][:])
+        scatter_on_vector(3, 2, v_c[1][:, 1, :])
+        for r in range(3):
+            scatter_on_scalar(r, 2, v_c[r // 2][:, r % 2, :])
+        for r, banks in ((3, (5, 6)), (0, (7, 3)), (1, (1, 2)), (2, (0, 4))):
+            add_and_store(r, banks)

@@ -97,17 +97,16 @@ def tile_moe_dyl_none_kernel(
         zeros = held([P, P], F32, "zeros")
         win = [held([P, T], F32, "win%d" % r) for r in range(4)]
 
-        def clear_window(r, first, last):
+        def clear_window(r):
             nc.scalar.activation(
-                win[r][:, P * first : P * last].rearrange("p (a b) -> p a b", b=P),
-                zeros[:].unsqueeze(1).to_broadcast([P, last - first, P]),
+                win[r][:].rearrange("p (a b) -> p a b", b=P),
+                zeros[:].unsqueeze(1).to_broadcast([P, T // P, P]),
                 COPY,
             )
 
-        nc.vector.memset(zeros[:], 0.0)
-        clear_window(0, 0, 1)
         clear(xs[:])
         clear(was[:])
+        nc.vector.memset(zeros[:], 0.0)
         clear(wbs[:])
         nc.vector.memset(win[3][:], 0.0)
         clear(ws[:].rearrange("p a n -> p (a n)"))
@@ -116,13 +115,14 @@ def tile_moe_dyl_none_kernel(
         make_identity(nc, ident[:], nomemset=True)
 
         nc.sync.dma_start(tok_list[:], offs)
-        load_words(nc.sync, xw[0][:], x_words[0])
+        load_words(nc.scalar, xw[0][:], x_words[0])
         load_words(nc.sync, xw[1][:], x_words[1])
         nc.sync.dma_start(wa_list[:], offs2)
         load_scale_rows([nc.scalar] * 4, xs, x_scales)
+        load_scale_rows([nc.sync, nc.sync, nc.scalar, nc.scalar], was, wa_scales)
         load_words(nc.sync, waw[0][:], wa_words[0])
         load_words(nc.sync, waw[1][:], wa_words[1])
-        load_scale_rows([nc.scalar] * 4, was, wa_scales)
+        clear_window(0)
         nc.sync.dma_start(wb_list[:], offs3)
         load_words(nc.sync, wbw[:], wb_words[0])
         load_scale_rows([nc.scalar] * 4, wbs, wb_scales)
@@ -140,9 +140,8 @@ def tile_moe_dyl_none_kernel(
             gather(xq[a], xw[a][:].bitcast(U32), tok_list[:])
         gather(xsq, xs[:], tok_list[:])
 
-        clear_window(0, 1, T // P)
         for r in (1, 2):
-            clear_window(r, 0, T // P)
+            clear_window(r)
 
         def columns_of(entries, g):
             return entries[:, g * 2 * H // 16 : (g + 1) * 2 * H // 16]
@@ -200,14 +199,14 @@ def tile_moe_dyl_none_kernel(
             )
             return hq, hqs
 
-        def second_product(banks, h, wb):
-            ys = [bank(number, [P, 2, PAIR]) for number in banks]
-            for r in range(4):
+        def second_product(number, rows, h, wb):
+            y = bank(number, [P, len(rows), PAIR])
+            for place, r in enumerate(rows):
                 for j in range(2):
                     slots = slice(P * j, P * (j + 1))
                     cols = slice(N * j + P * r, N * j + P * (r + 1))
                     mx(
-                        ys[r // 2][:, r % 2, slots],
+                        y[:, place, slots],
                         wb[0][:, cols],
                         FP8X4,
                         wb[1][:, cols],
@@ -217,7 +216,7 @@ def tile_moe_dyl_none_kernel(
                         True,
                         True,
                     )
-            return ys
+            return y
 
         def gated(g, dst, y):
             weights = gate_sb[:, PAIR * g : PAIR * (g + 1)]
@@ -258,7 +257,7 @@ def tile_moe_dyl_none_kernel(
         wb = wb_of(0)
         wasq = wa_scales_of(1)
         h = quantise(0, grouped, placed([P, PAIR], U32, "hq_a", 4 * KIB))
-        y_a = second_product((7, 4), h, wb)
+        y_a = [second_product(5, (0, 1), h, wb), second_product(4, (2, 3), h, wb)]
 
         hts = [bank(j, [P, H]) for j in range(2)]
         first_pass(1, 0, hts, wasq, placed([P, 2 * H], U32, "waq_b0", 0))
@@ -268,7 +267,7 @@ def tile_moe_dyl_none_kernel(
         wb = wb_of(1)
         wasq = wa_scales_of(2)
         grouped = placed([P, PAIR, 4], BF16, "grouped_b", 8 * KIB)
-        turn_h(hts, [held([P, H], BF16, "hb_b0"), placed([P, H], BF16, "hb_b1", 16 * KIB)], 3, grouped)
+        turn_h(hts, [held([P, H], BF16, "hb_b0"), placed([P, H], BF16, "hb_b1", 16 * KIB)], 7, grouped)
         for r in range(2):
             scatter_on_scalar(r, 0, v01_a[:, r, :])
         v23_a = placed([P, 2, PAIR], F32, "v23_a", 16 * KIB)
@@ -276,31 +275,31 @@ def tile_moe_dyl_none_kernel(
         h = quantise(1, grouped, placed([P, PAIR], U32, "hq_b", 12 * KIB))
         for r in range(2):
             scatter_on_scalar(2 + r, 0, v23_a[:, r, :])
-        y_b = second_product((5, 6), h, wb)
+        y_b = [second_product(6, (0,), h, wb), second_product(3, (1, 2), h, wb), second_product(4, (3,), h, wb)]
 
         hts = [bank(j, [P, H]) for j in range(2)]
         first_pass(2, 0, hts, wasq, placed([P, 2 * H], U32, "waq_c0", 8 * KIB))
         v0_b = held([P, 1, PAIR], F32, "v0_b")
-        gated(1, v0_b[:], y_b[0][:, :1, :])
+        gated(1, v0_b[:], y_b[0][:])
         first_pass(2, 1, hts, wasq, placed([P, 2 * H], U32, "waq_c1", 12 * KIB))
         wb = wb_of(2)
         grouped = held([P, PAIR, 4], BF16, "grouped_c")
-        turn_h(hts, [held([P, H], BF16, "hb_c0"), placed([P, H], BF16, "hb_c1", 19 * KIB - 512)], 2, grouped)
+        turn_h(hts, [held([P, H], BF16, "hb_c0"), placed([P, H], BF16, "hb_c1", 22 * KIB - 512)], 2, grouped)
         scatter_on_scalar(0, 1, v0_b[:, 0, :])
-        v1_b = placed([P, 1, PAIR], F32, "v1_b", 18 * KIB)
-        gated(1, v1_b[:], y_b[0][:, 1:, :])
-        v23_b = placed([P, 2, PAIR], F32, "v23_b", 19 * KIB)
-        gated(1, v23_b[:], y_b[1][:])
+        v12_b = placed([P, 2, PAIR], F32, "v12_b", 20 * KIB)
+        gated(1, v12_b[:], y_b[1][:])
+        v3_b = placed([P, 1, PAIR], F32, "v3_b", 22 * KIB)
+        gated(1, v3_b[:], y_b[2][:])
         h = quantise(2, grouped, held([P, PAIR], U32, "hq_c"))
-        scatter_on_scalar(1, 1, v1_b[:, 0, :])
-        scatter_on_scalar(2, 1, v23_b[:, 0, :])
-        scatter_on_vector(3, 1, v23_b[:, 1, :])
-        y_c = second_product((0, 4), h, wb)
-        v_c = [held([P, 2, PAIR], F32, "v_c%d" % half) for half in range(2)]
-        for half in range(2):
-            gated(2, v_c[half][:], y_c[half][:])
-        scatter_on_vector(3, 2, v_c[1][:, 1, :])
+        for r in (1, 2):
+            scatter_on_scalar(r, 1, v12_b[:, r - 1, :])
+        scatter_on_vector(3, 1, v3_b[:, 0, :])
+        v_c = {}
+        for r, number in ((3, 4), (0, 0), (1, 2), (2, 3)):
+            v_c[r] = held([P, 1, PAIR], F32, "v%d_c" % r)
+            gated(2, v_c[r][:], second_product(number, (r,), h, wb)[:])
+        scatter_on_vector(3, 2, v_c[3][:, 0, :])
         for r in range(3):
-            scatter_on_scalar(r, 2, v_c[r // 2][:, r % 2, :])
-        for r, banks in ((3, (5, 6)), (0, (7, 3)), (1, (1, 2)), (2, (0, 4))):
+            scatter_on_scalar(r, 2, v_c[r][:, 0, :])
+        for r, banks in ((3, (5, 6)), (0, (7, 1)), (1, (4, 0)), (2, (2, 3))):
             add_and_store(r, banks)

@@ -115,17 +115,16 @@ def tile_moe_dyl_none_kernel(
         make_identity(nc, ident[:], nomemset=True)
 
         nc.sync.dma_start(tok_list[:], offs)
-        load_words(nc.scalar, xw[0][:], x_words[0])
+        load_words(nc.sync, xw[0][:], x_words[0])
         load_words(nc.sync, xw[1][:], x_words[1])
         nc.sync.dma_start(wa_list[:], offs2)
         load_scale_rows([nc.scalar] * 4, xs, x_scales)
-        load_scale_rows([nc.sync, nc.sync, nc.scalar, nc.scalar], was, wa_scales)
+        load_scale_rows([nc.sync] * 4, was, wa_scales)
         load_words(nc.sync, waw[0][:], wa_words[0])
         load_words(nc.sync, waw[1][:], wa_words[1])
-        clear_window(0)
         nc.sync.dma_start(wb_list[:], offs3)
-        load_words(nc.sync, wbw[:], wb_words[0])
         load_scale_rows([nc.scalar] * 4, wbs, wb_scales)
+        load_words(nc.sync, wbw[:], wb_words[0])
         nc.sync.dma_start(out=gate_sb[:], in_=gate)
         nc.sync.dma_start(out=ww[:].bitcast(I32), in_=w_words.rearrange("a p c -> p a c").bitcast(I32))
         for q in range(4):
@@ -140,7 +139,7 @@ def tile_moe_dyl_none_kernel(
             gather(xq[a], xw[a][:].bitcast(U32), tok_list[:])
         gather(xsq, xs[:], tok_list[:])
 
-        for r in (1, 2):
+        for r in range(3):
             clear_window(r)
 
         def columns_of(entries, g):

@@ -104,8 +104,8 @@ def tile_moe_dyl_none_kernel(
                 COPY,
             )
 
-        clear(xs[:])
         clear(was[:])
+        clear(xs[:])
         nc.vector.memset(zeros[:], 0.0)
         clear(wbs[:])
         nc.vector.memset(win[3][:], 0.0)
@@ -116,15 +116,15 @@ def tile_moe_dyl_none_kernel(
 
         nc.sync.dma_start(tok_list[:], offs)
         load_words(nc.sync, xw[0][:], x_words[0])
-        load_words(nc.sync, xw[1][:], x_words[1])
         nc.sync.dma_start(wa_list[:], offs2)
+        load_words(nc.sync, xw[1][:], x_words[1])
+        load_scale_rows([nc.scalar] * 4, was, wa_scales)
         load_scale_rows([nc.scalar] * 4, xs, x_scales)
-        load_scale_rows([nc.sync] * 4, was, wa_scales)
         load_words(nc.sync, waw[0][:], wa_words[0])
         load_words(nc.sync, waw[1][:], wa_words[1])
         nc.sync.dma_start(wb_list[:], offs3)
-        load_scale_rows([nc.scalar] * 4, wbs, wb_scales)
         load_words(nc.sync, wbw[:], wb_words[0])
+        load_scale_rows([nc.scalar] * 4, wbs, wb_scales)
         nc.sync.dma_start(out=gate_sb[:], in_=gate)
         nc.sync.dma_start(out=ww[:].bitcast(I32), in_=w_words.rearrange("a p c -> p a c").bitcast(I32))
         for q in range(4):
@@ -137,7 +137,6 @@ def tile_moe_dyl_none_kernel(
         xq = [held([P, SLOTS], U32, "xq%d" % a) for a in range(PASSES)]
         for a in range(PASSES):
             gather(xq[a], xw[a][:].bitcast(U32), tok_list[:])
-        gather(xsq, xs[:], tok_list[:])
 
         for r in range(3):
             clear_window(r)
@@ -248,6 +247,7 @@ def tile_moe_dyl_none_kernel(
                 nc.sync.dma_start(out=out[P * r : P * (r + 1), toks], in_=result[:])
 
         wasq = wa_scales_of(0)
+        gather(xsq, xs[:], tok_list[:])
         hts = [bank(j, [P, H]) for j in range(2)]
         for a in range(PASSES):
             first_pass(0, a, hts, wasq, held([P, 2 * H], U32, "waq_a%d" % a))

@@ -1,7 +1,6 @@
 from contextlib import ExitStack
 
 import concourse.mybir as mybir
-from concourse.masks import make_identity
 
 K, T, E, B, H, N = 1024, 1024, 4, 6, 512, 512
 FLOPS = 2 * K * N * T + 2 * 128 * B * (K * H + H * N)
@@ -92,7 +91,6 @@ def tile_moe_dyl_none_kernel(
         wbw = held([P, E * N], I32, "wbw")
         ww = held([P, PASSES, 2 * N], U8, "ww")
         ws = held([P, PASSES, N], U8, "ws")
-        ident = held([P, P], F32, "ident")
         gate_sb = held([P, SLOTS], F32, "gate_sb")
         zeros = held([P, P], F32, "zeros")
         win = [held([P, T], F32, "win%d" % r) for r in range(4)]
@@ -104,27 +102,25 @@ def tile_moe_dyl_none_kernel(
                 COPY,
             )
 
-        clear(was[:])
         clear(xs[:])
+        clear(was[:])
         nc.vector.memset(zeros[:], 0.0)
         clear(wbs[:])
         nc.vector.memset(win[3][:], 0.0)
         clear(ws[:].rearrange("p a n -> p (a n)"))
         clear(xs_low[96:, :])
-        nc.gpsimd.memset(ident[:], 0.0)
-        make_identity(nc, ident[:], nomemset=True)
 
         nc.sync.dma_start(tok_list[:], offs)
         load_words(nc.sync, xw[0][:], x_words[0])
-        nc.sync.dma_start(wa_list[:], offs2)
         load_words(nc.sync, xw[1][:], x_words[1])
-        load_scale_rows([nc.scalar] * 4, was, wa_scales)
+        nc.sync.dma_start(wa_list[:], offs2)
         load_scale_rows([nc.scalar] * 4, xs, x_scales)
+        load_scale_rows([nc.sync] * 4, was, wa_scales)
         load_words(nc.sync, waw[0][:], wa_words[0])
         load_words(nc.sync, waw[1][:], wa_words[1])
         nc.sync.dma_start(wb_list[:], offs3)
-        load_words(nc.sync, wbw[:], wb_words[0])
         load_scale_rows([nc.scalar] * 4, wbs, wb_scales)
+        load_words(nc.sync, wbw[:], wb_words[0])
         nc.sync.dma_start(out=gate_sb[:], in_=gate)
         nc.sync.dma_start(out=ww[:].bitcast(I32), in_=w_words.rearrange("a p c -> p a c").bitcast(I32))
         for q in range(4):
@@ -137,6 +133,7 @@ def tile_moe_dyl_none_kernel(
         xq = [held([P, SLOTS], U32, "xq%d" % a) for a in range(PASSES)]
         for a in range(PASSES):
             gather(xq[a], xw[a][:].bitcast(U32), tok_list[:])
+        gather(xsq, xs[:], tok_list[:])
 
         for r in range(3):
             clear_window(r)
@@ -147,41 +144,35 @@ def tile_moe_dyl_none_kernel(
         def tokens_of(g):
             return tok_list[:, g * PAIR // 16 : (g + 1) * PAIR // 16]
 
+        def dealt(tile):
+            return tile[:].rearrange("p (j t q) -> p j q t", j=2, t=4)
+
         def wa_scales_of(g):
             wasq = shared([P, 2 * H], U8, "wasq")
-            gather(wasq, was[:], columns_of(wa_list, g))
+            nc.vector.tensor_copy(dealt(wasq), was[:].indirect(columns_of(wa_list, g)))
             return wasq
 
         def first_pass(g, a, hts, wasq, waq):
-            gather(waq, waw[a][:].bitcast(U32), columns_of(wa_list, g))
+            nc.vector.tensor_copy(dealt(waq), waw[a][:].bitcast(U32).indirect(columns_of(wa_list, g)))
             for j in range(2):
                 slots = slice(PAIR * g + P * j, PAIR * g + P * (j + 1))
-                cols = slice(H * j, H * (j + 1))
-                mx(
-                    hts[j][:],
-                    xq[a][:, slots],
-                    FP8X4,
-                    xsq[4 * a :, slots],
-                    waq[:, cols],
-                    FP8X4,
-                    wasq[4 * a :, cols],
-                    a == 0,
-                    a == PASSES - 1,
-                )
+                for t in range(4):
+                    cols = slice(H * j + P * t, H * j + P * (t + 1))
+                    mx(
+                        hts[j][:, t, :],
+                        waq[:, cols],
+                        FP8X4,
+                        wasq[4 * a :, cols],
+                        xq[a][:, slots],
+                        FP8X4,
+                        xsq[4 * a :, slots],
+                        (a, t) == (0, 0),
+                        (a, t) == (PASSES - 1, 3),
+                    )
 
-        def turn_h(hts, hbs, number, grouped):
-            turned = bank(number, [P, 2, 2, P])
+        def round_h(hts, grouped):
             for j in range(2):
-                nc.scalar.copy(
-                    out=hbs[j][:].rearrange("s (u p e) -> s u p e", u=2, e=2),
-                    in_=hts[j][:].rearrange("s (p u e) -> s u p e", u=2, e=2),
-                )
-                for u in range(2):
-                    nc.tensor.transpose(turned[:, j, u, :], hbs[j][:].bitcast(F32)[:, P * u : P * (u + 1)], ident[:])
-            nc.scalar.copy(
-                out=grouped[:].bitcast(F32).rearrange("p (j s) u -> p j s u", j=2),
-                in_=turned[:].rearrange("p j u s -> p j s u"),
-            )
+                nc.scalar.copy(out=grouped[:, P * j : P * (j + 1), :], in_=hts[j][:].rearrange("p t s -> p s t"))
 
         def wb_of(g):
             wbsq = shared([P, 2 * N], U8, "wbsq")
@@ -247,18 +238,17 @@ def tile_moe_dyl_none_kernel(
                 nc.sync.dma_start(out=out[P * r : P * (r + 1), toks], in_=result[:])
 
         wasq = wa_scales_of(0)
-        gather(xsq, xs[:], tok_list[:])
-        hts = [bank(j, [P, H]) for j in range(2)]
+        hts = [bank(j, [P, 4, P]) for j in range(2)]
         for a in range(PASSES):
             first_pass(0, a, hts, wasq, held([P, 2 * H], U32, "waq_a%d" % a))
         grouped = placed([P, PAIR, 4], BF16, "grouped_a", 0)
-        turn_h(hts, [held([P, H], BF16, "hb_a%d" % j) for j in range(2)], 2, grouped)
+        round_h(hts, grouped)
         wb = wb_of(0)
         wasq = wa_scales_of(1)
         h = quantise(0, grouped, placed([P, PAIR], U32, "hq_a", 4 * KIB))
-        y_a = [second_product(5, (0, 1), h, wb), second_product(4, (2, 3), h, wb)]
+        y_a = [second_product(5, (0, 1), h, wb), second_product(7, (2, 3), h, wb)]
 
-        hts = [bank(j, [P, H]) for j in range(2)]
+        hts = [bank(j, [P, 4, P]) for j in range(2)]
         first_pass(1, 0, hts, wasq, placed([P, 2 * H], U32, "waq_b0", 0))
         v01_a = held([P, 2, PAIR], F32, "v01_a")
         gated(0, v01_a[:], y_a[0][:])
@@ -266,30 +256,30 @@ def tile_moe_dyl_none_kernel(
         wb = wb_of(1)
         wasq = wa_scales_of(2)
         grouped = placed([P, PAIR, 4], BF16, "grouped_b", 8 * KIB)
-        turn_h(hts, [held([P, H], BF16, "hb_b0"), placed([P, H], BF16, "hb_b1", 16 * KIB)], 7, grouped)
+        round_h(hts, grouped)
         for r in range(2):
             scatter_on_scalar(r, 0, v01_a[:, r, :])
-        v23_a = placed([P, 2, PAIR], F32, "v23_a", 16 * KIB)
+        v23_a = placed([P, 2, PAIR], F32, "v23_a", 6 * KIB)
         gated(0, v23_a[:], y_a[1][:])
         h = quantise(1, grouped, placed([P, PAIR], U32, "hq_b", 12 * KIB))
         for r in range(2):
             scatter_on_scalar(2 + r, 0, v23_a[:, r, :])
-        y_b = [second_product(6, (0,), h, wb), second_product(3, (1, 2), h, wb), second_product(4, (3,), h, wb)]
+        y_b = [second_product(6, (0,), h, wb), second_product(3, (1, 2), h, wb), second_product(2, (3,), h, wb)]
 
-        hts = [bank(j, [P, H]) for j in range(2)]
+        hts = [bank(j, [P, 4, P]) for j in range(2)]
         first_pass(2, 0, hts, wasq, placed([P, 2 * H], U32, "waq_c0", 8 * KIB))
         v0_b = held([P, 1, PAIR], F32, "v0_b")
         gated(1, v0_b[:], y_b[0][:])
         first_pass(2, 1, hts, wasq, placed([P, 2 * H], U32, "waq_c1", 12 * KIB))
         wb = wb_of(2)
-        grouped = held([P, PAIR, 4], BF16, "grouped_c")
-        turn_h(hts, [held([P, H], BF16, "hb_c0"), placed([P, H], BF16, "hb_c1", 22 * KIB - 512)], 2, grouped)
+        grouped = placed([P, PAIR, 4], BF16, "grouped_c", 16 * KIB)
+        round_h(hts, grouped)
         scatter_on_scalar(0, 1, v0_b[:, 0, :])
-        v12_b = placed([P, 2, PAIR], F32, "v12_b", 20 * KIB)
+        v12_b = placed([P, 2, PAIR], F32, "v12_b", 14 * KIB)
         gated(1, v12_b[:], y_b[1][:])
-        v3_b = placed([P, 1, PAIR], F32, "v3_b", 22 * KIB)
-        gated(1, v3_b[:], y_b[2][:])
         h = quantise(2, grouped, held([P, PAIR], U32, "hq_c"))
+        v3_b = placed([P, 1, PAIR], F32, "v3_b", 16 * KIB)
+        gated(1, v3_b[:], y_b[2][:])
         for r in (1, 2):
             scatter_on_scalar(r, 1, v12_b[:, r - 1, :])
         scatter_on_vector(3, 1, v3_b[:, 0, :])

@@ -93,7 +93,7 @@ def tile_moe_dyl_none_kernel(
         ws = held([P, PASSES, N], U8, "ws")
         gate_sb = held([P, SLOTS], F32, "gate_sb")
         zeros = held([P, P], F32, "zeros")
-        win = [held([P, T], F32, "win%d" % r) for r in range(4)]
+        win = {r: held([P, T], F32, "win%d" % r) for r in (0, 1, 3)}
 
         def clear_window(r):
             nc.scalar.activation(
@@ -135,7 +135,7 @@ def tile_moe_dyl_none_kernel(
             gather(xq[a], xw[a][:].bitcast(U32), tok_list[:])
         gather(xsq, xs[:], tok_list[:])
 
-        for r in range(3):
+        for r in range(2):
             clear_window(r)
 
         def columns_of(entries, g):
@@ -240,7 +240,9 @@ def tile_moe_dyl_none_kernel(
         wasq = wa_scales_of(0)
         hts = [bank(j, [P, 4, P]) for j in range(2)]
         for a in range(PASSES):
-            first_pass(0, a, hts, wasq, held([P, 2 * H], U32, "waq_a%d" % a))
+            first_pass(0, a, hts, wasq, shared([P, 2 * H], U32, "waq_a%d" % a))
+        win[2] = shared([P, T], F32, "waq_a1")
+        clear_window(2)
         grouped = placed([P, PAIR, 4], BF16, "grouped_a", 0)
         round_h(hts, grouped)
         wb = wb_of(0)

@@ -148,7 +148,7 @@ def tile_moe_dyl_none_kernel(
             return tile[:].rearrange("p (j t q) -> p j q t", j=2, t=4)
 
         def wa_scales_of(g):
-            wasq = shared([P, 2 * H], U8, "wasq")
+            wasq = held([P, 2 * H], U8, "wasq%d" % g)
             nc.vector.tensor_copy(dealt(wasq), was[:].indirect(columns_of(wa_list, g)))
             return wasq
 
@@ -174,12 +174,14 @@ def tile_moe_dyl_none_kernel(
             for j in range(2):
                 nc.scalar.copy(out=grouped[:, P * j : P * (j + 1), :], in_=hts[j][:].rearrange("p t s -> p s t"))
 
-        def wb_of(g):
-            wbsq = shared([P, 2 * N], U8, "wbsq")
+        def wb_scales_of(g, wbsq):
             gather(wbsq, wbs[:], columns_of(wb_list, g))
+            return wbsq
+
+        def wb_words_of(g):
             wbq = shared([P, 2 * N], U32, "wbq")
             gather(wbq, wbw[:].bitcast(U32), columns_of(wb_list, g))
-            return wbq, wbsq
+            return wbq
 
         def quantise(g, grouped, hq):
             hqs = held([P, PAIR], U8, "hqs%d" % g)
@@ -237,54 +239,57 @@ def tile_moe_dyl_none_kernel(
                 nc.vector.tensor_tensor(result[:], acc[:], win[r][:, toks], ADD)
                 nc.sync.dma_start(out=out[P * r : P * (r + 1), toks], in_=result[:])
 
-        wasq = wa_scales_of(0)
+        wasq = [wa_scales_of(g) for g in range(3)]
         hts = [bank(j, [P, 4, P]) for j in range(2)]
         for a in range(PASSES):
-            first_pass(0, a, hts, wasq, shared([P, 2 * H], U32, "waq_a%d" % a))
+            first_pass(0, a, hts, wasq[0], shared([P, 2 * H], U32, "waq_a%d" % a))
         win[2] = shared([P, T], F32, "waq_a1")
         clear_window(2)
         grouped = placed([P, PAIR, 4], BF16, "grouped_a", 0)
         round_h(hts, grouped)
-        wb = wb_of(0)
-        wasq = wa_scales_of(1)
+        wbsq = [wb_scales_of(g, held([P, 2 * N], U8, "wbsq%d" % g)) for g in range(2)]
+        wb = (wb_words_of(0), wbsq[0])
         h = quantise(0, grouped, placed([P, PAIR], U32, "hq_a", 4 * KIB))
         y_a = [second_product(5, (0, 1), h, wb), second_product(7, (2, 3), h, wb)]
 
         hts = [bank(j, [P, 4, P]) for j in range(2)]
-        first_pass(1, 0, hts, wasq, placed([P, 2 * H], U32, "waq_b0", 0))
-        v01_a = held([P, 2, PAIR], F32, "v01_a")
-        gated(0, v01_a[:], y_a[0][:])
-        first_pass(1, 1, hts, wasq, placed([P, 2 * H], U32, "waq_b1", 4 * KIB))
-        wb = wb_of(1)
-        wasq = wa_scales_of(2)
-        grouped = placed([P, PAIR, 4], BF16, "grouped_b", 8 * KIB)
+        first_pass(1, 0, hts, wasq[1], placed([P, 2 * H], U32, "waq_b0", 0))
+        v0_a = held([P, 1, PAIR], F32, "v0_a")
+        gated(0, v0_a[:], y_a[0][:, :1, :])
+        first_pass(1, 1, hts, wasq[1], placed([P, 2 * H], U32, "waq_b1", 4 * KIB))
+        wb = (wb_words_of(1), wbsq[1])
+        grouped = placed([P, PAIR, 4], BF16, "grouped_b", 11 * KIB)
         round_h(hts, grouped)
-        for r in range(2):
-            scatter_on_scalar(r, 0, v01_a[:, r, :])
+        scatter_on_scalar(0, 0, v0_a[:, 0, :])
+        v1_a = placed([P, 1, PAIR], F32, "v1_a", 5 * KIB)
+        gated(0, v1_a[:], y_a[0][:, 1:, :])
         v23_a = placed([P, 2, PAIR], F32, "v23_a", 6 * KIB)
         gated(0, v23_a[:], y_a[1][:])
-        h = quantise(1, grouped, placed([P, PAIR], U32, "hq_b", 12 * KIB))
+        wbsq.append(wb_scales_of(2, placed([P, 2 * N], U8, "wbsq2", 4 * KIB)))
+        h = quantise(1, grouped, held([P, PAIR], U32, "hq_b"))
+        scatter_on_scalar(1, 0, v1_a[:, 0, :])
         for r in range(2):
             scatter_on_scalar(2 + r, 0, v23_a[:, r, :])
         y_b = [second_product(6, (0,), h, wb), second_product(3, (1, 2), h, wb), second_product(2, (3,), h, wb)]
 
         hts = [bank(j, [P, 4, P]) for j in range(2)]
-        first_pass(2, 0, hts, wasq, placed([P, 2 * H], U32, "waq_c0", 8 * KIB))
-        v0_b = held([P, 1, PAIR], F32, "v0_b")
-        gated(1, v0_b[:], y_b[0][:])
-        first_pass(2, 1, hts, wasq, placed([P, 2 * H], U32, "waq_c1", 12 * KIB))
-        wb = wb_of(2)
+        for a in range(PASSES):
+            first_pass(2, a, hts, wasq[2], placed([P, 2 * H], U32, "waq_c%d" % a, (8 + 4 * a) * KIB))
+        wb = (wb_words_of(2), wbsq[2])
         grouped = placed([P, PAIR, 4], BF16, "grouped_c", 16 * KIB)
         round_h(hts, grouped)
-        scatter_on_scalar(0, 1, v0_b[:, 0, :])
+        v0_b = placed([P, 1, PAIR], F32, "v0_b", 13 * KIB)
+        gated(1, v0_b[:], y_b[0][:])
         v12_b = placed([P, 2, PAIR], F32, "v12_b", 14 * KIB)
         gated(1, v12_b[:], y_b[1][:])
         h = quantise(2, grouped, held([P, PAIR], U32, "hq_c"))
         v3_b = placed([P, 1, PAIR], F32, "v3_b", 16 * KIB)
         gated(1, v3_b[:], y_b[2][:])
-        for r in (1, 2):
-            scatter_on_scalar(r, 1, v12_b[:, r - 1, :])
+        scatter_on_scalar(0, 1, v0_b[:, 0, :])
+        scatter_on_scalar(1, 1, v12_b[:, 0, :])
         scatter_on_vector(3, 1, v3_b[:, 0, :])
+        nc.vector.tensor_copy(win[2][:].indirect(tokens_of(1)[:, : P // 16]), v12_b[:, 1, :P])
+        nc.scalar.activation(win[2][:].indirect(tokens_of(1)[:, P // 16 :]), v12_b[:, 1, P:], COPY)
         v_c = {}
         for r, number in ((3, 4), (0, 0), (1, 2), (2, 3)):
             v_c[r] = held([P, 1, PAIR], F32, "v%d_c" % r)

@@ -21,9 +21,8 @@ P = 128
 PASSES = K // 512
 SLOTS = P * B
 BANK = 512
-PAIR = 2 * P
 KIB = 1024
-LOWERED = 112
+LOWERED = 100
 
 
 def tile_moe_dyl_none_kernel(
@@ -38,41 +37,29 @@ def tile_moe_dyl_none_kernel(
         def held(shape, dtype, name):
             return keep.tile(shape, dtype, name=name, align_bytes=64)
 
-        def shared(shape, dtype, tag):
-            return keep.tile(shape, dtype, name=tag, tag=tag, align_bytes=64)
-
         def placed(shape, dtype, name, offset):
             return reuse.tile(shape, dtype, name=name, offset=offset, align_bytes=64)
 
         def bank(number, shape):
             return psum.tile(shape, F32, name="bank%d" % number, offset=4 * BANK * number)
 
-        def clear(region):
-            nc.vector.memset(region.bitcast(I32), 0)
+        def load(tile, source):
+            nc.sync.dma_start(out=tile.bitcast(I32), in_=source.bitcast(I32))
 
-        def load_words(queue, tile, words):
-            queue.dma_start(out=tile, in_=words.rearrange("p c d -> p (c d)").bitcast(I32))
+        def load_words(tile, words):
+            load(tile[:], words.rearrange("p c d -> p (c d)"))
 
-        def load_scale_rows(queues, plane, scales):
+        def load_scale_rows(plane, scales):
             rows = 4 * scales.shape[0]
             for q in range(4):
-                queues[q].dma_start(
-                    out=plane[32 * q : 32 * q + rows, :].bitcast(I32),
-                    in_=scales[:, 4 * q : 4 * q + 4, :].bitcast(I32),
-                )
+                load(plane[32 * q : 32 * q + rows, :], scales[:, 4 * q : 4 * q + 4, :])
 
-        def lower(queue, dst, src):
-            queue.dma_start(out=dst[:LOWERED, :].bitcast(I32), in_=src[4 : 4 + LOWERED, :].bitcast(I32))
-
-        def gather(dst, window, entries):
-            nc.vector.tensor_copy(dst[:], window.indirect(entries))
-
-        def mx(acc, lhs, lhs_type, lhs_scale, rhs, rhs_type, rhs_scale, start, stop):
+        def mx(acc, lhs, lhs_type, lhs_scale, rhs, rhs_scale, start, stop):
             nc.tensor.matmul_mx(
                 out=acc,
                 lhsT=lhs.bitcast(lhs_type),
                 lhsT_scale=lhs_scale,
-                rhs=rhs.bitcast(rhs_type),
+                rhs=rhs.bitcast(FP8X4),
                 rhs_scale=rhs_scale,
                 start=start,
                 stop=stop,
@@ -84,140 +71,126 @@ def tile_moe_dyl_none_kernel(
         xw = [held([P, T], I32, "xw%d" % a) for a in range(PASSES)]
         xs = held([P, T], U8, "xs")
         xs_low = held([P, T], U8, "xs_low")
-        xsq = held([P, SLOTS], U8, "xsq")
         was = held([P, E * H], U8, "was")
         waw = [held([P, E * H], I32, "waw%d" % a) for a in range(PASSES)]
         wbs = held([P, E * N], U8, "wbs")
         wbw = held([P, E * N], I32, "wbw")
         ww = held([P, PASSES, 2 * N], U8, "ww")
         ws = held([P, PASSES, N], U8, "ws")
-        gate_sb = held([P, SLOTS], F32, "gate_sb")
+        gate_first = held([P, P], F32, "gate_first")
+        gate_rest = held([P, SLOTS - P], F32, "gate_rest")
         zeros = held([P, P], F32, "zeros")
-        win = {r: held([P, T], F32, "win%d" % r) for r in (0, 1, 3)}
+        win = [held([P, T], F32, "win%d" % r) for r in range(4)]
 
-        def clear_window(r):
+        nc.vector.memset(xs[:].bitcast(I32), 0)
+        nc.vector.memset(was[:].bitcast(I32), 0)
+        nc.vector.memset(zeros[:], 0.0)
+        nc.vector.memset(wbs[:].bitcast(I32), 0)
+        nc.vector.memset(ws[:].rearrange("p a n -> p (a n)").bitcast(I32), 0)
+        nc.vector.memset(xs_low[96:, :].bitcast(I32), 0)
+        for r in range(4):
             nc.scalar.activation(
                 win[r][:].rearrange("p (a b) -> p a b", b=P),
                 zeros[:].unsqueeze(1).to_broadcast([P, T // P, P]),
                 COPY,
             )
 
-        clear(xs[:])
-        clear(was[:])
-        nc.vector.memset(zeros[:], 0.0)
-        clear(wbs[:])
-        nc.vector.memset(win[3][:], 0.0)
-        clear(ws[:].rearrange("p a n -> p (a n)"))
-        clear(xs_low[96:, :])
-
         nc.sync.dma_start(tok_list[:], offs)
-        load_words(nc.sync, xw[0][:], x_words[0])
-        load_words(nc.sync, xw[1][:], x_words[1])
+        load_scale_rows(xs, x_scales)
+        for a in range(PASSES):
+            load_words(xw[a], x_words[a])
         nc.sync.dma_start(wa_list[:], offs2)
-        load_scale_rows([nc.scalar] * 4, xs, x_scales)
-        load_scale_rows([nc.sync] * 4, was, wa_scales)
-        load_words(nc.sync, waw[0][:], wa_words[0])
-        load_words(nc.sync, waw[1][:], wa_words[1])
+        load_scale_rows(was, wa_scales)
+        load_words(waw[0], wa_words[0])
         nc.sync.dma_start(wb_list[:], offs3)
-        load_scale_rows([nc.scalar] * 4, wbs, wb_scales)
-        load_words(nc.sync, wbw[:], wb_words[0])
-        nc.sync.dma_start(out=gate_sb[:], in_=gate)
-        nc.sync.dma_start(out=ww[:].bitcast(I32), in_=w_words.rearrange("a p c -> p a c").bitcast(I32))
+        load_scale_rows(wbs, wb_scales)
+        load_words(waw[1], wa_words[1])
+        load_words(wbw, wb_words[0])
+        nc.sync.dma_start(out=gate_first[:], in_=gate[:, :P])
+        nc.sync.dma_start(out=gate_rest[:], in_=gate[:, P:])
+        load(ww[:], w_words.rearrange("a p c -> p a c"))
         for q in range(4):
-            nc.sync.dma_start(
-                out=ws[32 * q : 32 * q + 4, :, :].bitcast(I32),
-                in_=w_scales[:, 4 * q : 4 * q + 4, :].rearrange("a r n -> r a n").bitcast(I32),
-            )
-        lower(nc.sync, xs_low, xs)
+            load(ws[32 * q : 32 * q + 4, :, :], w_scales[:, 4 * q : 4 * q + 4, :].rearrange("a r n -> r a n"))
+        load(xs_low[:LOWERED, :], xs[4 : 4 + LOWERED, :])
 
+        xsq = held([P, SLOTS], U8, "xsq")
+        nc.vector.tensor_copy(xsq[:], xs[:].indirect(tok_list[:]))
         xq = [held([P, SLOTS], U32, "xq%d" % a) for a in range(PASSES)]
         for a in range(PASSES):
-            gather(xq[a], xw[a][:].bitcast(U32), tok_list[:])
-        gather(xsq, xs[:], tok_list[:])
+            nc.vector.tensor_copy(xq[a][:], xw[a][:].bitcast(U32).indirect(tok_list[:]))
 
-        for r in range(2):
-            clear_window(r)
+        def columns_of(entries, blocks):
+            return entries[:, blocks[0] * H // 16 : (blocks[-1] + 1) * H // 16]
 
-        def columns_of(entries, g):
-            return entries[:, g * 2 * H // 16 : (g + 1) * 2 * H // 16]
+        def tokens_of(blocks):
+            return tok_list[:, blocks[0] * P // 16 : (blocks[-1] + 1) * P // 16]
 
-        def tokens_of(g):
-            return tok_list[:, g * PAIR // 16 : (g + 1) * PAIR // 16]
+        def gather(dst, window, entries, blocks):
+            nc.vector.tensor_copy(dst[:], window.indirect(columns_of(entries, blocks)))
+            return {m: dst[:, N * j : N * (j + 1)] for j, m in enumerate(blocks)}
 
-        def dealt(tile):
-            return tile[:].rearrange("p (j t q) -> p j q t", j=2, t=4)
+        def gather_dealt(dst, window, blocks):
+            dealt = dst[:].rearrange("p (j t q) -> p j q t", j=len(blocks), t=4)
+            nc.vector.tensor_copy(dealt, window.indirect(columns_of(wa_list, blocks)))
+            return {m: dst[:, H * j : H * (j + 1)] for j, m in enumerate(blocks)}
 
-        def wa_scales_of(g):
-            wasq = held([P, 2 * H], U8, "wasq%d" % g)
-            nc.vector.tensor_copy(dealt(wasq), was[:].indirect(columns_of(wa_list, g)))
-            return wasq
-
-        def first_pass(g, a, hts, wasq, waq):
-            nc.vector.tensor_copy(dealt(waq), waw[a][:].bitcast(U32).indirect(columns_of(wa_list, g)))
-            for j in range(2):
-                slots = slice(PAIR * g + P * j, PAIR * g + P * (j + 1))
+        def first_product(a, blocks, dst, scales, hts):
+            words = gather_dealt(dst, waw[a][:].bitcast(U32), blocks)
+            for m in blocks:
+                slots = slice(P * m, P * (m + 1))
                 for t in range(4):
-                    cols = slice(H * j + P * t, H * j + P * (t + 1))
+                    cols = slice(P * t, P * (t + 1))
                     mx(
-                        hts[j][:, t, :],
-                        waq[:, cols],
+                        hts[m][:, t, :],
+                        words[m][:, cols],
                         FP8X4,
-                        wasq[4 * a :, cols],
+                        scales[m][4 * a :, cols],
                         xq[a][:, slots],
-                        FP8X4,
                         xsq[4 * a :, slots],
                         (a, t) == (0, 0),
                         (a, t) == (PASSES - 1, 3),
                     )
 
-        def round_h(hts, grouped):
-            for j in range(2):
-                nc.scalar.copy(out=grouped[:, P * j : P * (j + 1), :], in_=hts[j][:].rearrange("p t s -> p s t"))
+        def round_h(blocks, hts, grouped):
+            for j, m in enumerate(blocks):
+                nc.scalar.copy(out=grouped[:, P * j : P * (j + 1), :], in_=hts[m][:].rearrange("p t s -> p s t"))
 
-        def wb_scales_of(g, wbsq):
-            gather(wbsq, wbs[:], columns_of(wb_list, g))
-            return wbsq
-
-        def wb_words_of(g):
-            wbq = shared([P, 2 * N], U32, "wbq")
-            gather(wbq, wbw[:].bitcast(U32), columns_of(wb_list, g))
-            return wbq
-
-        def quantise(g, grouped, hq):
-            hqs = held([P, PAIR], U8, "hqs%d" % g)
+        def quantise(blocks, grouped, hq):
+            hqs = held([P, P * len(blocks)], U8, "hqs%d" % blocks[0])
             nc.vector.quantize_mx(
                 out=hq[:].bitcast(FP8X4), scales=hqs[:], in_=grouped[:].rearrange("p s t -> p (s t)")
             )
-            return hq, hqs
+            return {m: (hq[:, P * j : P * (j + 1)], hqs[:, P * j : P * (j + 1)]) for j, m in enumerate(blocks)}
 
-        def second_product(number, rows, h, wb):
-            y = bank(number, [P, len(rows), PAIR])
+        def second_product(number, rows, blocks, h, words, scales):
+            y = bank(number, [P, len(rows), P * len(blocks)])
             for place, r in enumerate(rows):
-                for j in range(2):
-                    slots = slice(P * j, P * (j + 1))
-                    cols = slice(N * j + P * r, N * j + P * (r + 1))
+                cols = slice(P * r, P * (r + 1))
+                for j, m in enumerate(blocks):
                     mx(
-                        y[:, place, slots],
-                        wb[0][:, cols],
+                        y[:, place, P * j : P * (j + 1)],
+                        words[m][:, cols],
                         FP8X4,
-                        wb[1][:, cols],
-                        h[0][:, slots],
-                        FP8X4,
-                        h[1][:, slots],
+                        scales[m][:, cols],
+                        h[m][0],
+                        h[m][1],
                         True,
                         True,
                     )
             return y
 
-        def gated(g, dst, y):
-            weights = gate_sb[:, PAIR * g : PAIR * (g + 1)]
-            nc.vector.tensor_tensor(dst, y, weights.unsqueeze(1).to_broadcast([P, y.shape[1], PAIR]), MULT)
+        def gated(blocks, dst, y):
+            width = P * len(blocks)
+            first = P * (blocks[0] - 1)
+            weights = gate_rest[:, first : first + width] if blocks[0] else gate_first[:]
+            nc.vector.tensor_tensor(dst[:], y, weights.unsqueeze(1).to_broadcast([P, y.shape[1], width]), MULT)
+            return dst
 
-        def scatter_on_scalar(r, g, values):
-            nc.scalar.activation(win[r][:].indirect(tokens_of(g)), values, COPY)
+        def scatter_on_scalar(r, blocks, values):
+            nc.scalar.activation(win[r][:].indirect(tokens_of(blocks)), values, COPY)
 
-        def scatter_on_vector(r, g, values):
-            nc.vector.tensor_copy(win[r][:].indirect(tokens_of(g)), values)
+        def scatter_on_vector(r, blocks, values):
+            nc.vector.tensor_copy(win[r][:].indirect(tokens_of(blocks)), values)
 
         def add_and_store(r, banks):
             for c in range(2):
@@ -230,7 +203,6 @@ def tile_moe_dyl_none_kernel(
                         FP4X4,
                         ws[:, a, P * r : P * (r + 1)],
                         xw[a][:, toks],
-                        FP8X4,
                         (xs, xs_low)[a][:, toks],
                         a == 0,
                         a == PASSES - 1,
@@ -239,63 +211,73 @@ def tile_moe_dyl_none_kernel(
                 nc.vector.tensor_tensor(result[:], acc[:], win[r][:, toks], ADD)
                 nc.sync.dma_start(out=out[P * r : P * (r + 1), toks], in_=result[:])
 
-        wasq = [wa_scales_of(g) for g in range(3)]
-        hts = [bank(j, [P, 4, P]) for j in range(2)]
-        for a in range(PASSES):
-            first_pass(0, a, hts, wasq[0], shared([P, 2 * H], U32, "waq_a%d" % a))
-        win[2] = shared([P, T], F32, "waq_a1")
-        clear_window(2)
-        grouped = placed([P, PAIR, 4], BF16, "grouped_a", 0)
-        round_h(hts, grouped)
-        wbsq = [wb_scales_of(g, held([P, 2 * N], U8, "wbsq%d" % g)) for g in range(2)]
-        wb = (wb_words_of(0), wbsq[0])
-        h = quantise(0, grouped, placed([P, PAIR], U32, "hq_a", 4 * KIB))
-        y_a = [second_product(5, (0, 1), h, wb), second_product(7, (2, 3), h, wb)]
+        wb_window = wbw[:].bitcast(U32)
 
-        hts = [bank(j, [P, 4, P]) for j in range(2)]
-        first_pass(1, 0, hts, wasq[1], placed([P, 2 * H], U32, "waq_b0", 0))
-        v0_a = held([P, 1, PAIR], F32, "v0_a")
-        gated(0, v0_a[:], y_a[0][:, :1, :])
-        first_pass(1, 1, hts, wasq[1], placed([P, 2 * H], U32, "waq_b1", 4 * KIB))
-        wb = (wb_words_of(1), wbsq[1])
-        grouped = placed([P, PAIR, 4], BF16, "grouped_b", 11 * KIB)
-        round_h(hts, grouped)
-        scatter_on_scalar(0, 0, v0_a[:, 0, :])
-        v1_a = placed([P, 1, PAIR], F32, "v1_a", 5 * KIB)
-        gated(0, v1_a[:], y_a[0][:, 1:, :])
-        v23_a = placed([P, 2, PAIR], F32, "v23_a", 6 * KIB)
-        gated(0, v23_a[:], y_a[1][:])
-        wbsq.append(wb_scales_of(2, placed([P, 2 * N], U8, "wbsq2", 4 * KIB)))
-        h = quantise(1, grouped, held([P, PAIR], U32, "hq_b"))
-        scatter_on_scalar(1, 0, v1_a[:, 0, :])
-        for r in range(2):
-            scatter_on_scalar(2 + r, 0, v23_a[:, r, :])
-        y_b = [second_product(6, (0,), h, wb), second_product(3, (1, 2), h, wb), second_product(2, (3,), h, wb)]
+        wasq = gather_dealt(held([P, 2 * H], U8, "wasq_01"), was[:], (0, 1))
+        hts = {m: bank(m, [P, 4, P]) for m in (0, 1)}
+        first_product(0, (0, 1), held([P, 2 * H], U32, "waq0_01"), wasq, hts)
+        wbsq = gather(placed([P, 2 * N], U8, "wbsq_01", 2 * KIB), wbs[:], wb_list, (0, 1))
+        grouped = {}
+        for m in (0, 1):
+            first_product(1, (m,), placed([P, H], U32, "waq1_%d" % m, 24 * KIB * m), wasq, hts)
+            grouped[m] = held([P, P, 4], BF16, "grouped_%d" % m)
+            round_h((m,), hts, grouped[m])
+        pair = (2, 3)
+        wasq = gather_dealt(placed([P, 2 * H], U8, "wasq_23", 0), was[:], pair)
+        wbq_0 = gather(placed([P, N], U32, "wbq_0", 3 * KIB), wb_window, wb_list, (0,))
+        h_0 = quantise((0,), grouped[0], placed([P, P], U32, "hq_0", 7 * KIB))
+        wbq_1 = gather(placed([P, N], U32, "wbq_1", 5 * KIB), wb_window, wb_list, (1,))
+        y_first = second_product(5, (0,), (0,), h_0, wbq_0, wbsq)
+        y_rest = second_product(6, (1, 2, 3), (0,), h_0, wbq_0, wbsq)
+        values = gated((0,), held([P, 1, P], F32, "v0_0"), y_first[:])
+        scatter_on_scalar(0, (0,), values[:, 0, :])
+        h_1 = quantise((1,), grouped[1], placed([P, P], U32, "hq_1", 7 * KIB))
+        y_1 = second_product(7, (0, 1, 2, 3), (1,), h_1, wbq_1, wbsq)
+        values = gated((0,), held([P, 3, P], F32, "v123_0"), y_rest[:])
+        for r in (1, 2, 3):
+            scatter_on_scalar(r, (0,), values[:, r - 1, :])
 
-        hts = [bank(j, [P, 4, P]) for j in range(2)]
-        for a in range(PASSES):
-            first_pass(2, a, hts, wasq[2], placed([P, 2 * H], U32, "waq_c%d" % a, (8 + 4 * a) * KIB))
-        wb = (wb_words_of(2), wbsq[2])
-        grouped = placed([P, PAIR, 4], BF16, "grouped_c", 16 * KIB)
-        round_h(hts, grouped)
-        v0_b = placed([P, 1, PAIR], F32, "v0_b", 13 * KIB)
-        gated(1, v0_b[:], y_b[0][:])
-        v12_b = placed([P, 2, PAIR], F32, "v12_b", 14 * KIB)
-        gated(1, v12_b[:], y_b[1][:])
-        h = quantise(2, grouped, held([P, PAIR], U32, "hq_c"))
-        v3_b = placed([P, 1, PAIR], F32, "v3_b", 16 * KIB)
-        gated(1, v3_b[:], y_b[2][:])
-        scatter_on_scalar(0, 1, v0_b[:, 0, :])
-        scatter_on_scalar(1, 1, v12_b[:, 0, :])
-        scatter_on_vector(3, 1, v3_b[:, 0, :])
-        nc.vector.tensor_copy(win[2][:].indirect(tokens_of(1)[:, : P // 16]), v12_b[:, 1, :P])
-        nc.scalar.activation(win[2][:].indirect(tokens_of(1)[:, P // 16 :]), v12_b[:, 1, P:], COPY)
-        v_c = {}
-        for r, number in ((3, 4), (0, 0), (1, 2), (2, 3)):
-            v_c[r] = held([P, 1, PAIR], F32, "v%d_c" % r)
-            gated(2, v_c[r][:], second_product(number, (r,), h, wb)[:])
-        scatter_on_vector(3, 2, v_c[3][:, 0, :])
-        for r in range(3):
-            scatter_on_scalar(r, 2, v_c[r][:, 0, :])
-        for r, banks in ((3, (5, 6)), (0, (7, 1)), (1, (4, 0)), (2, (2, 3))):
+        hts = {m: bank(m % 2, [P, 4, P]) for m in pair}
+        first_product(0, pair, placed([P, 2 * H], U32, "waq0_23", 3 * KIB), wasq, hts)
+        first_product(1, pair, placed([P, 2 * H], U32, "waq1_23", 7 * KIB), wasq, hts)
+        grouped = placed([P, 2 * P, 4], BF16, "grouped_23", 19 * KIB)
+        round_h(pair, hts, grouped)
+        wbsq = gather(placed([P, 2 * N], U8, "wbsq_23", 2 * KIB), wbs[:], wb_list, pair)
+        values = gated((1,), placed([P, 4, P], F32, "v_1", 7 * KIB), y_1[:])
+        for r in range(4):
+            scatter_on_scalar(r, (1,), values[:, r, :])
+        wbq = gather(placed([P, 2 * N], U32, "wbq_23", 9 * KIB), wb_window, wb_list, pair)
+        h = quantise(pair, grouped, placed([P, 2 * P], U32, "hq_23", 13 * KIB))
+        y_0 = second_product(2, (0,), pair, h, wbq, wbsq)
+        y_12 = second_product(3, (1, 2), pair, h, wbq, wbsq)
+        y_3 = second_product(4, (3,), pair, h, wbq, wbsq)
+
+        last = (4, 5)
+        wasq = gather_dealt(placed([P, 2 * H], U8, "wasq_45", 19 * KIB), was[:], last)
+        values = gated(pair, held([P, 1, 2 * P], F32, "v0_23"), y_0[:])
+        scatter_on_scalar(0, pair, values[:, 0, :])
+        values = gated(pair, held([P, 1, 2 * P], F32, "v1_23"), y_12[:, :1, :])
+        scatter_on_scalar(1, pair, values[:, 0, :])
+        hts = {m: bank(m % 2, [P, 4, P]) for m in last}
+        first_product(0, last, placed([P, 2 * H], U32, "waq0_45", 9 * KIB), wasq, hts)
+        first_product(1, last, placed([P, 2 * H], U32, "waq1_45", 13 * KIB), wasq, hts)
+        grouped = placed([P, 2 * P, 4], BF16, "grouped_45", 22 * KIB)
+        round_h(last, hts, grouped)
+        wbsq = gather(placed([P, 2 * N], U8, "wbsq_45", 2 * KIB), wbs[:], wb_list, last)
+        values = gated((2,), placed([P, 1, P], F32, "v3_2", 14 * KIB), y_3[:, :, :P])
+        scatter_on_scalar(3, (2,), values[:, 0, :])
+        values = gated(pair, placed([P, 1, 2 * P], F32, "v2_23", 13 * KIB), y_12[:, 1:, :])
+        scatter_on_scalar(2, pair, values[:, 0, :])
+        wbq = gather(placed([P, 2 * N], U32, "wbq_45", 14 * KIB + 512), wb_window, wb_list, last)
+        h = quantise(last, grouped, held([P, 2 * P], U32, "hq_45"))
+        values = gated((3,), placed([P, 1, P], F32, "v3_3", 22 * KIB), y_3[:, :, P:])
+        scatter_on_vector(3, (3,), values[:, 0, :])
+        values = gated(last, held([P, 1, 2 * P], F32, "v0_45"), second_product(2, (0,), last, h, wbq, wbsq)[:])
+        scatter_on_scalar(0, last, values[:, 0, :])
+        v_3 = gated(last, held([P, 1, 2 * P], F32, "v3_45"), second_product(3, (3,), last, h, wbq, wbsq)[:])
+        values = gated(last, held([P, 2, 2 * P], F32, "v12_45"), second_product(4, (1, 2), last, h, wbq, wbsq)[:])
+        scatter_on_vector(3, last, v_3[:, 0, :])
+        for r in (1, 2):
+            scatter_on_scalar(r, last, values[:, r - 1, :])
+        for r, banks in ((3, (5, 6)), (0, (7, 0)), (1, (2, 3)), (2, (4, 5))):
             add_and_store(r, banks)

@@ -248,8 +248,8 @@ def tile_moe_dyl_none_kernel(
             scatter_on_scalar(r, (1,), values[:, r, :])
         wbq = gather(placed([P, 2 * N], U32, "wbq_23", 9 * KIB), wb_window, wb_list, pair)
         h = quantise(pair, grouped, placed([P, 2 * P], U32, "hq_23", 13 * KIB))
-        y_0 = second_product(2, (0,), pair, h, wbq, wbsq)
-        y_12 = second_product(3, (1, 2), pair, h, wbq, wbsq)
+        y_0 = second_product(5, (0,), pair, h, wbq, wbsq)
+        y_12 = second_product(6, (1, 2), pair, h, wbq, wbsq)
         y_3 = second_product(4, (3,), pair, h, wbq, wbsq)
 
         last = (4, 5)
@@ -279,5 +279,5 @@ def tile_moe_dyl_none_kernel(
         scatter_on_vector(3, last, v_3[:, 0, :])
         for r in (1, 2):
             scatter_on_scalar(r, last, values[:, r - 1, :])
-        for r, banks in ((3, (5, 6)), (0, (7, 0)), (1, (2, 3)), (2, (4, 5))):
+        for r, banks in ((3, (7, 5)), (0, (6, 2)), (1, (3, 4)), (2, (7, 5))):
             add_and_store(r, banks)

@@ -77,10 +77,16 @@ def tile_moe_dyl_none_kernel(
         wbw = held([P, E * N], I32, "wbw")
         ww = held([P, PASSES, 2 * N], U8, "ww")
         ws = held([P, PASSES, N], U8, "ws")
-        gate_first = held([P, P], F32, "gate_first")
-        gate_rest = held([P, SLOTS - P], F32, "gate_rest")
+        gate_sb = held([P, SLOTS], F32, "gate_sb")
         zeros = held([P, P], F32, "zeros")
-        win = [held([P, T], F32, "win%d" % r) for r in range(4)]
+        win = {r: held([P, T], F32, "win%d" % r) for r in (0, 1, 3)}
+
+        def clear(region):
+            nc.scalar.activation(
+                region.rearrange("p (a b) -> p a b", b=P),
+                zeros[:].unsqueeze(1).to_broadcast([P, region.shape[1] // P, P]),
+                COPY,
+            )
 
         nc.vector.memset(xs[:].bitcast(I32), 0)
         nc.vector.memset(was[:].bitcast(I32), 0)
@@ -88,12 +94,8 @@ def tile_moe_dyl_none_kernel(
         nc.vector.memset(wbs[:].bitcast(I32), 0)
         nc.vector.memset(ws[:].rearrange("p a n -> p (a n)").bitcast(I32), 0)
         nc.vector.memset(xs_low[96:, :].bitcast(I32), 0)
-        for r in range(4):
-            nc.scalar.activation(
-                win[r][:].rearrange("p (a b) -> p a b", b=P),
-                zeros[:].unsqueeze(1).to_broadcast([P, T // P, P]),
-                COPY,
-            )
+        for r in (0, 1, 3):
+            clear(win[r][:])
 
         nc.sync.dma_start(tok_list[:], offs)
         load_scale_rows(xs, x_scales)
@@ -106,8 +108,7 @@ def tile_moe_dyl_none_kernel(
         load_scale_rows(wbs, wb_scales)
         load_words(waw[1], wa_words[1])
         load_words(wbw, wb_words[0])
-        nc.sync.dma_start(out=gate_first[:], in_=gate[:, :P])
-        nc.sync.dma_start(out=gate_rest[:], in_=gate[:, P:])
+        nc.sync.dma_start(out=gate_sb[:], in_=gate)
         load(ww[:], w_words.rearrange("a p c -> p a c"))
         for q in range(4):
             load(ws[32 * q : 32 * q + 4, :, :], w_scales[:, 4 * q : 4 * q + 4, :].rearrange("a r n -> r a n"))
@@ -134,9 +135,11 @@ def tile_moe_dyl_none_kernel(
             nc.vector.tensor_copy(dealt, window.indirect(columns_of(wa_list, blocks)))
             return {m: dst[:, H * j : H * (j + 1)] for j, m in enumerate(blocks)}
 
-        def first_product(a, blocks, dst, scales, hts):
-            words = gather_dealt(dst, waw[a][:].bitcast(U32), blocks)
-            for m in blocks:
+        def wa_words_of(a, blocks, dst):
+            return gather_dealt(dst, waw[a][:].bitcast(U32), blocks)
+
+        def first_product(a, opens, words, scales, hts):
+            for m in words:
                 slots = slice(P * m, P * (m + 1))
                 for t in range(4):
                     cols = slice(P * t, P * (t + 1))
@@ -147,13 +150,16 @@ def tile_moe_dyl_none_kernel(
                         scales[m][4 * a :, cols],
                         xq[a][:, slots],
                         xsq[4 * a :, slots],
-                        (a, t) == (0, 0),
-                        (a, t) == (PASSES - 1, 3),
+                        opens and t == 0,
+                        not opens and t == 3,
                     )
 
-        def round_h(blocks, hts, grouped):
+        def round_h(m, hts, dst):
+            nc.scalar.copy(out=dst, in_=hts[m][:].rearrange("p t s -> p s t"))
+
+        def round_pair(blocks, hts, grouped):
             for j, m in enumerate(blocks):
-                nc.scalar.copy(out=grouped[:, P * j : P * (j + 1), :], in_=hts[m][:].rearrange("p t s -> p s t"))
+                round_h(m, hts, grouped[:, P * j : P * (j + 1), :])
 
         def quantise(blocks, grouped, hq):
             hqs = held([P, P * len(blocks)], U8, "hqs%d" % blocks[0])
@@ -181,8 +187,7 @@ def tile_moe_dyl_none_kernel(
 
         def gated(blocks, dst, y):
             width = P * len(blocks)
-            first = P * (blocks[0] - 1)
-            weights = gate_rest[:, first : first + width] if blocks[0] else gate_first[:]
+            weights = gate_sb[:, P * blocks[0] : P * blocks[0] + width]
             nc.vector.tensor_tensor(dst[:], y, weights.unsqueeze(1).to_broadcast([P, y.shape[1], width]), MULT)
             return dst
 
@@ -213,71 +218,60 @@ def tile_moe_dyl_none_kernel(
 
         wb_window = wbw[:].bitcast(U32)
 
-        wasq = gather_dealt(held([P, 2 * H], U8, "wasq_01"), was[:], (0, 1))
-        hts = {m: bank(m, [P, 4, P]) for m in (0, 1)}
-        first_product(0, (0, 1), held([P, 2 * H], U32, "waq0_01"), wasq, hts)
-        wbsq = gather(placed([P, 2 * N], U8, "wbsq_01", 2 * KIB), wbs[:], wb_list, (0, 1))
-        grouped = {}
-        for m in (0, 1):
-            first_product(1, (m,), placed([P, H], U32, "waq1_%d" % m, 24 * KIB * m), wasq, hts)
-            grouped[m] = held([P, P, 4], BF16, "grouped_%d" % m)
-            round_h((m,), hts, grouped[m])
-        pair = (2, 3)
-        wasq = gather_dealt(placed([P, 2 * H], U8, "wasq_23", 0), was[:], pair)
-        wbq_0 = gather(placed([P, N], U32, "wbq_0", 3 * KIB), wb_window, wb_list, (0,))
-        h_0 = quantise((0,), grouped[0], placed([P, P], U32, "hq_0", 7 * KIB))
-        wbq_1 = gather(placed([P, N], U32, "wbq_1", 5 * KIB), wb_window, wb_list, (1,))
-        y_first = second_product(5, (0,), (0,), h_0, wbq_0, wbsq)
-        y_rest = second_product(6, (1, 2, 3), (0,), h_0, wbq_0, wbsq)
-        values = gated((0,), held([P, 1, P], F32, "v0_0"), y_first[:])
-        scatter_on_scalar(0, (0,), values[:, 0, :])
-        h_1 = quantise((1,), grouped[1], placed([P, P], U32, "hq_1", 7 * KIB))
-        y_1 = second_product(7, (0, 1, 2, 3), (1,), h_1, wbq_1, wbsq)
-        values = gated((0,), held([P, 3, P], F32, "v123_0"), y_rest[:])
-        for r in (1, 2, 3):
-            scatter_on_scalar(r, (0,), values[:, r - 1, :])
+        first, second, last = (0, 1), (2, 3), (4, 5)
 
-        hts = {m: bank(m % 2, [P, 4, P]) for m in pair}
-        first_product(0, pair, placed([P, 2 * H], U32, "waq0_23", 3 * KIB), wasq, hts)
-        first_product(1, pair, placed([P, 2 * H], U32, "waq1_23", 7 * KIB), wasq, hts)
+        def scatter_rows(rows, blocks, values):
+            for place, r in enumerate(rows):
+                scatter_on_scalar(r, blocks, values[:, place, :])
+
+        wasq = gather_dealt(held([P, 2 * H], U8, "wasq_01"), was[:], first)
+        hts = {m: bank(m, [P, 4, P]) for m in range(4)}
+        first_product(0, True, wa_words_of(0, first, held([P, 2 * H], U32, "waq0_01")), wasq, hts)
+        wbsq = gather(placed([P, 2 * N], U8, "wbsq_01", 8 * KIB), wbs[:], wb_list, first)
+        first_product(1, False, wa_words_of(1, first, placed([P, 2 * H], U32, "waq1_01", 0)), wasq, hts)
+        waq1 = {pair: wa_words_of(1, pair, held([P, 2 * H], U32, "waq1_%d" % pair[0])) for pair in (second, last)}
+        grouped = placed([P, 2 * P, 4], BF16, "grouped_01", 4 * KIB)
+        win[2] = placed([P, T], F32, "win2", 0)
+        for j in range(2):
+            round_h(first[j], hts, grouped[:, P * j : P * (j + 1), :])
+            clear(win[2][:, BANK * j : BANK * (j + 1)])
+        wbq = gather(placed([P, 2 * N], U32, "wbq_01", 9 * KIB), wb_window, wb_list, first)
+        h = quantise(first, grouped, placed([P, 2 * P], U32, "hq_01", 16 * KIB))
+        y_01 = second_product(4, (0, 1), first, h, wbq, wbsq)
+        y_23 = second_product(5, (2, 3), first, h, wbq, wbsq)
+
+        wasq = gather_dealt(placed([P, 2 * H], U8, "wasq_23", 4 * KIB), was[:], second)
+        first_product(1, True, waq1[second], wasq, hts)
+        scatter_rows((0, 1), first, gated(first, held([P, 2, 2 * P], F32, "v01_01"), y_01[:]))
+        first_product(0, False, wa_words_of(0, second, placed([P, 2 * H], U32, "waq0_23", 10 * KIB)), wasq, hts)
         grouped = placed([P, 2 * P, 4], BF16, "grouped_23", 19 * KIB)
-        round_h(pair, hts, grouped)
-        wbsq = gather(placed([P, 2 * N], U8, "wbsq_23", 2 * KIB), wbs[:], wb_list, pair)
-        values = gated((1,), placed([P, 4, P], F32, "v_1", 7 * KIB), y_1[:])
-        for r in range(4):
-            scatter_on_scalar(r, (1,), values[:, r, :])
-        wbq = gather(placed([P, 2 * N], U32, "wbq_23", 9 * KIB), wb_window, wb_list, pair)
-        h = quantise(pair, grouped, placed([P, 2 * P], U32, "hq_23", 13 * KIB))
-        y_0 = second_product(5, (0,), pair, h, wbq, wbsq)
-        y_12 = second_product(6, (1, 2), pair, h, wbq, wbsq)
-        y_3 = second_product(4, (3,), pair, h, wbq, wbsq)
-
-        last = (4, 5)
-        wasq = gather_dealt(placed([P, 2 * H], U8, "wasq_45", 19 * KIB), was[:], last)
-        values = gated(pair, held([P, 1, 2 * P], F32, "v0_23"), y_0[:])
-        scatter_on_scalar(0, pair, values[:, 0, :])
-        values = gated(pair, held([P, 1, 2 * P], F32, "v1_23"), y_12[:, :1, :])
-        scatter_on_scalar(1, pair, values[:, 0, :])
+        round_pair(second, hts, grouped)
+        wbsq = gather(placed([P, 2 * N], U8, "wbsq_23", 8 * KIB), wbs[:], wb_list, second)
+        wasq = gather_dealt(placed([P, 2 * H], U8, "wasq_45", 16 * KIB), was[:], last)
         hts = {m: bank(m % 2, [P, 4, P]) for m in last}
-        first_product(0, last, placed([P, 2 * H], U32, "waq0_45", 9 * KIB), wasq, hts)
-        first_product(1, last, placed([P, 2 * H], U32, "waq1_45", 13 * KIB), wasq, hts)
-        grouped = placed([P, 2 * P, 4], BF16, "grouped_45", 22 * KIB)
-        round_h(last, hts, grouped)
-        wbsq = gather(placed([P, 2 * N], U8, "wbsq_45", 2 * KIB), wbs[:], wb_list, last)
-        values = gated((2,), placed([P, 1, P], F32, "v3_2", 14 * KIB), y_3[:, :, :P])
-        scatter_on_scalar(3, (2,), values[:, 0, :])
-        values = gated(pair, placed([P, 1, 2 * P], F32, "v2_23", 13 * KIB), y_12[:, 1:, :])
-        scatter_on_scalar(2, pair, values[:, 0, :])
-        wbq = gather(placed([P, 2 * N], U32, "wbq_45", 14 * KIB + 512), wb_window, wb_list, last)
+        first_product(1, True, waq1[last], wasq, hts)
+        scatter_rows((2, 3), first, gated(first, placed([P, 2, 2 * P], F32, "v23_01", 9 * KIB), y_23[:]))
+        wbq = gather(placed([P, 2 * N], U32, "wbq_23", 11 * KIB), wb_window, wb_list, second)
+        h = quantise(second, grouped, held([P, 2 * P], U32, "hq_23"))
+        y_01 = second_product(6, (0, 1), second, h, wbq, wbsq)
+        y_23 = second_product(7, (2, 3), second, h, wbq, wbsq)
+
+        first_product(0, False, wa_words_of(0, last, placed([P, 2 * H], U32, "waq0_45", 20 * KIB)), wasq, hts)
+        wbsq = gather(placed([P, 2 * N], U8, "wbsq_45", 19 * KIB), wbs[:], wb_list, last)
+        grouped = placed([P, 2 * P, 4], BF16, "grouped_45", 24 * KIB)
+        round_pair(last, hts, grouped)
+        scatter_rows((0, 1), second, gated(second, held([P, 2, 2 * P], F32, "v01_23"), y_01[:]))
+        wbq = gather(placed([P, 2 * N], U32, "wbq_45", 11 * KIB), wb_window, wb_list, last)
         h = quantise(last, grouped, held([P, 2 * P], U32, "hq_45"))
-        values = gated((3,), placed([P, 1, P], F32, "v3_3", 22 * KIB), y_3[:, :, P:])
-        scatter_on_vector(3, (3,), values[:, 0, :])
-        values = gated(last, held([P, 1, 2 * P], F32, "v0_45"), second_product(2, (0,), last, h, wbq, wbsq)[:])
-        scatter_on_scalar(0, last, values[:, 0, :])
-        v_3 = gated(last, held([P, 1, 2 * P], F32, "v3_45"), second_product(3, (3,), last, h, wbq, wbsq)[:])
-        values = gated(last, held([P, 2, 2 * P], F32, "v12_45"), second_product(4, (1, 2), last, h, wbq, wbsq)[:])
-        scatter_on_vector(3, last, v_3[:, 0, :])
-        for r in (1, 2):
-            scatter_on_scalar(r, last, values[:, r - 1, :])
-        for r, banks in ((3, (7, 5)), (0, (6, 2)), (1, (3, 4)), (2, (7, 5))):
+        values = gated(second, placed([P, 2, 2 * P], F32, "v23_23", 24 * KIB), y_23[:])
+        scatter_on_vector(3, second, values[:, 1, :])
+        scatter_on_scalar(2, second, values[:, 0, :])
+        v_03 = gated(last, held([P, 2, 2 * P], F32, "v03_45"), second_product(2, (0, 3), last, h, wbq, wbsq)[:])
+        scatter_on_scalar(0, last, v_03[:, 0, :])
+        v_12 = gated(last, held([P, 2, 2 * P], F32, "v12_45"), second_product(3, (1, 2), last, h, wbq, wbsq)[:])
+        scatter_on_vector(3, last, v_03[:, 1, :])
+        scatter_on_scalar(1, last, v_12[:, 0, :])
+        scatter_on_vector(2, last[1:], v_12[:, 1, P:])
+        scatter_on_scalar(2, last[:1], v_12[:, 1, :P])
+        for r, banks in ((3, (4, 5)), (0, (6, 0)), (1, (7, 2)), (2, (3, 4))):
             add_and_store(r, banks)

@@ -43,16 +43,15 @@ def tile_moe_dyl_none_kernel(
         def bank(number, shape):
             return psum.tile(shape, F32, name="bank%d" % number, offset=4 * BANK * number)
 
-        def load(tile, source):
-            nc.sync.dma_start(out=tile.bitcast(I32), in_=source.bitcast(I32))
+        def load(tile, source, queue=nc.sync):
+            queue.dma_start(out=tile.bitcast(I32), in_=source.bitcast(I32))
 
         def load_words(tile, words):
             load(tile[:], words.rearrange("p c d -> p (c d)"))
 
-        def load_scale_rows(plane, scales):
-            rows = 4 * scales.shape[0]
+        def load_scale_rows(plane, scales, queue):
             for q in range(4):
-                load(plane[32 * q : 32 * q + rows, :], scales[:, 4 * q : 4 * q + 4, :])
+                load(plane[32 * q : 32 * q + 4 * PASSES, :], scales[:, 4 * q : 4 * q + 4, :], queue)
 
         def mx(acc, lhs, lhs_type, lhs_scale, rhs, rhs_scale, start, stop):
             nc.tensor.matmul_mx(
@@ -90,23 +89,24 @@ def tile_moe_dyl_none_kernel(
 
         nc.vector.memset(xs[:].bitcast(I32), 0)
         nc.vector.memset(was[:].bitcast(I32), 0)
-        nc.vector.memset(zeros[:], 0.0)
         nc.vector.memset(wbs[:].bitcast(I32), 0)
+        nc.vector.memset(zeros[:], 0.0)
         nc.vector.memset(ws[:].rearrange("p a n -> p (a n)").bitcast(I32), 0)
         nc.vector.memset(xs_low[96:, :].bitcast(I32), 0)
-        for r in (0, 1, 3):
-            clear(win[r][:])
 
         nc.sync.dma_start(tok_list[:], offs)
-        load_scale_rows(xs, x_scales)
+        nc.sync.dma_start(wa_list[:], offs2)
+        nc.sync.dma_start(wb_list[:], offs3)
+        load_scale_rows(xs, x_scales, nc.scalar)
+        load_scale_rows(was, wa_scales, nc.sync)
+        for r in range(4):
+            load(wbs[r:P:32, :], wb_scales[0, r:16:4, :], nc.scalar)
+        for r in (0, 1, 3):
+            clear(win[r][:])
         for a in range(PASSES):
             load_words(xw[a], x_words[a])
-        nc.sync.dma_start(wa_list[:], offs2)
-        load_scale_rows(was, wa_scales)
-        load_words(waw[0], wa_words[0])
-        nc.sync.dma_start(wb_list[:], offs3)
-        load_scale_rows(wbs, wb_scales)
-        load_words(waw[1], wa_words[1])
+        for a in range(PASSES):
+            load_words(waw[a], wa_words[a])
         load_words(wbw, wb_words[0])
         nc.sync.dma_start(out=gate_sb[:], in_=gate)
         load(ww[:], w_words.rearrange("a p c -> p a c"))

@@ -197,7 +197,7 @@ def tile_moe_dyl_none_kernel(
         def scatter_on_vector(r, blocks, values):
             nc.vector.tensor_copy(win[r][:].indirect(tokens_of(blocks)), values)
 
-        def add_and_store(r, banks):
+        def add_and_store(r, banks, last_pieces):
             for c in range(2):
                 toks = slice(BANK * c, BANK * (c + 1))
                 acc = bank(banks[c], [P, BANK])
@@ -212,9 +212,14 @@ def tile_moe_dyl_none_kernel(
                         a == 0,
                         a == PASSES - 1,
                     )
-                result = held([P, BANK], F32, "result%d_%d" % (r, c))
-                nc.vector.tensor_tensor(result[:], acc[:], win[r][:, toks], ADD)
-                nc.sync.dma_start(out=out[P * r : P * (r + 1), toks], in_=result[:])
+                pieces = last_pieces if c else 1
+                width = BANK // pieces
+                for piece in range(pieces):
+                    part = slice(width * piece, width * (piece + 1))
+                    toks = slice(BANK * c + part.start, BANK * c + part.stop)
+                    result = held([P, width], F32, "result%d_%d_%d" % (r, c, piece))
+                    nc.vector.tensor_tensor(result[:], acc[:, part], win[r][:, toks], ADD)
+                    nc.sync.dma_start(out=out[P * r : P * (r + 1), toks], in_=result[:])
 
         wb_window = wbw[:].bitcast(U32)
 
@@ -237,12 +242,14 @@ def tile_moe_dyl_none_kernel(
             clear(win[2][:, BANK * j : BANK * (j + 1)])
         wbq = gather(placed([P, 2 * N], U32, "wbq_01", 9 * KIB), wb_window, wb_list, first)
         h = quantise(first, grouped, placed([P, 2 * P], U32, "hq_01", 16 * KIB))
-        y_01 = second_product(4, (0, 1), first, h, wbq, wbsq)
+        y_0 = second_product(4, (0,), first, h, wbq, wbsq)
+        y_1 = second_product(6, (1,), first, h, wbq, wbsq)
         y_23 = second_product(5, (2, 3), first, h, wbq, wbsq)
 
         wasq = gather_dealt(placed([P, 2 * H], U8, "wasq_23", 4 * KIB), was[:], second)
         first_product(1, True, waq1[second], wasq, hts)
-        scatter_rows((0, 1), first, gated(first, held([P, 2, 2 * P], F32, "v01_01"), y_01[:]))
+        for r, y in enumerate((y_0, y_1)):
+            scatter_rows((r,), first, gated(first, held([P, 1, 2 * P], F32, "v%d_01" % r), y[:]))
         first_product(0, False, wa_words_of(0, second, placed([P, 2 * H], U32, "waq0_23", 10 * KIB)), wasq, hts)
         grouped = placed([P, 2 * P, 4], BF16, "grouped_23", 19 * KIB)
         round_pair(second, hts, grouped)
@@ -263,15 +270,14 @@ def tile_moe_dyl_none_kernel(
         scatter_rows((0, 1), second, gated(second, held([P, 2, 2 * P], F32, "v01_23"), y_01[:]))
         wbq = gather(placed([P, 2 * N], U32, "wbq_45", 11 * KIB), wb_window, wb_list, last)
         h = quantise(last, grouped, held([P, 2 * P], U32, "hq_45"))
-        values = gated(second, placed([P, 2, 2 * P], F32, "v23_23", 24 * KIB), y_23[:])
-        scatter_on_vector(3, second, values[:, 1, :])
-        scatter_on_scalar(2, second, values[:, 0, :])
+        v_3 = gated(second, placed([P, 1, 2 * P], F32, "v3_23", 24 * KIB), y_23[:, 1:, :])
+        v_2 = gated(second, placed([P, 1, 2 * P], F32, "v2_23", 25 * KIB), y_23[:, :1, :])
+        scatter_on_vector(3, second, v_3[:, 0, :])
+        scatter_on_scalar(2, second, v_2[:, 0, :])
         v_03 = gated(last, held([P, 2, 2 * P], F32, "v03_45"), second_product(2, (0, 3), last, h, wbq, wbsq)[:])
         scatter_on_scalar(0, last, v_03[:, 0, :])
         v_12 = gated(last, held([P, 2, 2 * P], F32, "v12_45"), second_product(3, (1, 2), last, h, wbq, wbsq)[:])
         scatter_on_vector(3, last, v_03[:, 1, :])
-        scatter_on_scalar(1, last, v_12[:, 0, :])
-        scatter_on_vector(2, last[1:], v_12[:, 1, P:])
-        scatter_on_scalar(2, last[:1], v_12[:, 1, :P])
+        scatter_rows((1, 2), last, v_12)
         for r, banks in ((3, (4, 5)), (0, (6, 0)), (1, (7, 2)), (2, (3, 4))):
-            add_and_store(r, banks)
+            add_and_store(r, banks, 2 if r == 2 else 1)

from contextlib import ExitStack

import concourse.mybir as mybir

K, T, E, B, H, N = 1024, 1024, 4, 6, 512, 512
FLOPS = 2 * K * N * T + 2 * 128 * B * (K * H + H * N)

F32 = mybir.dt.float32
BF16 = mybir.dt.bfloat16
I32 = mybir.dt.int32
U32 = mybir.dt.uint32
U16 = mybir.dt.uint16
U8 = mybir.dt.uint8
FP8X4 = mybir.dt.float8_e4m3fn_x4
FP4X4 = mybir.dt.float4_e2m1fn_x4
MULT = mybir.AluOpType.mult
ADD = mybir.AluOpType.add
COPY = mybir.ActivationFunctionType.Copy

P = 128
PASSES = K // 512
SLOTS = P * B
BANK = 512
KIB = 1024
LOWERED = 100


def tile_moe_dyl_none_kernel(
    tc, x_words, x_scales, w_words, w_scales, wa_words, wa_scales, wb_words, wb_scales, gate, offs, offs2, offs3, out
):
    nc = tc.nc
    with ExitStack() as ctx:
        keep = ctx.enter_context(tc.tile_pool(name="keep", bufs=1))
        reuse = ctx.enter_context(tc.tile_pool(name="reuse", bufs=1))
        psum = ctx.enter_context(tc.psum_pool(name="psum", bufs=1))

        def held(shape, dtype, name):
            return keep.tile(shape, dtype, name=name, align_bytes=64)

        def placed(shape, dtype, name, offset):
            return reuse.tile(shape, dtype, name=name, offset=offset, align_bytes=64)

        def bank(number, shape):
            return psum.tile(shape, F32, name="bank%d" % number, offset=4 * BANK * number)

        def load(tile, source, queue=nc.sync):
            queue.dma_start(out=tile.bitcast(I32), in_=source.bitcast(I32))

        def load_words(tile, words):
            load(tile[:], words.rearrange("p c d -> p (c d)"))

        def load_scale_rows(plane, scales, queue):
            for q in range(4):
                load(plane[32 * q : 32 * q + 4 * PASSES, :], scales[:, 4 * q : 4 * q + 4, :], queue)

        def mx(acc, lhs, lhs_type, lhs_scale, rhs, rhs_scale, start, stop):
            nc.tensor.matmul_mx(
                out=acc,
                lhsT=lhs.bitcast(lhs_type),
                lhsT_scale=lhs_scale,
                rhs=rhs.bitcast(FP8X4),
                rhs_scale=rhs_scale,
                start=start,
                stop=stop,
            )

        tok_list = held([P, SLOTS // 16], U16, "tok_list")
        wa_list = held([P, B * H // 16], U16, "wa_list")
        wb_list = held([P, B * N // 16], U16, "wb_list")
        xw = [held([P, T], I32, "xw%d" % a) for a in range(PASSES)]
        xs = held([P, T], U8, "xs")
        xs_low = held([P, T], U8, "xs_low")
        was = held([P, E * H], U8, "was")
        waw = [held([P, E * H], I32, "waw%d" % a) for a in range(PASSES)]
        wbs = held([P, E * N], U8, "wbs")
        wbw = held([P, E * N], I32, "wbw")
        ww = held([P, PASSES, 2 * N], U8, "ww")
        ws = held([P, PASSES, N], U8, "ws")
        gate_sb = held([P, SLOTS], F32, "gate_sb")
        zeros = held([P, P], F32, "zeros")
        win = {r: held([P, T], F32, "win%d" % r) for r in (0, 1, 3)}

        def clear(region):
            nc.scalar.activation(
                region.rearrange("p (a b) -> p a b", b=P),
                zeros[:].unsqueeze(1).to_broadcast([P, region.shape[1] // P, P]),
                COPY,
            )

        nc.vector.memset(xs[:].bitcast(I32), 0)
        nc.vector.memset(was[:].bitcast(I32), 0)
        nc.vector.memset(wbs[:].bitcast(I32), 0)
        nc.vector.memset(zeros[:], 0.0)
        nc.vector.memset(ws[:].rearrange("p a n -> p (a n)").bitcast(I32), 0)
        nc.vector.memset(xs_low[96:, :].bitcast(I32), 0)

        nc.sync.dma_start(tok_list[:], offs)
        nc.sync.dma_start(wa_list[:], offs2)
        nc.sync.dma_start(wb_list[:], offs3)
        load_scale_rows(xs, x_scales, nc.scalar)
        load_scale_rows(was, wa_scales, nc.sync)
        for r in range(4):
            load(wbs[r:P:32, :], wb_scales[0, r:16:4, :], nc.scalar)
        for r in (0, 1, 3):
            clear(win[r][:])
        for a in range(PASSES):
            load_words(xw[a], x_words[a])
        for a in range(PASSES):
            load_words(waw[a], wa_words[a])
        load_words(wbw, wb_words[0])
        nc.sync.dma_start(out=gate_sb[:], in_=gate)
        load(ww[:], w_words.rearrange("a p c -> p a c"))
        for q in range(4):
            load(ws[32 * q : 32 * q + 4, :, :], w_scales[:, 4 * q : 4 * q + 4, :].rearrange("a r n -> r a n"))
        load(xs_low[:LOWERED, :], xs[4 : 4 + LOWERED, :])

        xsq = held([P, SLOTS], U8, "xsq")
        nc.vector.tensor_copy(xsq[:], xs[:].indirect(tok_list[:]))
        xq = [held([P, SLOTS], U32, "xq%d" % a) for a in range(PASSES)]
        for a in range(PASSES):
            nc.vector.tensor_copy(xq[a][:], xw[a][:].bitcast(U32).indirect(tok_list[:]))

        def columns_of(entries, blocks):
            return entries[:, blocks[0] * H // 16 : (blocks[-1] + 1) * H // 16]

        def tokens_of(blocks):
            return tok_list[:, blocks[0] * P // 16 : (blocks[-1] + 1) * P // 16]

        def gather(dst, window, entries, blocks):
            nc.vector.tensor_copy(dst[:], window.indirect(columns_of(entries, blocks)))
            return {m: dst[:, N * j : N * (j + 1)] for j, m in enumerate(blocks)}

        def gather_dealt(dst, window, blocks):
            dealt = dst[:].rearrange("p (j t q) -> p j q t", j=len(blocks), t=4)
            nc.vector.tensor_copy(dealt, window.indirect(columns_of(wa_list, blocks)))
            return {m: dst[:, H * j : H * (j + 1)] for j, m in enumerate(blocks)}

        def wa_words_of(a, blocks, dst):
            return gather_dealt(dst, waw[a][:].bitcast(U32), blocks)

        def first_product(a, opens, words, scales, hts):
            for m in words:
                slots = slice(P * m, P * (m + 1))
                for t in range(4):
                    cols = slice(P * t, P * (t + 1))
                    mx(
                        hts[m][:, t, :],
                        words[m][:, cols],
                        FP8X4,
                        scales[m][4 * a :, cols],
                        xq[a][:, slots],
                        xsq[4 * a :, slots],
                        opens and t == 0,
                        not opens and t == 3,
                    )

        def round_h(m, hts, dst):
            nc.scalar.copy(out=dst, in_=hts[m][:].rearrange("p t s -> p s t"))

        def round_pair(blocks, hts, grouped):
            for j, m in enumerate(blocks):
                round_h(m, hts, grouped[:, P * j : P * (j + 1), :])

        def quantise(blocks, grouped, hq):
            hqs = held([P, P * len(blocks)], U8, "hqs%d" % blocks[0])
            nc.vector.quantize_mx(
                out=hq[:].bitcast(FP8X4), scales=hqs[:], in_=grouped[:].rearrange("p s t -> p (s t)")
            )
            return {m: (hq[:, P * j : P * (j + 1)], hqs[:, P * j : P * (j + 1)]) for j, m in enumerate(blocks)}

        def second_product(number, rows, blocks, h, words, scales):
            y = bank(number, [P, len(rows), P * len(blocks)])
            for place, r in enumerate(rows):
                cols = slice(P * r, P * (r + 1))
                for j, m in enumerate(blocks):
                    mx(
                        y[:, place, P * j : P * (j + 1)],
                        words[m][:, cols],
                        FP8X4,
                        scales[m][:, cols],
                        h[m][0],
                        h[m][1],
                        True,
                        True,
                    )
            return y

        def gated(blocks, dst, y):
            width = P * len(blocks)
            weights = gate_sb[:, P * blocks[0] : P * blocks[0] + width]
            nc.vector.tensor_tensor(dst[:], y, weights.unsqueeze(1).to_broadcast([P, y.shape[1], width]), MULT)
            return dst

        def scatter_on_scalar(r, blocks, values):
            nc.scalar.activation(win[r][:].indirect(tokens_of(blocks)), values, COPY)

        def scatter_on_vector(r, blocks, values):
            nc.vector.tensor_copy(win[r][:].indirect(tokens_of(blocks)), values)

        def add_and_store(r, banks, last_pieces):
            for c in range(2):
                toks = slice(BANK * c, BANK * (c + 1))
                acc = bank(banks[c], [P, BANK])
                for a in range(PASSES):
                    mx(
                        acc[:],
                        ww[:, a, 2 * P * r : 2 * P * (r + 1)],
                        FP4X4,
                        ws[:, a, P * r : P * (r + 1)],
                        xw[a][:, toks],
                        (xs, xs_low)[a][:, toks],
                        a == 0,
                        a == PASSES - 1,
                    )
                pieces = last_pieces if c else 1
                width = BANK // pieces
                for piece in range(pieces):
                    part = slice(width * piece, width * (piece + 1))
                    toks = slice(BANK * c + part.start, BANK * c + part.stop)
                    result = held([P, width], F32, "result%d_%d_%d" % (r, c, piece))
                    nc.vector.tensor_tensor(result[:], acc[:, part], win[r][:, toks], ADD)
                    nc.sync.dma_start(out=out[P * r : P * (r + 1), toks], in_=result[:])

        wb_window = wbw[:].bitcast(U32)

        first, second, last = (0, 1), (2, 3), (4, 5)

        def scatter_rows(rows, blocks, values):
            for place, r in enumerate(rows):
                scatter_on_scalar(r, blocks, values[:, place, :])

        wasq = gather_dealt(held([P, 2 * H], U8, "wasq_01"), was[:], first)
        hts = {m: bank(m, [P, 4, P]) for m in range(4)}
        first_product(0, True, wa_words_of(0, first, held([P, 2 * H], U32, "waq0_01")), wasq, hts)
        wbsq = gather(placed([P, 2 * N], U8, "wbsq_01", 8 * KIB), wbs[:], wb_list, first)
        first_product(1, False, wa_words_of(1, first, placed([P, 2 * H], U32, "waq1_01", 0)), wasq, hts)
        waq1 = {pair: wa_words_of(1, pair, held([P, 2 * H], U32, "waq1_%d" % pair[0])) for pair in (second, last)}
        grouped = placed([P, 2 * P, 4], BF16, "grouped_01", 4 * KIB)
        win[2] = placed([P, T], F32, "win2", 0)
        for j in range(2):
            round_h(first[j], hts, grouped[:, P * j : P * (j + 1), :])
            clear(win[2][:, BANK * j : BANK * (j + 1)])
        wbq = gather(placed([P, 2 * N], U32, "wbq_01", 9 * KIB), wb_window, wb_list, first)
        h = quantise(first, grouped, placed([P, 2 * P], U32, "hq_01", 16 * KIB))
        y_0 = second_product(4, (0,), first, h, wbq, wbsq)
        y_1 = second_product(6, (1,), first, h, wbq, wbsq)
        y_23 = second_product(5, (2, 3), first, h, wbq, wbsq)

        wasq = gather_dealt(placed([P, 2 * H], U8, "wasq_23", 4 * KIB), was[:], second)
        first_product(1, True, waq1[second], wasq, hts)
        for r, y in enumerate((y_0, y_1)):
            scatter_rows((r,), first, gated(first, held([P, 1, 2 * P], F32, "v%d_01" % r), y[:]))
        first_product(0, False, wa_words_of(0, second, placed([P, 2 * H], U32, "waq0_23", 10 * KIB)), wasq, hts)
        grouped = placed([P, 2 * P, 4], BF16, "grouped_23", 19 * KIB)
        round_pair(second, hts, grouped)
        wbsq = gather(placed([P, 2 * N], U8, "wbsq_23", 8 * KIB), wbs[:], wb_list, second)
        wasq = gather_dealt(placed([P, 2 * H], U8, "wasq_45", 16 * KIB), was[:], last)
        hts = {m: bank(m % 2, [P, 4, P]) for m in last}
        first_product(1, True, waq1[last], wasq, hts)
        scatter_rows((2, 3), first, gated(first, placed([P, 2, 2 * P], F32, "v23_01", 9 * KIB), y_23[:]))
        wbq = gather(placed([P, 2 * N], U32, "wbq_23", 11 * KIB), wb_window, wb_list, second)
        h = quantise(second, grouped, held([P, 2 * P], U32, "hq_23"))
        y_01 = second_product(6, (0, 1), second, h, wbq, wbsq)
        y_23 = second_product(7, (2, 3), second, h, wbq, wbsq)

        first_product(0, False, wa_words_of(0, last, placed([P, 2 * H], U32, "waq0_45", 20 * KIB)), wasq, hts)
        wbsq = gather(placed([P, 2 * N], U8, "wbsq_45", 19 * KIB), wbs[:], wb_list, last)
        grouped = placed([P, 2 * P, 4], BF16, "grouped_45", 24 * KIB)
        round_pair(last, hts, grouped)
        scatter_rows((0, 1), second, gated(second, held([P, 2, 2 * P], F32, "v01_23"), y_01[:]))
        wbq = gather(placed([P, 2 * N], U32, "wbq_45", 11 * KIB), wb_window, wb_list, last)
        h = quantise(last, grouped, held([P, 2 * P], U32, "hq_45"))
        v_3 = gated(second, placed([P, 1, 2 * P], F32, "v3_23", 24 * KIB), y_23[:, 1:, :])
        v_2 = gated(second, placed([P, 1, 2 * P], F32, "v2_23", 25 * KIB), y_23[:, :1, :])
        scatter_on_vector(3, second, v_3[:, 0, :])
        scatter_on_scalar(2, second, v_2[:, 0, :])
        v_03 = gated(last, held([P, 2, 2 * P], F32, "v03_45"), second_product(2, (0, 3), last, h, wbq, wbsq)[:])
        scatter_on_scalar(0, last, v_03[:, 0, :])
        v_12 = gated(last, held([P, 2, 2 * P], F32, "v12_45"), second_product(3, (1, 2), last, h, wbq, wbsq)[:])
        scatter_on_vector(3, last, v_03[:, 1, :])
        scatter_rows((1, 2), last, v_12)
        for r, banks in ((3, (4, 5)), (0, (6, 0)), (1, (7, 2)), (2, (3, 4))):
            add_and_store(r, banks, 2 if r == 2 else 1)
